import numpy as np, ml_dtypes
CORES = [2,3,42,43,82,83,122,123]
N = 8
import mx_ref
BF = ml_dtypes.bfloat16
def gentries(a):
    return np.ascontiguousarray(a.reshape(8, 16, -1).transpose(0, 2, 1)).reshape(8, -1)
def gtable(e):
    e = np.asarray(e); return np.ascontiguousarray(e.reshape(8, -1, 16).transpose(0, 2, 1)).reshape(128, -1).astype(np.int32)
def gcols(t, e):
    v = np.concatenate([t.reshape(8, 16, -1, 4), np.zeros((8, 16, 1, 4), BF)], axis=2)
    return np.ascontiguousarray(np.stack([v[g][:, e[g]] for g in range(8)])).reshape(128, -1)
def tile(rs):
    return np.stack(rs, axis=2).reshape(128, -1).astype(BF)
def cut(t, i, w=512):
    return t[:, w * i:w * i + w]
def pick(q, e):
    c = np.concatenate([q[0].reshape(128, -1, 4), np.zeros((128, 1, 4), np.uint8)], axis=1); s = np.concatenate([q[1], np.ones((16, 1), np.uint8)], axis=1)
    return (np.ascontiguousarray(c[:, e].reshape(128, -1)), np.ascontiguousarray(s[:, e]))
def join(*qs):
    return (np.concatenate([q[0] for q in qs], axis=1), np.concatenate([q[1] for q in qs], axis=1))
def put(q, e, v):
    c, s = q[0].reshape(128, -1, 4).copy(), q[1].copy(); c[:, e] = v[0].reshape(128, -1, 4); s[:, e] = v[1]
    return (c.reshape(128, -1), s)
def pk(c, s):
    return (np.ascontiguousarray(c), mx_ref.live(s))
def emit(q):
    return q[0], q[1]
def packed(v, rng):
    q = [mx_ref.quantize(np.ascontiguousarray(v[r])) for r in range(N)]
    return np.stack([a for a, b in q]), np.stack([mx_ref.plane(b, rng) for a, b in q])
def values_of_codes():
    e, c = np.zeros((128, 128, 4), np.float32), np.zeros((128, 2, 4), np.uint8)
    e[np.arange(128), np.arange(128), 0] = 1
    c[:127, :, 0] = np.arange(256).reshape(2, 128).T[:127]
    return mx_ref.matmul(mx_ref.quantize(e.reshape(128, 512).astype(BF)), (c.reshape(128, 8), np.full((16, 2), 127, np.uint8))).T.reshape(-1).astype(np.float64)
CODE_VALUE, SCALE_VALUE = values_of_codes(), 2.0 ** (np.arange(256) - 127.0)
def decode(q):
    return (CODE_VALUE[q[0]].reshape(16, 8, -1, 4) * SCALE_VALUE[q[1]][:, None, :, None] + 0.0).reshape(128, -1).astype(np.float32)
def f(rng, *shape):
    return mx_ref.flush((rng.standard_normal(shape, dtype=np.float32) * np.exp2(rng.integers(-2, 3, shape[:-1] + (1,)))).astype(BF))
def wide(rng, *shape, cols=0):
    v = rng.standard_normal(shape, dtype=np.float32) * np.exp2(rng.integers(-12, 13, shape)).astype(np.float32)
    if cols: v *= np.repeat(np.exp2(rng.integers(-cols, cols + 1, shape[:-2] + (1, shape[-1] // 4))) * (rng.random(shape[:-2] + (1, shape[-1] // 4)) > 0.0625), 4, axis=-1).astype(np.float32)
    return mx_ref.flush(v.astype(BF))
C, A, R = 384, 192, 3
STEP = [1, 2, 4]
def layout(bad, sz, pr):
    g, n = np.arange(8)[:, None], np.arange(C)
    p = np.bitwise_xor.accumulate(np.concatenate([np.zeros((8, 1), np.int64), bad], axis=1), axis=1)
    odd = np.concatenate([p[g, n + sz] != p[g, n], np.zeros((8, 1), bool)], axis=1)
    up = np.where(pr < 0, C, pr)
    end = np.where(pr < 0, 0, pr + sz[g, pr])
    sib = np.where(n > pr + 1, pr + 1, np.where(n + sz < end, n + sz, C))
    pair = odd[:, :C] & odd[g, sib]
    top = np.where(odd[:, :C] & odd[g, up] & ~pair, up, n)
    for i in range(9): top = top[g, top]
    other = np.where(pair, sib, n)[g, top]
    name, rise = np.minimum(top, other), top < other
    begin = np.zeros((8, C), np.int64)
    np.maximum.at(begin, (g, name), np.where(rise, n, name))
    key = np.where(odd[:, :C], begin[g, name] * 2 * C + np.where(rise, C - 1 - n, C + n), 2 * C * C + n)
    o = np.argsort(key, axis=1, kind="stable")
    same = name[g, o[:, :-1]] == name[g, o[:, 1:]]
    return o, np.concatenate([np.where(same, o[:, 1:], -1), np.full((8, 1), -1)], axis=1)
def differences(t, o, follow):
    return (gcols(t, o).astype(np.float32) - gcols(t, follow).astype(np.float32)).astype(BF)
def big(v):
    v = v.astype(np.float32)
    v[np.abs(v) < np.float32(2.0 ** -16)] = 0
    return v.astype(BF)
def numbers_of(rng):
    return {"x": big(f(rng, N, 128, 4 * C)), "u": np.array(f(rng, N, 128, 512)), "v": np.array(f(rng, N, 128, 512))}
def weights(rng, still=[]):
    w = big(f(rng, N, 128, 2048)).reshape(N, 8, 16, 4, 8, 16, 4)
    for i in still:
        w[:, :, i] = 0
        w[:, :, :, :, :, i] = 0
    c, p = packed(np.ascontiguousarray(w).reshape(N, 128, 2048), rng)
    return {"wc": c, "ws": p}
def grown(rng):
    a, kids, way = [-1] * C, [0] * C, [0]
    back = (rng.geometric(rng.choice([0.4, 0.6, 0.8, 0.95]), C) - 1).tolist()
    for n in range(1, C):
        del way[max(1, len(way) - back[n]):]
        p = way[-1]
        a[n] = p
        kids[p] += 1
        if kids[p] == 2: way.pop()
        way.append(n)
    return np.array(a)
def chain():
    return np.arange(C) - 1
def fork(h):
    a = np.arange(C) - 1
    a[h] = 0
    return a
def comb():
    a = (np.arange(C) - 1) // 2 * 2
    a[0] = -1
    return a
def rake():
    n, h = np.arange(C), C // 2 + 1
    return np.where(n < h, n - 1, 2 * h - 2 - n)
def halves():
    a, todo = np.zeros(C, np.int64), [(0, C, -1)]
    while todo:
        lo, hi, p = todo.pop()
        a[lo] = p
        m = lo + 1 + (hi - lo) // 2
        if m > lo + 1: todo.append((lo + 1, m, lo))
        if hi > m: todo.append((m, hi, lo))
    return a
def trees(rng):
    return np.stack([np.stack([grown(rng) for g in range(8)]) for r in range(N)])
def stored(a):
    k, i = a.reshape(8 * N, C), np.arange(8 * N)
    s = np.ones((8 * N, C), np.int64)
    for n in range(C - 1, 0, -1): s[i, k[:, n]] += s[:, n]
    return {"sz": np.stack([gtable(e) for e in s.reshape(N, 8, C)]), "pr": np.stack([gtable(e) for e in a])}
def planted(rng, a, bad, still=[0]):
    d = numbers_of(rng)
    x = d["x"].reshape(N, 8, 16, C, 4)
    x[:, :, 0] = 0
    x[:, :, 0, :, 0] = np.where(bad, 1.0, -1.0).astype(np.float32).astype(BF)
    u = d["u"].reshape(N, 128, 128, 4)
    u[:, :, ::16] = 0
    for h in range(0, 128, 16): u[:, h, h, 0] = 1
    return {"x": x.reshape(N, 128, 4 * C), "u": u.reshape(N, 128, 512), "v": d["v"], **weights(rng, still), **stored(a)}
def setup_inputs(rng):
    return {**numbers_of(rng), **weights(rng), **stored(trees(rng))}
def setup_inputs_zeros(rng):
    d = numbers_of(rng)
    x = d["x"].reshape(N, 8, 16, C, 4)
    u = d["u"].reshape(N, 128, 128, 4)
    u[:, :, ::16] = 0
    e = rng.permutation(N)
    for i in range(N):
        r, body, by = e[i], np.zeros((8, 4)), np.zeros((8, 4))
        if i % 2:
            body[:] = 2.0 ** 26
            by[:] = 2.0 ** 30
        else:
            body[:2, 0] = [9 * 2.0 ** -33, 10 * 2.0 ** -33]
            by[:2, 0] = [9 * 2.0 ** -33, -8 * 2.0 ** -33]
        m = np.stack([rng.permutation(C) % 3 - 1.0 for g in range(8)])
        if i == 0: m[:] = 1
        z = m[:, None, :, None] * body[None, :, None, :]
        x[r][:, :8] = z.astype(np.float32).astype(BF)
        k = by.astype(np.float32).astype(BF)
        for h in range(0, 128, 16): u[r, h:h + 8, h] = k
    x[e[1]] = 0
    return {"x": x.reshape(N, 128, 4 * C), "u": u.reshape(N, 128, 512), "v": d["v"], **weights(rng, range(8)), **stored(trees(rng))}
def setup_inputs_chains(rng):
    a = np.broadcast_to(chain(), (N, 8, C)).copy()
    bad = np.zeros((N, 8, C), bool)
    h, e = int(rng.integers(8)), int(rng.integers(N))
    for r in range(N):
        k = np.insert(rng.permutation(np.delete(np.arange(8), h)), 5, h)
        for i, n in enumerate([1, A - 1, A, A + 1, C - 1, C]): bad[r, k[i], n - 1] = True
        bad[r, k[6]] = True
    d = planted(rng, a, bad, [0, 8])
    d["x"].reshape(N, 8, 16, C, 4)[e, h, 8, :, 0] = np.where(np.arange(C) % 2 == 1, -2.0 ** 28, 2.0 ** 28).astype(np.float32).astype(BF)
    d["v"][:, 16 * h + 8] = 0
    return d
def setup_inputs_forks(rng):
    a, bad = np.zeros((N, 8, C), np.int64), np.zeros((N, 8, C), bool)
    for r in range(N):
        k = rng.permutation(8)
        for i, h in enumerate([2, A, A + 1, C - 1]):
            a[r, k[i]] = fork(h)
            bad[r, k[i], [h - 1, C - 1]] = True
        bad[r, k[1], 0] = True
        for i, b in enumerate([comb(), rake(), halves()]):
            a[r, k[4 + i]] = b
            bad[r, k[4 + i]] = ~np.isin(np.arange(C), b)
        a[r, k[7]] = grown(rng)
        bad[r, k[7]] = True
    return planted(rng, a, bad)
def setup_inputs_spread(rng):
    d = setup_inputs(rng)
    d["x"] = big(wide(rng, N, 128, 4 * C, cols=6))
    return d
def check_inputs(d):
    b = []
    for k in ("x", "u", "v"):
        a = np.abs(d[k].astype(np.float32))
        if not (np.isfinite(a).all() and ((a == 0) | (a >= 2.0 ** -30) & (a <= 2.0 ** 30)).all()): b.append("a value of " + k)
    none, least, most = [emit(mx_ref.quantize(np.full((128, 16), k, np.float32).astype(BF)))[1][0, 0] for k in (0.0, 2.0 ** -30, 2.0 ** 30)]
    g, n = np.arange(8)[:, None], np.arange(C)
    for r in range(N):
        if ((d["wc"][r] == 0x7F) | (d["wc"][r] == 0xFF)).any(): b.append("wc: a code that is no number")
        s = mx_ref.live(d["ws"][r])
        if ((s != none) & ((s < least) | (s > most))).any(): b.append("ws: a scale out of range")
        s, p = gentries(d["sz"][r]).astype(np.int64), gentries(d["pr"][r]).astype(np.int64)
        e = n + s
        if (s < 1).any() or (e > C).any() or (s[:, 0] != C).any(): b.append("sz: a size out of range")
        above = np.max(np.where((n[:, None] < n) & (e[:, :, None] > n), n[:, None], -1), axis=1)
        if (above != p).any(): b.append("pr: not the parent")
        elif (e > e[g, np.maximum(p, 0)]).any(): b.append("sz: a subtree that goes beyond the parent's")
        elif np.max(np.sum(p[:, :, None] == n, axis=1)) > 2: b.append("pr: more than two children")
    return b
def reference(x, u, v, wc, ws, sz, pr):
    qu = [mx_ref.quantize(u[r]) for r in range(N)]
    lay = [pk(wc[r], ws[r]) for r in range(N)]
    now = [x[r] for r in range(N)]
    for t in range(R):
        sent, paths = [], []
        for r in range(N):
            q = mx_ref.quantize(now[r])
            p = mx_ref.matmul(qu[r], q)
            sent.append(q)
            paths.append(layout(p[::16] > 0, gentries(sz[r]), gentries(pr[r])))
        came = decode(join(*sent)).astype(BF)
        made = []
        for r in range(N):
            e = (r - STEP[t]) % N
            z = np.concatenate([differences(cut(came, e, 4 * C), *paths[e])[:, :4 * A], differences(now[r], *paths[r])[:, 4 * A:]], axis=1)
            q = mx_ref.quantize(np.ascontiguousarray(z))
            made.append(tile([mx_ref.matmul(pick(lay[r], np.arange(128 * b, 128 * b + 128)), q) * np.float32(0.0078125) + z[:, b::4].astype(np.float32) for b in range(4)]))
        now = made
    y, ot = np.zeros((N, 128, C), np.float32), np.zeros((N, 8, C), np.float32)
    oc, osc = np.zeros((N, 128, 4 * C), np.uint8), np.zeros((N, 16, C), np.uint8)
    for r in range(N):
        q = mx_ref.quantize(now[r])
        y[r] = mx_ref.matmul(mx_ref.quantize(v[r]), q)
        ot[r] = paths[r][0]
        oc[r], osc[r] = emit(q)
    return {"y": y, "ot": ot, "oc": oc, "osc": osc}

@@ -1,0 +1,522 @@
+from concourse.mybir import dt, AluOpType, ActivationFunctionType
+
+C, A, NR = 384, 192, 3
+STEP = [1, 2, 4]
+W = 1152
+B = 2048.0
+LAM = 512.0
+MAGIC = 12582912.0
+NS = 14
+P = C + 16
+
+F, H, I, U, Q, S = "float32", "bfloat16", "int32", "uint16", "float8_e4m3fn_x4", "uint8"
+SCRATCH = {}
+
+
+def _sb(dtype, **kw):
+    for k in kw:
+        SCRATCH[k] = ("sbuf", [128, kw[k]], dtype)
+
+
+_sb(H, x0=4 * C, xt=4 * C, xp=4 * C, xq=4 * P, yp=4 * P, zt=4 * C, z128=4 * C, ut=512, vt=512, et=2048, junk=4800,
+    sg=C, pp=C + 16, pb=C, eb=C, dy=C, qq=C, oddx=C + 16, neg2=C, ones=C, go=4 * 208, gr=4 * 208)
+_sb(Q, qu=128, qur=128, qv=128, qe=512, qw=512, qz=C, qx0=C, qx1=C, qx2=C, qx3=C, ql0=C, ql1=C, ql2=C)
+_sb(S, su=128, sur=128, sv=128, se=512, sw=512, szz=C, sx0=C, sx1=C, sx2=C, sx3=C, sl0=C, sl1=C, sl2=C)
+_sb(I, tz=24, tp=24, i1=24, i2=24, i3=16, wi=24, oi=24, oj=24)
+_sb(U, lend=24, lpr=24, loff=24, lpost=24, lcl=24, lhinv=24, lh=24, luph=24, lj1=24, lj2=24, lj3=24, ld=24, ldw=24,
+    lca=24, lsg=24, lsib=24, lnm=24, lp16=24, llt=24, lu=8, l1=24, l2=24, lpos=24,
+    lst0=48, lst1=48, lst2=48, ll0=48, ll1=48, ll2=48)
+_sb(F, iot=408, iob=1416, sm=24 * 56, c16=48, cor=16, cv1=C, cv2=C, er=392, ra=C, rb=C, rc=C, rd=392, nh=392, sc=C, sc2=C,
+    prr=C, hr=C, nhd=C, cde=C, d1=C, nd=C, ndf=C, ca=C, sgn=C, dw=W, aw=W, bt=W, b2=W, base=W + 8,
+    dx=C, rp=392, m0=C, m1=C, ma=C, mb=C, nr=C, yy=C, orow=392, otr=C, yo=C)
+SCRATCH["pd"] = ("psum", [128, 2048], F)
+SCRATCH["pq"] = ("psum", [128, 2048], F)
+
+SEMAPHORES = (["v%d" % i for i in range(NS)] + ["a%d" % i for i in range(NS)] + ["p%d" % i for i in range(NS)]
+              + ["g%d" % i for i in range(NS)] + ["ltree", "lu_", "lx", "lw", "lv", "sent", "out"]
+              + ["ac%d" % t for t in range(NR)] + ["al%d" % t for t in range(NR)])
+
+
+def rank_program(g, core, T, topo):
+    rank = T.rank_of(core)
+    if rank is None:
+        return
+    op_ = AluOpType
+    act = ActivationFunctionType
+    n_ranks = len(T.cores)
+    eng = {"v": g.vector, "a": g.scalar, "p": g.tensor, "g": g, "s": g.sync}
+    known = {e: {} for e in eng}
+    turn = {e: 0 for e in eng}
+    count = {}
+    writer, readers = {}, {}
+
+    def need(e, ev):
+        sem, n, seen = ev
+        if known[e].get(sem, 0) < n:
+            eng[e].wait_ge(T.sem[sem], n)
+            known[e][sem] = n
+        for k in seen:
+            if known[e].get(k, 0) < seen[k]:
+                known[e][k] = seen[k]
+
+    def before(e, r, w):
+        evs = [writer[k] for k in r + w if k in writer]
+        for k in w:
+            evs = evs + readers.get(k, [])
+        for ev in reversed(evs):
+            need(e, ev)
+
+    def after(ev, r, w):
+        for k in r:
+            readers.setdefault(k, []).append(ev)
+        for k in w:
+            writer[k] = ev
+            readers[k] = []
+
+    def run(e, r, w, make):
+        r, w = r.split(), w.split()
+        before(e, r, w)
+        sem = "%s%d" % (e, turn[e] % NS)
+        turn[e] += 1
+        n = count.get(sem, 0)
+        if n:
+            need(e, (sem, n, {}))
+        make().then_inc(T.sem[sem], 1)
+        count[sem] = n + 1
+        after((sem, n + 1, dict(known[e])), r, w)
+
+    def dmas(e, sem, r, w, pairs):
+        r, w = r.split(), w.split()
+        before(e, r, w)
+        for o, i in pairs:
+            eng[e].dma_start(o, i).then_inc(T.sem[sem], 16)
+        count[sem] = count.get(sem, 0) + 16 * len(pairs)
+        after((sem, count[sem], dict(known[e])), r, w)
+
+    V = g.vector
+
+    def tt(r, w, out, a, b, o):
+        run("v", r, w, lambda: V.tensor_tensor(out, a, b, o))
+
+    def ts(r, w, out, a, s1, o1, s2=None, o2=None):
+        if o2 is None:
+            run("v", r, w, lambda: V.tensor_scalar(out, a, s1, None, o1))
+        else:
+            run("v", r, w, lambda: V.tensor_scalar(out, a, s1, s2, o1, o2))
+
+    def cp(r, w, out, a):
+        run("v", r, w, lambda: V.tensor_copy(out, a))
+
+    def scan(r, w, out, a, b, init, o1, o2):
+        run("v", r, w, lambda: V.tensor_tensor_scan(out, a, b, init, o1, o2))
+
+    def fill(w, out, c):
+        run("v", "", w, lambda: V.memset(out, c))
+
+    def ac(r, w, out, a, scale=1.0, bias=0.0, func=None):
+        f = func
+        if f is None:
+            f = act.Copy if bias == 0.0 else act.Identity
+        if f == act.Copy:
+            run("a", r, w, lambda: g.scalar.activation(out, a, f, scale=scale))
+        else:
+            run("a", r, w, lambda: g.scalar.activation(out, a, f, bias=bias, scale=scale))
+
+    def iota(w, out, pat, base, cm, small):
+        if small:
+            run("g", "", w, lambda: g.iota(out, pat, base, cm, allow_small_or_imprecise_dtypes=True))
+        else:
+            run("g", "", w, lambda: g.iota(out, pat, base, cm))
+
+    def quant(r, w, q, s, x):
+        run("v", r, w, lambda: V.quantize_mx(q, s, x))
+
+    def mm(r, w, out, lq, ls, rq, rs):
+        run("p", r, w, lambda: g.tensor.matmul_mx(out, lq, ls, rq, rs, True, True))
+
+    slot = {}
+
+    def sm(name):
+        if name not in slot:
+            slot[name] = len(slot)
+        return T.sm[:, 24 * slot[name]:24 * slot[name] + 24]
+
+    def cor(j):
+        return T.cor[:, j:j + 1]
+
+    def ind(buf, n, lst):
+        return T[buf][:, 0:n].indirect(T[lst][:, 0:24])
+
+    def conv(r, src, dst="sc", const="cv1"):
+        scan(r + " " + const, dst, T[dst][:, 0:C], src, T[const][:, 0:C], 2.0 * B * (1.0 if const == "cv1" else 4096.0), op_.min, op_.add)
+        return T[dst][:, 15:C:16]
+
+    add, sub, mul, mx, mn = op_.add, op_.subtract, op_.mult, op_.max, op_.min
+
+    dmas("a", "ltree", "", "tz tp", [(T.tz[:], T.sz[:]), (T.tp[:], T.pr[:])])
+    dmas("s", "lx", "", "x0", [(T.x0[:], T.x[:])])
+    dmas("a", "lu_", "", "ut", [(T.ut[:], T.u[:])])
+    dmas("s", "lw", "x0", "qw", [(T.qw[:].bitcast(dt.uint8), T.wc[:]), (T.sw[:], T.ws[:])])
+    dmas("s", "lv", "", "vt", [(T.vt[:], T.v[:])])
+
+    iota("i1", T.i1[:], [[0, 24]], 0, 1, False)
+    iota("i2", T.i2[:], [[16, 24]], 0, 0, False)
+    iota("i3", T.i3[:], [[1, 16]], 128, -1, False)
+    iota("iot", T.iot[:], [[1, 408]], 0, 0, True)
+    iota("iob", T.iob[:], [[1, 1416]], 0, 0, True)
+    iota("et", T.et[:], [[0, 2048]], 1, 0, True)
+
+    fill("er_", T.er[:, C:392], float(C))
+    fill("neg2", T.neg2[:], -2.0)
+    ts("i1", "i1", T.i1[:], T.i1[:], 15, op_.bitwise_and)
+    fill("ones", T.ones[:], 1.0)
+    ts("i3", "i3", T.i3[:], T.i3[:], 15, op_.bitwise_and)
+    tt("i1 i2", "n", sm("n"), T.i1[:], T.i2[:], add)
+    cp("i1", "lp16", T.lp16[:], T.i1[:])
+    ts("i3", "c16a", T.c16[:, 16:32], T.i3[:], 0.0, op_.is_equal, -B, mul)
+    ts("i3", "c16b", T.c16[:, 32:48], T.i3[:], 15.0, op_.is_equal, 2.0 * B, mul)
+    ts("i1", "kb", cor(8), T.i1[:, 0:1], 0.0, op_.is_equal, -2.0 * B, mul)
+    ts("n", "nb", sm("nb"), sm("n"), -1.0, mul, -0.5, add)
+    tt("c16a c16b", "c16", T.c16[:, 0:16], T.c16[:, 16:32], T.c16[:, 32:48], add)
+    ts("n", "root", sm("root"), sm("n"), 0.0, op_.is_equal, float(C + 1), mul)
+    ac("iot", "ndf0", T.yy[:], T.iot[:, 0:C], 1.0 / 2048)
+    ac("c16 lp16", "cv1", T.cv1[:], ind("c16", 16, "lp16"))
+    for j, (m, c) in enumerate([(1.0, B), (1.0, B - 511.0), (-2.0, -2.0 * B), (1.0, B + MAGIC), (4096.0, 4096.0 * B),
+                                (-8192.0, -8192.0 * B), (-2.0, 1.0 - 2.0 * B), (1.0, B - 1.125)]):
+        ts("kb", "k%d" % j, cor(j), cor(8), m, mul, c, add)
+    cp("i2", "lu", T.lu[:], T.i2[:, 0:8])
+    ts("n", "t5", sm("t5"), sm("n"), 2.0, mul, -16.0, add)
+    tt("tz n", "end", sm("end"), T.tz[:], sm("n"), add)
+    tt("tp root", "prc", sm("prc"), T.tp[:], sm("root"), add)
+    cp("end", "lend", T.lend[:], sm("end"))
+    cp("prc", "lpr", T.lpr[:], sm("prc"))
+    cp("iot lend", "er", T.er[:, 0:C], ind("iot", 392, "lend"))
+
+    at = 0
+    for c in range(23, -1, -1):
+        n = 16 * (c + 1)
+        run("a", "er nb", "dc%d" % c, lambda: g.scalar.activation(
+            T.junk[:, at:at + n], T.er[:, 0:n], act.Sign, bias=sm("nb")[:, c:c + 1], scale=1.0, accum_out=sm("dc")[:, c:c + 1]))
+        at += n
+
+    ts("tp", "pr1", sm("pr1"), T.tp[:], 1.0, add)
+    cp("er er_ lpr", "ra", T.ra[:], ind("er", 392, "lpr"))
+    tt("n pr1", "b", sm("b"), sm("n"), sm("pr1"), sub)
+    s = conv("ra", T.ra[:])
+    tt("b tz", "l2_", sm("l2_"), sm("b"), T.tz[:], op_.is_ge)
+    ts("sc k0", "ep", sm("ep"), s, cor(0), add)
+    ts("pr1", "lnm", T.lnm[:], sm("pr1"), 2.0, mul, float(C + 1), add)
+    tt("ep end", "a", sm("a"), sm("ep"), sm("end"), sub)
+    ts("b", "iss", sm("iss"), sm("b"), 0.0, op_.is_gt)
+    tt("a tz", "l1_", sm("l1_"), sm("a"), T.tz[:], op_.is_gt)
+    tt("a b", "szs", sm("szs"), sm("a"), sm("b"), add)
+    tt("l1_ l2_", "light", sm("light"), sm("l1_"), sm("l2_"), add)
+    ts("a", "isf", sm("isf"), sm("a"), 0.0, op_.is_gt)
+    tt("light szs", "off", sm("off"), sm("light"), sm("szs"), mul)
+    cp("light", "llt", T.llt[:], sm("light"))
+    ts("off", "loff", T.loff[:], sm("off"), 1.0, add)
+    ac("iot loff", "rb", T.rb[:], ind("iot", 392, "loff"))
+    tt("end isf", "t1", sm("t1"), sm("end"), sm("isf"), mul)
+    tt("iss isf", "t2", sm("t2"), sm("iss"), sm("isf"), sub)
+    ts("t1", "lsib", T.lsib[:], sm("t1"), 2.0, mul, float(C + 1), add)
+    ts("t2", "lsg", T.lsg[:], sm("t2"), 1.0, add)
+    ts("t2", "t6", sm("t6"), sm("t2"), -LAM, mul, LAM + 1.0, add)
+    tt("t5 i2", "st2", sm("st2"), sm("t5"), T.i2[:], sub)
+    tt("t6 iss", "t3", sm("t3"), sm("t6"), sm("iss"), sub)
+    ts("isf", "t4", sm("t4"), sm("isf"), -512.0, mul, 512.0, add)
+
+    quant("x0", "qxo0 qxr0", T.qx0[:], T.sx0[:], T.x0[:])
+    quant("ut", "qu", T.qu[:], T.su[:], T.ut[:])
+    fill("pp_", T.pp[:, 0:1], 32.0)
+    cp("qu lu", "qur", T.qur[:].bitcast(dt.uint32), T.qu[:].bitcast(dt.uint32).indirect(T.lu[:]))
+    cp("qu lu", "sur", T.sur[:], T.su[:].indirect(T.lu[:]))
+
+    def send(t, what):
+        dst = T.cores[(rank + STEP[t]) % n_ranks]
+        rid, pid, _ = topo.addr(dst)
+        mask = topo.mask(core, dst)
+        k = len(topo.engines(core, dst))
+        if what == "codes":
+            r = ["qxo%d" % t, "qxr%d" % t]
+            pairs = [(T["ql%d" % t][:].bitcast(dt.uint8), T["qx%d" % t][:].bitcast(dt.uint8)), (T["sl%d" % t][:], T["sx%d" % t][:])]
+            sem = "ac%d" % t
+        else:
+            r = ["lsto%d" % t, "lstf%d" % t]
+            pairs = [(T["ll%d" % t][:, 0:38], T["lst%d" % t][:, 0:38])]
+            sem = "al%d" % t
+        before("g", r, [])
+        for o, i in pairs:
+            g.remote_dma(o, i, T.sem[sem], T.sem.sent, pid, rid, mask)
+        count["sent"] = count.get("sent", 0) + k * len(pairs)
+        src = T.cores[(rank - STEP[t]) % n_ranks]
+        count[sem] = len(topo.engines(src, core)) * len(pairs)
+        writer[sem] = (sem, count[sem], {})
+
+    def score(t, own):
+        h, c0, bank = ("o", A, 0) if own else ("r", 0, 1)
+        qx, sx = T["qx%d" % t], T["sx%d" % t]
+        mm("qur sur qx%s%d" % (h, t), "pd%d" % bank, T.pd[:, 512 * bank:512 * bank + A], T.qur[:], T.sur[:], qx[:, c0:c0 + A], sx[:, c0:c0 + A])
+
+    def signs(own):
+        h, c0, bank = ("o", A, 0) if own else ("r", 0, 1)
+        ts("pd%d" % bank, "sg" + h, T.sg[:, c0:c0 + A], T.pd[:, 512 * bank:512 * bank + A], 0.0, op_.is_gt, 0.5, sub)
+
+    def front(t):
+        scan("sgo sgr neg2", "pp", T.pp[:, 1:C + 1], T.sg[:], T.neg2[:], 32.0, mul, mul)
+        scan("sgo sgr neg2", "pb", T.pb[:], T.sg[:], T.neg2[:], 32.0, mul, mul)
+        ac("sgo sgr", "dx", T.dx[:], T.sg[:], 2047.0, -0.5)
+        ac("sgo sgr", "dy", T.dy[:], T.sg[:], 2048.0)
+        tt("pp pp_ pb lend", "eb", T.eb[:], ind("pp", C + 1, "lend"), T.pb[:], mul)
+        tt("eb dx", "rp", T.rp[:, 0:C], T.eb[:], T.dx[:], mx)
+
+    def parity(t):
+        tt("eb dy", "qq", T.qq[:], T.eb[:], T.dy[:], add)
+        ac("qq", "oddx", T.oddx[:, 1:C + 1], T.qq[:], 1.0 / 2048, 0.0, act.Abs)
+
+    score(0, True)
+    score(0, False)
+    send(0, "codes")
+    run("g", "et", "et", lambda: g.affine_select(T.et[:], T.et[:], [[-1, 4], [1, 512]], op_.is_equal, 0.0, 0, -4))
+    iota("bt", T.bt[:], [[0, W]], 0, 0, True)
+    iota("aw", T.aw[:], [[0, W]], -2048, 0, True)
+    iota("b2", T.b2[:], [[0, W]], 0, 0, True)
+    for b in range(4):
+        iota("xq_%d" % b, T.xq[:, P * b:P * b + 16], [[0, 16]], 0, 0, True)
+        iota("yp_%d" % b, T.yp[:, P * b:P * b + 16], [[0, 16]], 0, 0, True)
+    tt("iot lpr ndf0", "prr", T.prr[:], ind("iot", 392, "lpr"), T.yy[:], add)
+    signs(True)
+    signs(False)
+
+    dcs = " ".join("dc%d" % c for c in range(24))
+    tt(dcs + " st2", "d2", sm("d2"), sm("dc"), sm("st2"), add)
+    fill("rd_", T.rd[:, 0:1], 512.0)
+    ts("d2", "d", sm("d"), sm("d2"), 0.5, mul)
+    fill("nh_", T.nh[:, C:392], 511.0)
+    tt("end d", "t8", sm("t8"), sm("end"), sm("d"), sub)
+    tt("n d", "t9", sm("t9"), sm("n"), sm("d"), sub)
+    ts("t8", "lpost", T.lpost[:], sm("t8"), -1.0, add)
+    cp("t9", "lcl", T.lcl[:], sm("t9"))
+    cp("rb lpost", "ra", ind("ra", C, "lpost"), T.rb[:])
+    scan("rb", "rc", T.rc[:], T.rb[:], T.rb[:], 0.0, add, mx)
+    scan("ra", "rd", T.rd[:, 1:C + 1], T.ra[:], T.ra[:], 512.0, add, mx)
+    cp("d", "ld", T.ld[:], sm("d"))
+    fill("rp_", T.rp[:, C:392], 1023.0)
+    tt("rd rd_ lcl rc", "nh", T.nh[:, 0:C], ind("rd", C + 1, "lcl"), T.rc[:], sub)
+    tt("d t3", "t10", sm("t10"), sm("d"), sm("t3"), add)
+    s = conv("nh", T.nh[:, 0:C])
+    tt("d t4", "t11", sm("t11"), sm("d"), sm("t4"), add)
+    ts("sc k1", "lhinv", T.lhinv[:], s, cor(1), add, -1.0, mul)
+    cp("t10", "ldw", T.ldw[:], sm("t10"))
+    cp("prr lhinv", "hr", ind("hr", C, "lhinv"), T.prr[:])
+    cp("t11", "lca", T.lca[:], sm("t11"))
+    s = conv("hr", T.hr[:])
+    ts("n k4", "i1c", sm("i1c"), sm("n"), 2048.0, mul, cor(4), sub)
+    ts("sc k0", "wi", T.wi[:], s, cor(0), add, 2048.0, mul)
+    fill("base_", T.base[:, C:C + 1], 0.0)
+    ts("wi", "oj", T.oj[:], T.wi[:], 11, op_.arith_shift_right)
+    ts("wi", "oi", T.oi[:], T.wi[:], 2047, op_.bitwise_and)
+    cp("oj", "luph", T.luph[:], T.oj[:])
+    cp("oi", "lh", T.lh[:], T.oi[:])
+    ac("iot llt", "m0", T.m0[:], ind("iot", 392, "llt"), -1.0, 1.0)
+    ac("cv1", "cv2", T.cv2[:], T.cv1[:], 4096.0)
+    ac("iot ld", "nd", T.nd[:], ind("iot", 392, "ld"), -1.0)
+    ac("nd", "d1", T.d1[:], T.nd[:], -1.0, 1.0)
+    ac("nd", "dw0", T.dw[:, 0:C], T.nd[:], -1.0)
+    ac("nd", "dw1", T.dw[:, C:3 * C:2], T.nd[:], -1.0)
+    ac("iot lsg", "sgn", T.sgn[:], ind("iot", 392, "lsg"), 1.0, -1.0)
+    ac("iob lca", "ca", T.ca[:], ind("iob", 1416, "lca"), -2.0, 1.0)
+    front(0)
+    ac("nh nh_ luph", "rb", T.rb[:], ind("nh", 392, "luph"))
+    ac("m0 lh", "nhd", T.nhd[:], ind("m0", C, "lh"))
+    ac("iot lh", "cde", T.cde[:], ind("iot", 392, "lh"), 2.0, float(C + 1 - 1024))
+    parity(0)
+    scan("nhd rb", "ra", T.ra[:], T.nhd[:], T.rb[:], 0.0, mul, mx)
+
+    def top(t):
+        tt("rp rp_ luph cde", "m1", T.m1[:], ind("rp", 392, "luph"), T.cde[:], add)
+        scan("nhd m1", "m0", T.m0[:], T.nhd[:], T.m1[:], 0.0, mul, mx)
+        ac("m0", "ma", T.ma[:], T.m0[:])
+
+    def jump(out, win, lst, other):
+        tt("%s %s %s" % (win, lst, other), out, T[out][:], ind(win, C, lst), T[other][:], mx)
+
+    fill("oddx_", T.oddx[:, 0:1], 1.0)
+    s = conv("ra", T.ra[:])
+    fill("orow_", T.orow[:, 7:8], 0.0)
+    ts("sc k1", "lj1", T.lj1[:], s, cor(1), add, -1.0, mul)
+    ac("ra lj1", "rb", T.rb[:], ind("ra", C, "lj1"))
+    top(0)
+    ac("rb lj1", "rc", T.rc[:], ind("rb", C, "lj1"))
+    s = conv("rb", T.rb[:])
+    jump("m1", "m0", "lj1", "ma")
+    ts("sc k1", "lj2", T.lj2[:], s, cor(1), add, -1.0, mul)
+    s = conv("rc", T.rc[:], "sc2")
+    jump("mb", "m1", "lj1", "m0")
+    ts("sc2 k1", "lj3", T.lj3[:], s, cor(1), add, -1.0, mul)
+    ac("iob ldw", "dw2", T.dw[:, C + 1:3 * C:2], ind("iob", 1416, "ldw"), 1.0, -LAM - 1.0)
+
+    def unpack(t):
+        for b in range(4):
+            mm("qe ac%d" % t, "pd%d" % b, T.pd[:, 512 * b:512 * b + C], T.qe[:, 128 * b:128 * b + 128], T.se[:, 128 * b:128 * b + 128],
+               T["ql%d" % t][:], T["sl%d" % t][:])
+        for b in range(4):
+            ac("pd%d" % b, "yp%d" % b, T.yp[:, P * b + 16:P * b + P], T.pd[:, 512 * b:512 * b + C])
+
+    for t in range(NR):
+        lst, ll = T["lst%d" % t], T["ll%d" % t]
+        if t:
+            front(t)
+            top(t)
+            parity(t)
+            jump("m1", "m0", "lj1", "ma")
+            jump("mb", "m1", "lj1", "m0")
+        ac("nd", "bt", T.bt[:, C:3 * C:2], T.nd[:], -1.0)
+        jump("m0", "mb", "lj2", "m1")
+        if t == 0:
+            quant("et", "qe", T.qe[:], T.se[:], T.et[:])
+        jump("m1", "m0", "lj3", "mb")
+        for b in range(4):
+            if t:
+                ac("xpo%d xpr%d" % (b, b), "xq%d" % b, T.xq[:, P * b + 16:P * b + P], T.xp[:, C * b:C * b + C], 0.0078125)
+            else:
+                ac("x0", "xq%d" % b, T.xq[:, P * b + 16:P * b + P], T.x0[:, b:4 * C:4])
+        unpack(t)
+        tt("m1 lhinv qq", "m0", T.m0[:], ind("m1", C, "lhinv"), T.qq[:], mul)
+        if t == 0:
+            tt("iot ld ndf0", "ndf", T.ndf[:], ind("iot", 392, "ld"), T.yy[:], sub)
+        s = conv("m0", T.m0[:], "sc", "cv2")
+        tt("sc i1c", "l1g", sm("l1g"), s, sm("i1c"), mx)
+        ts("sc k5", "l2a", sm("l2a"), s, -1.0, mul, cor(5), add)
+        ts("l1g k4", "l1", T.l1[:], sm("l1g"), cor(4), add, 1.0 / 2048, mul)
+        tt("l1g l2a", "l2g", sm("l2g"), sm("l2a"), sm("l1g"), mx)
+        cp("d1 l1", "bt", ind("bt", W, "l1"), T.d1[:])
+        ts("l2g k4", "l2", T.l2[:], sm("l2g"), cor(4), add, 1.0 / 2048, mul)
+        tt("bt lsib ca", "aw", T.aw[:, C + 1:3 * C:2], ind("bt", W, "lsib"), T.ca[:], add)
+        tt("dw0 dw1 dw2 l2 ndf", "nr", T.nr[:], ind("dw", W, "l2"), T.ndf[:], sub)
+        tt("aw l1 nd", "yy ndf0", T.yy[:], ind("aw", W, "l1"), T.nd[:], mx)
+        scan("bt yy", "base0", T.base[:, C + 2:3 * C + 2:2], T.bt[:, C:3 * C:2], T.yy[:], 0.0, add, add)
+        tt("base0 base_ nr", "m1", T.m1[:], T.base[:, C:3 * C:2], T.nr[:], sub)
+        scan("base0 oddx oddx_ ones", "base1", T.base[:, 0:C], T.ones[:], T.oddx[:, 0:C], T.base[:, 3 * C:3 * C + 1], add, sub)
+        cp("m1 l1", "b2", ind("b2", W, "l1"), T.m1[:])
+        tt("b2 lnm sgn", "base2", T.base[:, C + 1:3 * C:2], ind("b2", W, "lnm"), T.sgn[:], mul)
+        tt("base0 base1 base2 base_ l2 nr", "m0", T.m0[:], ind("base", W, "l2"), T.nr[:], sub)
+        s = conv("m0", T.m0[:])
+        ts("sc k2", "g1", sm("g1"), s, -1.0, mul, cor(2), add)
+        tt("sc g1", "g2", sm("g2"), s, sm("g1"), mx)
+        ts("g2 k3", "lpos", T.lpos[:], sm("g2"), cor(3), add, MAGIC, sub)
+        cp("nr lpos", "orow", T.orow[:, 8:8 + C].indirect(T.lpos[:]), T.nr[:])
+        s = conv("orow", T.orow[:, 8:8 + C])
+        s2 = conv("orow orow_", T.orow[:, 7:7 + C], "sc2")
+        ts("sc k0", "wi", T.wi[:], s, cor(0), add, 2048.0, mul)
+        ts("sc k6", "f1", sm("f1"), s, -1.0, mul, cor(6), add)
+        ts("wi", "oi", T.oi[:], T.wi[:], 2047, op_.bitwise_and)
+        tt("sc2 f1", "f2", sm("f2"), s2, sm("f1"), mx)
+        ts("oi", "lsto%d" % t, lst[:, 0:24], T.oi[:], 16.0, add)
+        ts("f2 k7", "f3", sm("f3"), sm("f2"), cor(7), add, 1024.0, mul)
+        if t == 0:
+            fill("go_", T.go[:, A:4 * 208:208], 0.0)
+        tt("f3 oi", "f4", sm("f4"), sm("f3"), T.oi[:], mn)
+        ts("f4", "lstf%d" % t, lst[:, 24:48], sm("f4"), 16.0, add)
+        send(t, "lists")
+
+        qn, sn = T["qx%d" % (t + 1)], T["sx%d" % (t + 1)]
+
+        def gath(b, own):
+            if own:
+                ac("xq%d xq_%d lstf%d" % (b, b, t), "go%d" % b, T.go[:, 208 * b:208 * b + A], T.xq[:, P * b:P * b + P].indirect(lst[:, 36:48]))
+            else:
+                ac("yp%d yp_%d al%d" % (b, b, t), "gr%d" % b, T.gr[:, 208 * b:208 * b + 208], T.yp[:, P * b:P * b + P].indirect(ll[:, 24:37]))
+
+        def diff(b, own):
+            if own:
+                tt("xq%d xq_%d go%d go_ lsto%d" % (b, b, b, t), "zo%d" % b, T.zt[:, 4 * A + b:4 * C:4],
+                   T.xq[:, P * b:P * b + P].indirect(lst[:, 12:24]), T.go[:, 208 * b + 1:208 * b + 1 + A], sub)
+            else:
+                tt("yp%d yp_%d gr%d al%d" % (b, b, b, t), "zr%d" % b, T.zt[:, b:4 * A:4],
+                   T.yp[:, P * b:P * b + P].indirect(ll[:, 0:12]), T.gr[:, 208 * b + 1:208 * b + 1 + A], sub)
+
+        def big(b, own):
+            h, c0 = ("o", A) if own else ("r", 0)
+            ac("z%s%d" % (h, b), "zb%s%d" % (h, b), T.z128[:, C * b + c0:C * b + c0 + A], T.zt[:, 4 * c0 + b:4 * (c0 + A):4], 128.0)
+
+        def product(own):
+            h, c0, ps, pn = ("o", A, T.pd, "pd") if own else ("r", 0, T.pq, "pq")
+            quant("z%s0 z%s1 z%s2 z%s3" % (h, h, h, h), "qz" + h, T.qz[:, c0:c0 + A], T.szz[:, c0:c0 + A], T.zt[:, 4 * c0:4 * (c0 + A)])
+            for b in range(4):
+                mm("qw qz" + h, "%s%d" % (pn, b), ps[:, 512 * b:512 * b + A], T.qw[:, 128 * b:128 * b + 128], T.sw[:, 128 * b:128 * b + 128],
+                   T.qz[:, c0:c0 + A], T.szz[:, c0:c0 + A])
+
+        def state(b, own):
+            h, c0, ps, pn = ("o", A, T.pd, "pd") if own else ("r", 0, T.pq, "pq")
+            tt("%s%d zb%s%d" % (pn, b, h, b), "xp%s%d" % (h, b), T.xp[:, C * b + c0:C * b + c0 + A], ps[:, 512 * b:512 * b + A],
+               T.z128[:, C * b + c0:C * b + c0 + A], add)
+
+        def tile(b, own):
+            h, c0 = ("o", A) if own else ("r", 0)
+            ac("xp%s%d" % (h, b), "xt%s%d" % (h, b), T.xt[:, 4 * c0 + b:4 * (c0 + A):4], T.xp[:, C * b + c0:C * b + c0 + A], 0.0078125)
+
+        def pack(own):
+            h, c0 = ("o", A) if own else ("r", 0)
+            quant("xt%s0 xt%s1 xt%s2 xt%s3" % (h, h, h, h), "qx%s%d" % (h, t + 1), qn[:, c0:c0 + A], sn[:, c0:c0 + A], T.xt[:, 4 * c0:4 * (c0 + A)])
+
+        def outputs(own):
+            h, c0, bank = ("o", A, 0) if own else ("r", 0, 1)
+            key = "qx%s3" % h
+            mm("qv " + key, "pd%d" % bank, T.pd[:, 512 * bank:512 * bank + A], T.qv[:], T.sv[:], qn[:, c0:c0 + A], sn[:, c0:c0 + A])
+            dmas("s", "out", key, "", [(T.oc[:, 4 * c0:4 * (c0 + A)], qn[:, c0:c0 + A].bitcast(dt.uint8))]
+                 + [(T.osc[4 * k:4 * k + 4, c0:c0 + A], sn[32 * k:32 * k + 4, c0:c0 + A]) for k in range(4)])
+
+        def result(own):
+            h, c0, bank = ("o", A, 0) if own else ("r", 0, 1)
+            ac("pd%d" % bank, "yo" + h, T.yo[:, c0:c0 + A], T.pd[:, 512 * bank:512 * bank + A])
+            dmas("a", "out", "yo" + h, "", [(T.y[:, c0:c0 + A], T.yo[:, c0:c0 + A])])
+
+        for b in range(4):
+            gath(b, True)
+        for b in range(4):
+            diff(b, True)
+        for b in range(4):
+            big(b, True)
+        if t == NR - 1:
+            ac("iot lsto%d" % t, "otr", T.otr[:], T.iot[:, 0:408].indirect(lst[:, 0:24]), 1.0, -16.0)
+            dmas("s", "out", "otr", "", [(T.ot[k:k + 1, :], T.otr[16 * k:16 * k + 1, :]) for k in range(8)])
+        product(True)
+        if t == NR - 1:
+            quant("vt", "qv", T.qv[:], T.sv[:], T.vt[:])
+        for b in range(4):
+            state(b, True)
+        tile(0, True)
+        tile(1, True)
+        for b in range(4):
+            gath(b, False)
+        for b in range(4):
+            diff(b, False)
+        tile(2, True)
+        big(0, False)
+        tile(3, True)
+        for b in range(1, 4):
+            big(b, False)
+        product(False)
+        pack(True)
+        if t == NR - 1:
+            outputs(True)
+        else:
+            score(t + 1, True)
+        for b in range(4):
+            state(b, False)
+            tile(b, False)
+        if t < NR - 1:
+            signs(True)
+        pack(False)
+        if t == NR - 1:
+            result(True)
+            outputs(False)
+            result(False)
+        else:
+            score(t + 1, False)
+            send(t + 1, "codes")
+            signs(False)
+
+    for sem in count:
+        if max(known[e].get(sem, 0) for e in eng) < count[sem]:
+            need("g", (sem, count[sem], {}))

@@ -3,10 +3,10 @@ from concourse.mybir import dt, AluOpType, ActivationFunctionType
 C, A, NR = 384, 192, 3
 STEP = [1, 2, 4]
 W = 1152
-B = 2048.0
-LAM = 512.0
+B = 2560.0
+LAM = 1024.0
+BIG = 4194304.0
 MAGIC = 12582912.0
-NS = 14
 P = C + 16
 
 F, H, I, U, Q, S = "float32", "bfloat16", "int32", "uint16", "float8_e4m3fn_x4", "uint8"
@@ -19,21 +19,20 @@ def _sb(dtype, **kw):
 
 
 _sb(H, x0=4 * C, xt=4 * C, xp=4 * C, xq=4 * P, yp=4 * P, zt=4 * C, z128=4 * C, ut=512, vt=512, et=2048, junk=4800,
-    sg=C, pp=C + 16, pb=C, eb=C, dy=C, qq=C, oddx=C + 16, neg2=C, ones=C, go=4 * 208, gr=4 * 208)
+    sg=C, pp=C + 16, pb=C, eb=C, dy=C, qq=C, oddx=C + 16, neg2=C, ones=512, go=4 * 208, gr=4 * 208)
 _sb(Q, qu=128, qur=128, qv=128, qe=512, qw=512, qz=C, qx0=C, qx1=C, qx2=C, qx3=C, ql0=C, ql1=C, ql2=C)
 _sb(S, su=128, sur=128, sv=128, se=512, sw=512, szz=C, sx0=C, sx1=C, sx2=C, sx3=C, sl0=C, sl1=C, sl2=C)
 _sb(I, tz=24, tp=24, i1=24, i2=24, i3=16, wi=24, oi=24, oj=24)
 _sb(U, lend=24, lpr=24, loff=24, lpost=24, lcl=24, lhinv=24, lh=24, luph=24, lj1=24, lj2=24, lj3=24, ld=24, ldw=24,
-    lca=24, lsg=24, lsib=24, lnm=24, lp16=24, llt=24, lu=8, l1=24, l2=24, lpos=24,
+    lca=24, lb=24, lsib=24, lnm=24, lp16=24, llt=24, lu=8, l1=24, l2=24, lpos=24,
     lst0=48, lst1=48, lst2=48, ll0=48, ll1=48, ll2=48)
-_sb(F, iot=408, iob=1416, sm=24 * 56, c16=48, cor=16, cv1=C, cv2=C, er=392, ra=C, rb=C, rc=C, rd=392, nh=392, sc=C, sc2=C,
-    prr=C, hr=C, nhd=C, cde=C, d1=C, nd=C, ndf=C, ca=C, sgn=C, dw=W, aw=W, bt=W, b2=W, base=W + 8,
+_sb(F, iot=408, iob=1416, tb=896, sm=24 * 56, c16=48, cor=16, cv1=C, cv2=C, er=392, ra=C, rb=C, rc=C, rd=392, nh=392, sc=C,
+    sc2=C, prr=C, hr=C, nhd=C, cde=C, nb2=C, nd=C, ndf=C, ca=C, dw=W, dv=W, aw=W, bt=W, base=W,
     dx=C, rp=392, m0=C, m1=C, ma=C, mb=C, nr=C, yy=C, orow=392, otr=C, yo=C)
 SCRATCH["pd"] = ("psum", [128, 2048], F)
 SCRATCH["pq"] = ("psum", [128, 2048], F)
 
-SEMAPHORES = (["v%d" % i for i in range(NS)] + ["a%d" % i for i in range(NS)] + ["p%d" % i for i in range(NS)]
-              + ["g%d" % i for i in range(NS)] + ["ltree", "lu_", "lx", "lw", "lv", "sent", "out"]
+SEMAPHORES = (["v0", "a0", "p0", "g0", "ltree", "lu_", "lx", "lw", "lv", "sent", "out"]
               + ["ac%d" % t for t in range(NR)] + ["al%d" % t for t in range(NR)])
 
 
@@ -46,7 +45,6 @@ def rank_program(g, core, T, topo):
     n_ranks = len(T.cores)
     eng = {"v": g.vector, "a": g.scalar, "p": g.tensor, "g": g, "s": g.sync}
     known = {e: {} for e in eng}
-    turn = {e: 0 for e in eng}
     count = {}
     writer, readers = {}, {}
 
@@ -63,8 +61,14 @@ def rank_program(g, core, T, topo):
         evs = [writer[k] for k in r + w if k in writer]
         for k in w:
             evs = evs + readers.get(k, [])
-        for ev in reversed(evs):
-            need(e, ev)
+        last = {}
+        for ev in evs:
+            if ev[0] not in last or last[ev[0]][1] < ev[1]:
+                last[ev[0]] = ev
+        evs = [last[k] for k in last]
+        for ev in evs:
+            if not [o for o in evs if o is not ev and o[2].get(ev[0], 0) >= ev[1]]:
+                need(e, ev)
 
     def after(ev, r, w):
         for k in r:
@@ -76,11 +80,8 @@ def rank_program(g, core, T, topo):
     def run(e, r, w, make):
         r, w = r.split(), w.split()
         before(e, r, w)
-        sem = "%s%d" % (e, turn[e] % NS)
-        turn[e] += 1
+        sem = e + "0"
         n = count.get(sem, 0)
-        if n:
-            need(e, (sem, n, {}))
         make().then_inc(T.sem[sem], 1)
         count[sem] = n + 1
         after((sem, n + 1, dict(known[e])), r, w)
@@ -163,13 +164,18 @@ def rank_program(g, core, T, topo):
     iota("i2", T.i2[:], [[16, 24]], 0, 0, False)
     iota("i3", T.i3[:], [[1, 16]], 128, -1, False)
     iota("iot", T.iot[:], [[1, 408]], 0, 0, True)
+    fill("ones", T.ones[:], 1.0)
+    for b in range(4):
+        run("g", "ones", "et%d" % b, lambda: g.affine_select(T.et[:, 512 * b:512 * b + 512], T.ones[:], [[1, 512]], op_.is_equal, 0.0, -b, -4))
     iota("iob", T.iob[:], [[1, 1416]], 0, 0, True)
-    iota("et", T.et[:], [[0, 2048]], 1, 0, True)
+    iota("tb0", T.tb[:, 0:512], [[-1, 512]], 0, 0, True)
+    iota("tb1", T.tb[:, 512:896], [[0, C]], int(BIG) + 1, 0, True)
+    iota("dv", T.dv[:], [[0, W]], int(BIG) + 1, 0, True)
+    iota("bt", T.bt[:], [[0, W]], 0, 0, True)
 
     fill("er_", T.er[:, C:392], float(C))
     fill("neg2", T.neg2[:], -2.0)
     ts("i1", "i1", T.i1[:], T.i1[:], 15, op_.bitwise_and)
-    fill("ones", T.ones[:], 1.0)
     ts("i3", "i3", T.i3[:], T.i3[:], 15, op_.bitwise_and)
     tt("i1 i2", "n", sm("n"), T.i1[:], T.i2[:], add)
     cp("i1", "lp16", T.lp16[:], T.i1[:])
@@ -181,11 +187,13 @@ def rank_program(g, core, T, topo):
     ts("n", "root", sm("root"), sm("n"), 0.0, op_.is_equal, float(C + 1), mul)
     ac("iot", "ndf0", T.yy[:], T.iot[:, 0:C], 1.0 / 2048)
     ac("c16 lp16", "cv1", T.cv1[:], ind("c16", 16, "lp16"))
-    for j, (m, c) in enumerate([(1.0, B), (1.0, B - 511.0), (-2.0, -2.0 * B), (1.0, B + MAGIC), (4096.0, 4096.0 * B),
-                                (-8192.0, -8192.0 * B), (-2.0, 1.0 - 2.0 * B), (1.0, B - 1.125)]):
+    for j, m, c in [(0, 1.0, B), (1, 1.0, B - 511.0), (3, 1.0, B + MAGIC - LAM / 2), (4, 4096.0, 4096.0 * B),
+                    (5, -8192.0, -8192.0 * B), (6, -2.0, 1.0 - 2.0 * B), (7, 1.0, B - 1.125)]:
         ts("kb", "k%d" % j, cor(j), cor(8), m, mul, c, add)
     cp("i2", "lu", T.lu[:], T.i2[:, 0:8])
     ts("n", "t5", sm("t5"), sm("n"), 2.0, mul, -16.0, add)
+    fill("pp_", T.pp[:, 0:1], 32.0)
+    tt("t5 i2", "st2", sm("st2"), sm("t5"), T.i2[:], sub)
     tt("tz n", "end", sm("end"), T.tz[:], sm("n"), add)
     tt("tp root", "prc", sm("prc"), T.tp[:], sm("root"), add)
     cp("end", "lend", T.lend[:], sm("end"))
@@ -217,17 +225,14 @@ def rank_program(g, core, T, topo):
     ts("off", "loff", T.loff[:], sm("off"), 1.0, add)
     ac("iot loff", "rb", T.rb[:], ind("iot", 392, "loff"))
     tt("end isf", "t1", sm("t1"), sm("end"), sm("isf"), mul)
-    tt("iss isf", "t2", sm("t2"), sm("iss"), sm("isf"), sub)
+    ts("isf", "t6", sm("t6"), sm("isf"), LAM, mul, 1.0, add)
     ts("t1", "lsib", T.lsib[:], sm("t1"), 2.0, mul, float(C + 1), add)
-    ts("t2", "lsg", T.lsg[:], sm("t2"), 1.0, add)
-    ts("t2", "t6", sm("t6"), sm("t2"), -LAM, mul, LAM + 1.0, add)
-    tt("t5 i2", "st2", sm("st2"), sm("t5"), T.i2[:], sub)
     tt("t6 iss", "t3", sm("t3"), sm("t6"), sm("iss"), sub)
     ts("isf", "t4", sm("t4"), sm("isf"), -512.0, mul, 512.0, add)
 
     quant("x0", "qxo0 qxr0", T.qx0[:], T.sx0[:], T.x0[:])
     quant("ut", "qu", T.qu[:], T.su[:], T.ut[:])
-    fill("pp_", T.pp[:, 0:1], 32.0)
+    fill("rd_", T.rd[:, 0:1], 512.0)
     cp("qu lu", "qur", T.qur[:].bitcast(dt.uint32), T.qu[:].bitcast(dt.uint32).indirect(T.lu[:]))
     cp("qu lu", "sur", T.sur[:], T.su[:].indirect(T.lu[:]))
 
@@ -276,43 +281,41 @@ def rank_program(g, core, T, topo):
     score(0, True)
     score(0, False)
     send(0, "codes")
-    run("g", "et", "et", lambda: g.affine_select(T.et[:], T.et[:], [[-1, 4], [1, 512]], op_.is_equal, 0.0, 0, -4))
-    iota("bt", T.bt[:], [[0, W]], 0, 0, True)
-    iota("aw", T.aw[:], [[0, W]], -2048, 0, True)
-    iota("b2", T.b2[:], [[0, W]], 0, 0, True)
+    iota("aw", T.aw[:], [[0, W]], -2 * int(BIG), 0, True)
     for b in range(4):
         iota("xq_%d" % b, T.xq[:, P * b:P * b + 16], [[0, 16]], 0, 0, True)
         iota("yp_%d" % b, T.yp[:, P * b:P * b + 16], [[0, 16]], 0, 0, True)
     tt("iot lpr ndf0", "prr", T.prr[:], ind("iot", 392, "lpr"), T.yy[:], add)
     signs(True)
     signs(False)
+    quant("et0 et1 et2 et3", "qe", T.qe[:], T.se[:], T.et[:])
 
     dcs = " ".join("dc%d" % c for c in range(24))
     tt(dcs + " st2", "d2", sm("d2"), sm("dc"), sm("st2"), add)
-    fill("rd_", T.rd[:, 0:1], 512.0)
-    ts("d2", "d", sm("d"), sm("d2"), 0.5, mul)
     fill("nh_", T.nh[:, C:392], 511.0)
+    ts("d2", "d", sm("d"), sm("d2"), 0.5, mul)
+    fill("rp_", T.rp[:, C:392], 1023.0)
     tt("end d", "t8", sm("t8"), sm("end"), sm("d"), sub)
     tt("n d", "t9", sm("t9"), sm("n"), sm("d"), sub)
     ts("t8", "lpost", T.lpost[:], sm("t8"), -1.0, add)
     cp("t9", "lcl", T.lcl[:], sm("t9"))
+    cp("d", "ld", T.ld[:], sm("d"))
     cp("rb lpost", "ra", ind("ra", C, "lpost"), T.rb[:])
     scan("rb", "rc", T.rc[:], T.rb[:], T.rb[:], 0.0, add, mx)
     scan("ra", "rd", T.rd[:, 1:C + 1], T.ra[:], T.ra[:], 512.0, add, mx)
-    cp("d", "ld", T.ld[:], sm("d"))
-    fill("rp_", T.rp[:, C:392], 1023.0)
-    tt("rd rd_ lcl rc", "nh", T.nh[:, 0:C], ind("rd", C + 1, "lcl"), T.rc[:], sub)
     tt("d t3", "t10", sm("t10"), sm("d"), sm("t3"), add)
-    s = conv("nh", T.nh[:, 0:C])
+    tt("rd rd_ lcl rc", "nh", T.nh[:, 0:C], ind("rd", C + 1, "lcl"), T.rc[:], sub)
     tt("d t4", "t11", sm("t11"), sm("d"), sm("t4"), add)
-    ts("sc k1", "lhinv", T.lhinv[:], s, cor(1), add, -1.0, mul)
+    s = conv("nh", T.nh[:, 0:C])
     cp("t10", "ldw", T.ldw[:], sm("t10"))
-    cp("prr lhinv", "hr", ind("hr", C, "lhinv"), T.prr[:])
+    ts("sc k1", "lhinv", T.lhinv[:], s, cor(1), add, -1.0, mul)
     cp("t11", "lca", T.lca[:], sm("t11"))
-    s = conv("hr", T.hr[:])
+    cp("prr lhinv", "hr", ind("hr", C, "lhinv"), T.prr[:])
     ts("n k4", "i1c", sm("i1c"), sm("n"), 2048.0, mul, cor(4), sub)
+    s = conv("hr", T.hr[:])
+    fill("rd_", T.rd[:, 0:1], 0.0)
     ts("sc k0", "wi", T.wi[:], s, cor(0), add, 2048.0, mul)
-    fill("base_", T.base[:, C:C + 1], 0.0)
+    fill("oddx_", T.oddx[:, 0:1], 1.0)
     ts("wi", "oj", T.oj[:], T.wi[:], 11, op_.arith_shift_right)
     ts("wi", "oi", T.oi[:], T.wi[:], 2047, op_.bitwise_and)
     cp("oj", "luph", T.luph[:], T.oj[:])
@@ -320,11 +323,11 @@ def rank_program(g, core, T, topo):
     ac("iot llt", "m0", T.m0[:], ind("iot", 392, "llt"), -1.0, 1.0)
     ac("cv1", "cv2", T.cv2[:], T.cv1[:], 4096.0)
     ac("iot ld", "nd", T.nd[:], ind("iot", 392, "ld"), -1.0)
-    ac("nd", "d1", T.d1[:], T.nd[:], -1.0, 1.0)
+    ac("nd", "nb2", T.nb2[:], T.nd[:], 1.0, -BIG)
     ac("nd", "dw0", T.dw[:, 0:C], T.nd[:], -1.0)
     ac("nd", "dw1", T.dw[:, C:3 * C:2], T.nd[:], -1.0)
-    ac("iot lsg", "sgn", T.sgn[:], ind("iot", 392, "lsg"), 1.0, -1.0)
-    ac("iob lca", "ca", T.ca[:], ind("iob", 1416, "lca"), -2.0, 1.0)
+    ac("iob ldw", "dw2", T.dw[:, C + 1:3 * C:2], ind("iob", 1416, "ldw"), 1.0, -1.0)
+    ac("iob lca", "ca", T.ca[:], ind("iob", 1416, "lca"), -2.0, 1.0 - 2.0 * BIG)
     front(0)
     ac("nh nh_ luph", "rb", T.rb[:], ind("nh", 392, "luph"))
     ac("m0 lh", "nhd", T.nhd[:], ind("m0", C, "lh"))
@@ -340,20 +343,21 @@ def rank_program(g, core, T, topo):
     def jump(out, win, lst, other):
         tt("%s %s %s" % (win, lst, other), out, T[out][:], ind(win, C, lst), T[other][:], mx)
 
-    fill("oddx_", T.oddx[:, 0:1], 1.0)
-    s = conv("ra", T.ra[:])
     fill("orow_", T.orow[:, 7:8], 0.0)
+    s = conv("ra", T.ra[:])
+    fill("go_", T.go[:, A:4 * 208:208], 0.0)
     ts("sc k1", "lj1", T.lj1[:], s, cor(1), add, -1.0, mul)
     ac("ra lj1", "rb", T.rb[:], ind("ra", C, "lj1"))
     top(0)
     ac("rb lj1", "rc", T.rc[:], ind("rb", C, "lj1"))
     s = conv("rb", T.rb[:])
+    tt("iot ld ndf0", "ndf", T.ndf[:], ind("iot", 392, "ld"), T.yy[:], sub)
     jump("m1", "m0", "lj1", "ma")
     ts("sc k1", "lj2", T.lj2[:], s, cor(1), add, -1.0, mul)
     s = conv("rc", T.rc[:], "sc2")
     jump("mb", "m1", "lj1", "m0")
     ts("sc2 k1", "lj3", T.lj3[:], s, cor(1), add, -1.0, mul)
-    ac("iob ldw", "dw2", T.dw[:, C + 1:3 * C:2], ind("iob", 1416, "ldw"), 1.0, -LAM - 1.0)
+    ac("tb0 tb1 lca", "dv", T.dv[:, C + 1:3 * C:2], ind("tb", 896, "lca"))
 
     def unpack(t):
         for b in range(4):
@@ -370,51 +374,49 @@ def rank_program(g, core, T, topo):
             parity(t)
             jump("m1", "m0", "lj1", "ma")
             jump("mb", "m1", "lj1", "m0")
-        ac("nd", "bt", T.bt[:, C:3 * C:2], T.nd[:], -1.0)
+        ac("nb2", "bt", T.bt[:, C:3 * C:2], T.nb2[:], -1.0)
         jump("m0", "mb", "lj2", "m1")
-        if t == 0:
-            quant("et", "qe", T.qe[:], T.se[:], T.et[:])
         jump("m1", "m0", "lj3", "mb")
         for b in range(4):
             if t:
                 ac("xpo%d xpr%d" % (b, b), "xq%d" % b, T.xq[:, P * b + 16:P * b + P], T.xp[:, C * b:C * b + C], 0.0078125)
             else:
                 ac("x0", "xq%d" % b, T.xq[:, P * b + 16:P * b + P], T.x0[:, b:4 * C:4])
-        unpack(t)
         tt("m1 lhinv qq", "m0", T.m0[:], ind("m1", C, "lhinv"), T.qq[:], mul)
-        if t == 0:
-            tt("iot ld ndf0", "ndf", T.ndf[:], ind("iot", 392, "ld"), T.yy[:], sub)
         s = conv("m0", T.m0[:], "sc", "cv2")
         tt("sc i1c", "l1g", sm("l1g"), s, sm("i1c"), mx)
         ts("sc k5", "l2a", sm("l2a"), s, -1.0, mul, cor(5), add)
         ts("l1g k4", "l1", T.l1[:], sm("l1g"), cor(4), add, 1.0 / 2048, mul)
         tt("l1g l2a", "l2g", sm("l2g"), sm("l2a"), sm("l1g"), mx)
-        cp("d1 l1", "bt", ind("bt", W, "l1"), T.d1[:])
+        tt("dv l1 ndf", "m1", T.m1[:], ind("dv", W, "l1"), T.ndf[:], add)
         ts("l2g k4", "l2", T.l2[:], sm("l2g"), cor(4), add, 1.0 / 2048, mul)
-        tt("bt lsib ca", "aw", T.aw[:, C + 1:3 * C:2], ind("bt", W, "lsib"), T.ca[:], add)
+        cp("m1 l1", "bt", ind("bt", W, "l1"), T.m1[:])
         tt("dw0 dw1 dw2 l2 ndf", "nr", T.nr[:], ind("dw", W, "l2"), T.ndf[:], sub)
-        tt("aw l1 nd", "yy ndf0", T.yy[:], ind("aw", W, "l1"), T.nd[:], mx)
-        scan("bt yy", "base0", T.base[:, C + 2:3 * C + 2:2], T.bt[:, C:3 * C:2], T.yy[:], 0.0, add, add)
-        tt("base0 base_ nr", "m1", T.m1[:], T.base[:, C:3 * C:2], T.nr[:], sub)
-        scan("base0 oddx oddx_ ones", "base1", T.base[:, 0:C], T.ones[:], T.oddx[:, 0:C], T.base[:, 3 * C:3 * C + 1], add, sub)
-        cp("m1 l1", "b2", ind("b2", W, "l1"), T.m1[:])
-        tt("b2 lnm sgn", "base2", T.base[:, C + 1:3 * C:2], ind("b2", W, "lnm"), T.sgn[:], mul)
-        tt("base0 base1 base2 base_ l2 nr", "m0", T.m0[:], ind("base", W, "l2"), T.nr[:], sub)
+        ac("bt lnm", "ma", T.ma[:], ind("bt", W, "lnm"))
+        ac("nr", "mb", T.mb[:], T.nr[:], 1.0, -LAM / 2, act.Abs)
+        tt("bt lsib ca", "aw", T.aw[:, C + 1:3 * C:2], ind("bt", W, "lsib"), T.ca[:], add)
+        s = conv("ma", T.ma[:])
+        tt("aw l1 nb2", "yy ndf0", T.yy[:], ind("aw", W, "l1"), T.nb2[:], mx)
+        ts("sc k0", "wi", T.wi[:], s, cor(0), add, -2048.0, mul)
+        scan("bt yy", "rd", T.rd[:, 1:C + 1], T.bt[:, C:3 * C:2], T.yy[:], 0.0, add, add)
+        ts("wi", "oi", T.oi[:], T.wi[:], 2047, op_.bitwise_and)
+        ac("rd rd_", "base0", T.base[:, C:3 * C:2], T.rd[:, 0:C])
+        unpack(t)
+        cp("oi", "lb", T.lb[:], T.oi[:])
+        scan("rd oddx oddx_ ones", "base1", T.base[:, 0:C], T.ones[:, 0:C], T.oddx[:, 0:C], T.rd[:, C:C + 1], add, sub)
+        tt("rd rd_ lb ma", "base2", T.base[:, C + 1:3 * C:2], ind("rd", C + 1, "lb"), T.ma[:], add)
+        tt("base0 base1 base2 l2 mb", "m0", T.m0[:], ind("base", W, "l2"), T.mb[:], add)
         s = conv("m0", T.m0[:])
-        ts("sc k2", "g1", sm("g1"), s, -1.0, mul, cor(2), add)
-        tt("sc g1", "g2", sm("g2"), s, sm("g1"), mx)
-        ts("g2 k3", "lpos", T.lpos[:], sm("g2"), cor(3), add, MAGIC, sub)
+        ts("sc k3", "lpos", T.lpos[:], s, cor(3), add, MAGIC, sub)
         cp("nr lpos", "orow", T.orow[:, 8:8 + C].indirect(T.lpos[:]), T.nr[:])
         s = conv("orow", T.orow[:, 8:8 + C])
         s2 = conv("orow orow_", T.orow[:, 7:7 + C], "sc2")
-        ts("sc k0", "wi", T.wi[:], s, cor(0), add, 2048.0, mul)
         ts("sc k6", "f1", sm("f1"), s, -1.0, mul, cor(6), add)
-        ts("wi", "oi", T.oi[:], T.wi[:], 2047, op_.bitwise_and)
+        ts("sc k0", "wi", T.wi[:], s, cor(0), add, 2048.0, mul)
         tt("sc2 f1", "f2", sm("f2"), s2, sm("f1"), mx)
-        ts("oi", "lsto%d" % t, lst[:, 0:24], T.oi[:], 16.0, add)
+        ts("wi", "oi", T.oi[:], T.wi[:], 2047, op_.bitwise_and)
         ts("f2 k7", "f3", sm("f3"), sm("f2"), cor(7), add, 1024.0, mul)
-        if t == 0:
-            fill("go_", T.go[:, A:4 * 208:208], 0.0)
+        ts("oi", "lsto%d" % t, lst[:, 0:24], T.oi[:], 16.0, add)
         tt("f3 oi", "f4", sm("f4"), sm("f3"), T.oi[:], mn)
         ts("f4", "lstf%d" % t, lst[:, 24:48], sm("f4"), 16.0, add)
         send(t, "lists")
@@ -422,10 +424,11 @@ def rank_program(g, core, T, topo):
         qn, sn = T["qx%d" % (t + 1)], T["sx%d" % (t + 1)]
 
         def gath(b, own):
+            call = ac if b else cp
             if own:
-                ac("xq%d xq_%d lstf%d" % (b, b, t), "go%d" % b, T.go[:, 208 * b:208 * b + A], T.xq[:, P * b:P * b + P].indirect(lst[:, 36:48]))
+                call("xq%d xq_%d lstf%d" % (b, b, t), "go%d" % b, T.go[:, 208 * b:208 * b + A], T.xq[:, P * b:P * b + P].indirect(lst[:, 36:48]))
             else:
-                ac("yp%d yp_%d al%d" % (b, b, t), "gr%d" % b, T.gr[:, 208 * b:208 * b + 208], T.yp[:, P * b:P * b + P].indirect(ll[:, 24:37]))
+                call("yp%d yp_%d al%d" % (b, b, t), "gr%d" % b, T.gr[:, 208 * b:208 * b + 208], T.yp[:, P * b:P * b + P].indirect(ll[:, 24:37]))
 
         def diff(b, own):
             if own:
@@ -464,7 +467,7 @@ def rank_program(g, core, T, topo):
             key = "qx%s3" % h
             mm("qv " + key, "pd%d" % bank, T.pd[:, 512 * bank:512 * bank + A], T.qv[:], T.sv[:], qn[:, c0:c0 + A], sn[:, c0:c0 + A])
             dmas("s", "out", key, "", [(T.oc[:, 4 * c0:4 * (c0 + A)], qn[:, c0:c0 + A].bitcast(dt.uint8))]
-                 + [(T.osc[4 * k:4 * k + 4, c0:c0 + A], sn[32 * k:32 * k + 4, c0:c0 + A]) for k in range(4)])
+                 + ([] if own else [(T.osc[4 * k:4 * k + 4, :], sn[32 * k:32 * k + 4, :]) for k in range(4)]))
 
         def result(own):
             h, c0, bank = ("o", A, 0) if own else ("r", 0, 1)
@@ -485,13 +488,12 @@ def rank_program(g, core, T, topo):
             quant("vt", "qv", T.qv[:], T.sv[:], T.vt[:])
         for b in range(4):
             state(b, True)
-        tile(0, True)
-        tile(1, True)
+        for b in range(3):
+            tile(b, True)
         for b in range(4):
             gath(b, False)
         for b in range(4):
             diff(b, False)
-        tile(2, True)
         big(0, False)
         tile(3, True)
         for b in range(1, 4):
@@ -507,9 +509,10 @@ def rank_program(g, core, T, topo):
             tile(b, False)
         if t < NR - 1:
             signs(True)
+        else:
+            result(True)
         pack(False)
         if t == NR - 1:
-            result(True)
             outputs(False)
             result(False)
         else:
@@ -517,6 +520,6 @@ def rank_program(g, core, T, topo):
             send(t + 1, "codes")
             signs(False)
 
-    for sem in count:
+    for sem in [k for k in count if k != "out"] + ["out"]:
         if max(known[e].get(sem, 0) for e in eng) < count[sem]:
             need("g", (sem, count[sem], {}))

@@ -2,14 +2,14 @@ from concourse.mybir import dt, AluOpType, ActivationFunctionType
 
 C, A, NR = 384, 192, 3
 STEP = [1, 2, 4]
-W = 1152
+CW = C + 16
+S0 = 1544
+W = S0 + 776
 B = 2560.0
-LAM = 1024.0
-BIG = 4194304.0
-MAGIC = 12582912.0
+BIG = 8388608.0
 P = C + 16
 
-F, H, I, U, Q, S = "float32", "bfloat16", "int32", "uint16", "float8_e4m3fn_x4", "uint8"
+F, H, G, I, U, Q, S = "float32", "bfloat16", "float16", "int32", "uint16", "float8_e4m3fn_x4", "uint8"
 SCRATCH = {}
 
 
@@ -18,17 +18,18 @@ def _sb(dtype, **kw):
         SCRATCH[k] = ("sbuf", [128, kw[k]], dtype)
 
 
-_sb(H, x0=4 * C, xt=4 * C, xp=4 * C, xq=4 * P, yp=4 * P, zt=4 * C, z128=4 * C, ut=512, vt=512, et=2048, junk=4800,
-    sg=C, pp=C + 16, pb=C, eb=C, dy=C, qq=C, oddx=C + 16, neg2=C, ones=512, go=4 * 208, gr=4 * 208)
+_sb(H, x0=4 * C, xt=4 * C, xp=4 * C, xq=4 * P, yp=4 * P, zt=4 * C, z128=4 * C, ut=512, vt=512, et=2048,
+    sg=C, pp=C + 16, pb=C, eb=C, oddx=C + 16, neg2=C, ones=512, go=4 * 208, gr=4 * 208, yb=C, cvb=C, scb=C, xg=CW,
+    iotb=CW, nl=CW, nh=CW, tk=CW, ti=CW, szr=CW + 16, szp=CW, keep1=CW, keepb=CW, inc=CW, kp=C)
+_sb(G, kc=CW, nv=CW, hh=CW, uu=CW, tr=2 * C, seg=C)
 _sb(Q, qu=128, qur=128, qv=128, qe=512, qw=512, qz=C, qx0=C, qx1=C, qx2=C, qx3=C, ql0=C, ql1=C, ql2=C)
 _sb(S, su=128, sur=128, sv=128, se=512, sw=512, szz=C, sx0=C, sx1=C, sx2=C, sx3=C, sl0=C, sl1=C, sl2=C)
-_sb(I, tz=24, tp=24, i1=24, i2=24, i3=16, wi=24, oi=24, oj=24)
-_sb(U, lend=24, lpr=24, loff=24, lpost=24, lcl=24, lhinv=24, lh=24, luph=24, lj1=24, lj2=24, lj3=24, ld=24, ldw=24,
-    lca=24, lb=24, lsib=24, lnm=24, lp16=24, llt=24, lu=8, l1=24, l2=24, lpos=24,
+_sb(I, tz=32, tp=24, i1=24, i2=24, i3=24, wi=24, oi=24)
+_sb(U, lend=24, lsz=26, lpx=26, lpr=26, ld=24, ldw=24, lca=24, lb=24, lsib=24, lnm=24, lp16=24, lu=8, l1=24, l2=24, lpos=24,
     lst0=48, lst1=48, lst2=48, ll0=48, ll1=48, ll2=48)
-_sb(F, iot=408, iob=1416, tb=896, sm=24 * 56, c16=48, cor=16, cv1=C, cv2=C, er=392, ra=C, rb=C, rc=C, rd=392, nh=392, sc=C,
-    sc2=C, prr=C, hr=C, nhd=C, cde=C, nb2=C, nd=C, ndf=C, ca=C, dw=W, dv=W, aw=W, bt=W, base=W,
-    dx=C, rp=392, m0=C, m1=C, ma=C, mb=C, nr=C, yy=C, orow=392, otr=C, yo=C)
+_sb(F, iot=776, sm=32 * 40, c16=64, c48=48, pk=48, pws=64, cor=24, cv1=C, krow=CW, pa=CW + 8, y32=CW + 8, dy=C,
+    rd=392, sc=C, sc2=C, nd1=C, vv=C, v2=C, ca=C, dw=W, aw=W, bt=W, base=W, dwg=C,
+    m0=C, ma=C, mb=C, nr=C, yy=C, orow=392, otr=C, yo=C)
 SCRATCH["pd"] = ("psum", [128, 2048], F)
 SCRATCH["pq"] = ("psum", [128, 2048], F)
 
@@ -114,14 +115,12 @@ def rank_program(g, core, T, topo):
     def fill(w, out, c):
         run("v", "", w, lambda: V.memset(out, c))
 
-    def ac(r, w, out, a, scale=1.0, bias=0.0, func=None):
-        f = func
-        if f is None:
-            f = act.Copy if bias == 0.0 else act.Identity
-        if f == act.Copy:
-            run("a", r, w, lambda: g.scalar.activation(out, a, f, scale=scale))
+    def ac(r, w, out, a, scale=1.0, bias=None, func=None):
+        if func is None and bias is None:
+            run("a", r, w, lambda: g.scalar.activation(out, a, act.Copy, scale=scale))
         else:
-            run("a", r, w, lambda: g.scalar.activation(out, a, f, bias=bias, scale=scale))
+            f = act.Identity if func is None else func
+            run("a", r, w, lambda: g.scalar.activation(out, a, f, bias=0.0 if bias is None else bias, scale=scale))
 
     def iota(w, out, pat, base, cm, small):
         if small:
@@ -137,104 +136,117 @@ def rank_program(g, core, T, topo):
 
     slot = {}
 
-    def sm(name):
+    def sm(name, a=0, b=24, step=1):
         if name not in slot:
             slot[name] = len(slot)
-        return T.sm[:, 24 * slot[name]:24 * slot[name] + 24]
+        return T.sm[:, 32 * slot[name] + a:32 * slot[name] + b:step]
 
     def cor(j):
         return T.cor[:, j:j + 1]
 
-    def ind(buf, n, lst):
-        return T[buf][:, 0:n].indirect(T[lst][:, 0:24])
-
-    def conv(r, src, dst="sc", const="cv1"):
-        scan(r + " " + const, dst, T[dst][:, 0:C], src, T[const][:, 0:C], 2.0 * B * (1.0 if const == "cv1" else 4096.0), op_.min, op_.add)
-        return T[dst][:, 15:C:16]
+    def ind(buf, n, lst, k=24):
+        return T[buf][:, 0:n].indirect(T[lst][:, 0:k])
 
     add, sub, mul, mx, mn = op_.add, op_.subtract, op_.mult, op_.max, op_.min
 
-    dmas("a", "ltree", "", "tz tp", [(T.tz[:], T.sz[:]), (T.tp[:], T.pr[:])])
+    def conv(r, src, dst="sc", init=2.0 * B):
+        scan(r + " cv1", dst, T[dst][:, 0:C], src, T.cv1[:, 0:C], init, mn, add)
+        return T[dst][:, 15:C:16]
+
+    def classes(r, src, o):
+        run("v", r, "tr0", lambda: V.transpose(T.tr[:, 0:C], src[:, 0:C]))
+        run("v", r, "tr1", lambda: V.transpose(T.tr[:, C:2 * C], src[:, 16:CW]))
+        scan("kp tr0 tr1", "seg", T.seg[:], T.kp[:], T.tr[:, 0:2 * C:2], 0.0, mul, o)
+        scan("seg c48a c48b", "pk", T.pk[:], T.seg[:, 7:C:8], T.c48[:], -4096.0, mx, add)
+        return T.pk[:, 1:24:2], T.pk[:, 25:48:2]
+
+    dmas("a", "ltree", "", "tz tp", [(T.tz[:, 4:28], T.sz[:]), (T.tp[:], T.pr[:])])
     dmas("s", "lx", "", "x0", [(T.x0[:], T.x[:])])
     dmas("a", "lu_", "", "ut", [(T.ut[:], T.u[:])])
     dmas("s", "lw", "x0", "qw", [(T.qw[:].bitcast(dt.uint8), T.wc[:]), (T.sw[:], T.ws[:])])
     dmas("s", "lv", "", "vt", [(T.vt[:], T.v[:])])
 
     iota("i1", T.i1[:], [[0, 24]], 0, 1, False)
+    iota("i3", T.i3[:, 0:16], [[1, 16]], 128, -1, False)
+    iota("pw", T.pws[:, 48:64], [[0, 8], [-1, 2]], 2, 0, True)
     iota("i2", T.i2[:], [[16, 24]], 0, 0, False)
-    iota("i3", T.i3[:], [[1, 16]], 128, -1, False)
-    iota("iot", T.iot[:], [[1, 408]], 0, 0, True)
+    iota("iot", T.iot[:, 0:CW], [[1, CW]], 0, 0, True)
     fill("ones", T.ones[:], 1.0)
+    run("g", "ones", "kp", lambda: g.affine_select(T.kp[:], T.ones[:, 0:C], [[0, 48], [1, 8]], op_.is_gt, 0.0, 0, 0))
+    iota("iot2", T.iot[:, CW:776], [[1, 776 - CW]], CW, 0, True)
     for b in range(4):
         run("g", "ones", "et%d" % b, lambda: g.affine_select(T.et[:, 512 * b:512 * b + 512], T.ones[:], [[1, 512]], op_.is_equal, 0.0, -b, -4))
-    iota("iob", T.iob[:], [[1, 1416]], 0, 0, True)
-    iota("tb0", T.tb[:, 0:512], [[-1, 512]], 0, 0, True)
-    iota("tb1", T.tb[:, 512:896], [[0, C]], int(BIG) + 1, 0, True)
-    iota("dv", T.dv[:], [[0, W]], int(BIG) + 1, 0, True)
-    iota("bt", T.bt[:], [[0, W]], 0, 0, True)
+    iota("bt", T.bt[:, S0:W], [[0, W - S0]], 0, 0, True)
 
-    fill("er_", T.er[:, C:392], float(C))
+    HI, LO, THR, TH2, THL, RT, K0, KZ, KR, KP_, K6, K7, H16, Z0 = range(14)
+    fill("tz_", T.tz[:, 0:4], 0)
+    fill("tze", T.tz[:, 28:32], 0)
+    fill("prc_", sm("prc", 0, 32), 0.0)
     fill("neg2", T.neg2[:], -2.0)
-    ts("i1", "i1", T.i1[:], T.i1[:], 15, op_.bitwise_and)
-    ts("i3", "i3", T.i3[:], T.i3[:], 15, op_.bitwise_and)
+    ts("i1", "ih", T.i3[:, 16:17], T.i1[:, 0:1], 4, op_.arith_shift_right, 1, op_.bitwise_and)
+    ts("i3", "i3", T.i3[:, 0:16], T.i3[:, 0:16], 15, op_.bitwise_and)
+    scan("pw", "pw2", T.pws[:, 0:16], T.pws[:, 48:64], T.pws[:, 48:64], 1.0, mul, mx)
+    ts("i1 ih", "i1", T.i1[:], T.i1[:], 15, op_.bitwise_and)
+    ts("i3", "c16m", T.c16[:, 48:64], T.i3[:, 0:16], 0.0, op_.is_equal)
+    cp("ih", "hi", cor(HI), T.i3[:, 16:17])
+    tt("c16m pw2", "pw3", T.pws[:, 16:32], T.c16[:, 48:64], T.pws[:, 0:16], mul)
     tt("i1 i2", "n", sm("n"), T.i1[:], T.i2[:], add)
+    scan("pw3", "thr", T.pws[:, 32:48], T.pws[:, 16:32], T.pws[:, 16:32], 0.0, add, mx)
+    thr = T.pws[:, 47:48]
+    ts("hi", "lo", cor(LO), cor(HI), -1.0, mul, 1.0, add)
+    ts("thr", "th2", cor(TH2), thr, 2.0, mul)
+    ts("thr", "thl0", cor(THR), thr, 2.0, op_.is_equal)
+    ac("iot", "iotb", T.iotb[:], T.iot[:, 0:CW])
+    ts("hi", "kr", cor(KR), cor(HI), -32.0, mul, 777.0, add)
+    tt("thr thl0", "thl", cor(THL), thr, cor(THR), sub)
+    ac("iot kr", "krow", T.krow[:], T.iot[:, 0:CW], 2.0, cor(KR))
+    ts("hi", "rt", cor(RT), cor(HI), -16.0, mul, float(CW + 1), add)
+    ts("hi", "h16", cor(H16), cor(HI), 16.0, mul)
+    ts("iotb thl", "nl", T.nl[:], T.iotb[:], cor(THL), op_.is_ge, 1.0, add)
+    ts("iotb th2", "nh", T.nh[:], T.iotb[:], cor(TH2), op_.is_lt, -2.0, add)
+    ac("nl", "tk", T.tk[:], T.nl[:], 4096.0, -3324.0)
+    ts("n rt", "root", sm("root"), sm("n"), 0.0, op_.is_equal, cor(RT), mul)
+    scan("nl nh", "ti", T.ti[:], T.nl[:], T.nh[:], 0.0, mx, add)
     cp("i1", "lp16", T.lp16[:], T.i1[:])
-    ts("i3", "c16a", T.c16[:, 16:32], T.i3[:], 0.0, op_.is_equal, -B, mul)
-    ts("i3", "c16b", T.c16[:, 32:48], T.i3[:], 15.0, op_.is_equal, 2.0 * B, mul)
-    ts("i1", "kb", cor(8), T.i1[:, 0:1], 0.0, op_.is_equal, -2.0 * B, mul)
-    ts("n", "nb", sm("nb"), sm("n"), -1.0, mul, -0.5, add)
-    tt("c16a c16b", "c16", T.c16[:, 0:16], T.c16[:, 16:32], T.c16[:, 32:48], add)
-    ts("n", "root", sm("root"), sm("n"), 0.0, op_.is_equal, float(C + 1), mul)
-    ac("iot", "ndf0", T.yy[:], T.iot[:, 0:C], 1.0 / 2048)
-    ac("c16 lp16", "cv1", T.cv1[:], ind("c16", 16, "lp16"))
-    for j, m, c in [(0, 1.0, B), (1, 1.0, B - 511.0), (3, 1.0, B + MAGIC - LAM / 2), (4, 4096.0, 4096.0 * B),
-                    (5, -8192.0, -8192.0 * B), (6, -2.0, 1.0 - 2.0 * B), (7, 1.0, B - 1.125)]:
-        ts("kb", "k%d" % j, cor(j), cor(8), m, mul, c, add)
-    cp("i2", "lu", T.lu[:], T.i2[:, 0:8])
-    ts("n", "t5", sm("t5"), sm("n"), 2.0, mul, -16.0, add)
-    fill("pp_", T.pp[:, 0:1], 32.0)
-    tt("t5 i2", "st2", sm("st2"), sm("t5"), T.i2[:], sub)
-    tt("tz n", "end", sm("end"), T.tz[:], sm("n"), add)
-    tt("tp root", "prc", sm("prc"), T.tp[:], sm("root"), add)
+    ts("c16m", "c16a", T.c16[:, 16:32], T.c16[:, 48:64], -B, mul)
+    ts("i3", "c16b", T.c16[:, 32:48], T.i3[:, 0:16], 15.0, op_.is_equal, 2.0 * B, mul)
+
+    ts("tz tze lo", "za", sm("za", 0, 26), T.tz[:, 4:30], cor(LO), mul)
+    ts("tz tz_ tze hi", "zb", sm("zb", 0, 26), T.tz[:, 3:29], cor(HI), mul)
+    tt("tp root prc_", "prc", sm("prc", 4, 28), T.tp[:], sm("root"), add)
+    tt("za zb", "zc", sm("zc", 0, 26), sm("za", 0, 26), sm("zb", 0, 26), add)
+    ts("prc lo", "pa_", sm("pa_", 0, 26), sm("prc", 4, 30), cor(LO), mul)
+    cp("zc", "lsz", T.lsz[:], sm("zc", 0, 26))
+    ts("prc hi", "pb_", sm("pb_", 0, 26), sm("prc", 3, 29), cor(HI), mul)
+    ac("iot lsz", "szr", T.szr[:, 0:CW], ind("iot", CW, "lsz", 25))
+    fill("szr_", T.szr[:, CW:CW + 16], 1024.0)
+    tt("pa_ pb_", "pc", sm("pc", 0, 26), sm("pa_", 0, 26), sm("pb_", 0, 26), add)
+    tt("tz n", "end", sm("end"), T.tz[:, 4:28], sm("n"), add)
+    ts("pc h16", "lpr", T.lpr[:], sm("pc", 0, 26), cor(H16), add)
+    cp("ti lsz", "inc", T.inc[:], ind("ti", CW, "lsz", 25))
+    ac("szr szr_ lpr", "szp", T.szp[:], ind("szr", CW + 16, "lpr", 25))
+    cp("pc", "lpx", T.lpx[:], sm("pc", 0, 26))
     cp("end", "lend", T.lend[:], sm("end"))
-    cp("prc", "lpr", T.lpr[:], sm("prc"))
-    cp("iot lend", "er", T.er[:, 0:C], ind("iot", 392, "lend"))
-
-    at = 0
-    for c in range(23, -1, -1):
-        n = 16 * (c + 1)
-        run("a", "er nb", "dc%d" % c, lambda: g.scalar.activation(
-            T.junk[:, at:at + n], T.er[:, 0:n], act.Sign, bias=sm("nb")[:, c:c + 1], scale=1.0, accum_out=sm("dc")[:, c:c + 1]))
-        at += n
-
+    tt("c16a c16b", "c16", T.c16[:, 0:16], T.c16[:, 16:32], T.c16[:, 32:48], add)
+    ts("i1", "z0", cor(Z0), T.i1[:, 0:1], 0.0, op_.is_equal)
+    ac("c16 lp16", "cv1", T.cv1[:], ind("c16", 16, "lp16"))
+    ac("cv1", "cvb", T.cvb[:], T.cv1[:], 4.0 / B)
+    cp("i2", "lu", T.lu[:], T.i2[:, 0:8])
+    fill("pa0", T.pa[:, CW:CW + 8], 0.0)
+    ts("ones hi", "c48x", sm("c48x"), T.ones[:, 0:24], cor(HI), mul)
     ts("tp", "pr1", sm("pr1"), T.tp[:], 1.0, add)
-    cp("er er_ lpr", "ra", T.ra[:], ind("er", 392, "lpr"))
-    tt("n pr1", "b", sm("b"), sm("n"), sm("pr1"), sub)
-    s = conv("ra", T.ra[:])
-    tt("b tz", "l2_", sm("l2_"), sm("b"), T.tz[:], op_.is_ge)
-    ts("sc k0", "ep", sm("ep"), s, cor(0), add)
-    ts("pr1", "lnm", T.lnm[:], sm("pr1"), 2.0, mul, float(C + 1), add)
-    tt("ep end", "a", sm("a"), sm("ep"), sm("end"), sub)
-    ts("b", "iss", sm("iss"), sm("b"), 0.0, op_.is_gt)
-    tt("a tz", "l1_", sm("l1_"), sm("a"), T.tz[:], op_.is_gt)
-    tt("a b", "szs", sm("szs"), sm("a"), sm("b"), add)
-    tt("l1_ l2_", "light", sm("light"), sm("l1_"), sm("l2_"), add)
-    ts("a", "isf", sm("isf"), sm("a"), 0.0, op_.is_gt)
-    tt("light szs", "off", sm("off"), sm("light"), sm("szs"), mul)
-    cp("light", "llt", T.llt[:], sm("light"))
-    ts("off", "loff", T.loff[:], sm("off"), 1.0, add)
-    ac("iot loff", "rb", T.rb[:], ind("iot", 392, "loff"))
-    tt("end isf", "t1", sm("t1"), sm("end"), sm("isf"), mul)
-    ts("isf", "t6", sm("t6"), sm("isf"), LAM, mul, 1.0, add)
-    ts("t1", "lsib", T.lsib[:], sm("t1"), 2.0, mul, float(C + 1), add)
-    tt("t6 iss", "t3", sm("t3"), sm("t6"), sm("iss"), sub)
-    ts("isf", "t4", sm("t4"), sm("isf"), -512.0, mul, 512.0, add)
+    ts("c48x", "c48a", T.c48[:, 0:48:2], sm("c48x"), -4096.0, mul, 2048.0, add)
+    ts("c48x", "c48b", T.c48[:, 1:48:2], sm("c48x"), 2048.0, mul, -2816.0, add)
+    ts("szp th2", "keep1", T.keep1[:], T.szp[:], cor(TH2), op_.is_lt)
+    ts("szp thr", "keepb", T.keepb[:], T.szp[:], thr, op_.is_lt, -2048.0, mul)
 
-    quant("x0", "qxo0 qxr0", T.qx0[:], T.sx0[:], T.x0[:])
+    scan("keep1 inc", "pa", T.pa[:, 0:CW], T.keep1[:], T.inc[:], 0.0, mul, sub)
     quant("ut", "qu", T.qu[:], T.su[:], T.ut[:])
-    fill("rd_", T.rd[:, 0:1], 512.0)
+    tt("pa pa0 lpr keepb", "hh", T.hh[:], ind("pa", CW + 8, "lpr", 25), T.keepb[:], add)
     cp("qu lu", "qur", T.qur[:].bitcast(dt.uint32), T.qu[:].bitcast(dt.uint32).indirect(T.lu[:]))
-    cp("qu lu", "sur", T.sur[:], T.su[:].indirect(T.lu[:]))
+    run("a", "qu lu", "sur", lambda: g.scalar.activation(T.sur[:], T.su[:].indirect(T.lu[:]), act.Copy))
+    scan("hh inc", "uu", T.uu[:], T.hh[:], T.inc[:], 0.0, mx, sub)
+    quant("x0", "qxo0 qxr0", T.qx0[:], T.sx0[:], T.x0[:])
 
     def send(t, what):
         dst = T.cores[(rank + STEP[t]) % n_ranks]
@@ -266,98 +278,61 @@ def rank_program(g, core, T, topo):
         h, c0, bank = ("o", A, 0) if own else ("r", 0, 1)
         ts("pd%d" % bank, "sg" + h, T.sg[:, c0:c0 + A], T.pd[:, 512 * bank:512 * bank + A], 0.0, op_.is_gt, 0.5, sub)
 
-    def front(t):
-        scan("sgo sgr neg2", "pp", T.pp[:, 1:C + 1], T.sg[:], T.neg2[:], 32.0, mul, mul)
-        scan("sgo sgr neg2", "pb", T.pb[:], T.sg[:], T.neg2[:], 32.0, mul, mul)
-        ac("sgo sgr", "dx", T.dx[:], T.sg[:], 2047.0, -0.5)
-        ac("sgo sgr", "dy", T.dy[:], T.sg[:], 2048.0)
-        tt("pp pp_ pb lend", "eb", T.eb[:], ind("pp", C + 1, "lend"), T.pb[:], mul)
-        tt("eb dx", "rp", T.rp[:, 0:C], T.eb[:], T.dx[:], mx)
-
-    def parity(t):
-        tt("eb dy", "qq", T.qq[:], T.eb[:], T.dy[:], add)
-        ac("qq", "oddx", T.oddx[:, 1:C + 1], T.qq[:], 1.0 / 2048, 0.0, act.Abs)
-
     score(0, True)
     score(0, False)
     send(0, "codes")
-    iota("aw", T.aw[:], [[0, W]], -2 * int(BIG), 0, True)
+    iota("aw", T.aw[:, 0:C], [[0, C]], -2048, 0, True)
+    iota("aw_", T.aw[:, S0:W], [[0, W - S0]], -2048, 0, True)
     for b in range(4):
         iota("xq_%d" % b, T.xq[:, P * b:P * b + 16], [[0, 16]], 0, 0, True)
         iota("yp_%d" % b, T.yp[:, P * b:P * b + 16], [[0, 16]], 0, 0, True)
-    tt("iot lpr ndf0", "prr", T.prr[:], ind("iot", 392, "lpr"), T.yy[:], add)
+
+    pe, po = classes("uu", T.uu, add)
+    tt("n pr1", "b", sm("b"), sm("n"), sm("pr1"), sub)
+    ts("pk", "de", sm("d", 0, 24, 2), pe, -1.0, mul, -769.0, add)
+    ts("pk", "do", sm("d", 1, 24, 2), po, -1.0, mul, -769.0, add)
+    ts("b", "s1", sm("s1"), sm("b"), 0.0, op_.is_gt, 775.0, mul)
+    cp("de do", "ld", T.ld[:], sm("d"))
+    ts("de do", "d2", sm("d2"), sm("d"), 2.0, mul)
+    ts("b", "s0", sm("s0"), sm("b"), 0.0, op_.is_equal, 771.0, mul)
+    ac("iot ld", "nd1", T.nd1[:], ind("iot", CW, "ld"), -1.0, -399.0)
+    tt("d2 s1", "t10", sm("t10"), sm("d2"), sm("s1"), mx)
+    tt("d2 s0", "t11", sm("t11"), sm("d2"), sm("s0"), mx)
+    fill("pp_", T.pp[:, 0:1], 24.0)
+    cp("t10", "lca", T.lca[:], sm("t10"))
+    cp("t11", "ldw", T.ldw[:], sm("t11"))
     signs(True)
     signs(False)
-    quant("et0 et1 et2 et3", "qe", T.qe[:], T.se[:], T.et[:])
+    tt("tk lsz krow", "kc", T.kc[:], ind("tk", CW, "lsz", 25), T.krow[:], mn)
+    fill("y32_", T.y32[:, C:CW + 8], -1152.0)
+    ac("iot", "yy", T.yy[:], T.iot[:, 0:C], -1.0 / 2048, 400.0)
 
-    dcs = " ".join("dc%d" % c for c in range(24))
-    tt(dcs + " st2", "d2", sm("d2"), sm("dc"), sm("st2"), add)
-    fill("nh_", T.nh[:, C:392], 511.0)
-    ts("d2", "d", sm("d"), sm("d2"), 0.5, mul)
-    fill("rp_", T.rp[:, C:392], 1023.0)
-    tt("end d", "t8", sm("t8"), sm("end"), sm("d"), sub)
-    tt("n d", "t9", sm("t9"), sm("n"), sm("d"), sub)
-    ts("t8", "lpost", T.lpost[:], sm("t8"), -1.0, add)
-    cp("t9", "lcl", T.lcl[:], sm("t9"))
-    cp("d", "ld", T.ld[:], sm("d"))
-    cp("rb lpost", "ra", ind("ra", C, "lpost"), T.rb[:])
-    scan("rb", "rc", T.rc[:], T.rb[:], T.rb[:], 0.0, add, mx)
-    scan("ra", "rd", T.rd[:, 1:C + 1], T.ra[:], T.ra[:], 512.0, add, mx)
-    tt("d t3", "t10", sm("t10"), sm("d"), sm("t3"), add)
-    tt("rd rd_ lcl rc", "nh", T.nh[:, 0:C], ind("rd", C + 1, "lcl"), T.rc[:], sub)
-    tt("d t4", "t11", sm("t11"), sm("d"), sm("t4"), add)
-    s = conv("nh", T.nh[:, 0:C])
-    cp("t10", "ldw", T.ldw[:], sm("t10"))
-    ts("sc k1", "lhinv", T.lhinv[:], s, cor(1), add, -1.0, mul)
-    cp("t11", "lca", T.lca[:], sm("t11"))
-    cp("prr lhinv", "hr", ind("hr", C, "lhinv"), T.prr[:])
-    ts("n k4", "i1c", sm("i1c"), sm("n"), 2048.0, mul, cor(4), sub)
-    s = conv("hr", T.hr[:])
-    fill("rd_", T.rd[:, 0:1], 0.0)
-    ts("sc k0", "wi", T.wi[:], s, cor(0), add, 2048.0, mul)
-    fill("oddx_", T.oddx[:, 0:1], 1.0)
-    ts("wi", "oj", T.oj[:], T.wi[:], 11, op_.arith_shift_right)
-    ts("wi", "oi", T.oi[:], T.wi[:], 2047, op_.bitwise_and)
-    cp("oj", "luph", T.luph[:], T.oj[:])
-    cp("oi", "lh", T.lh[:], T.oi[:])
-    ac("iot llt", "m0", T.m0[:], ind("iot", 392, "llt"), -1.0, 1.0)
-    ac("cv1", "cv2", T.cv2[:], T.cv1[:], 4096.0)
-    ac("iot ld", "nd", T.nd[:], ind("iot", 392, "ld"), -1.0)
-    ac("nd", "nb2", T.nb2[:], T.nd[:], 1.0, -BIG)
-    ac("nd", "dw0", T.dw[:, 0:C], T.nd[:], -1.0)
-    ac("nd", "dw1", T.dw[:, C:3 * C:2], T.nd[:], -1.0)
-    ac("iob ldw", "dw2", T.dw[:, C + 1:3 * C:2], ind("iob", 1416, "ldw"), 1.0, -1.0)
-    ac("iob lca", "ca", T.ca[:], ind("iob", 1416, "lca"), -2.0, 1.0 - 2.0 * BIG)
+    def front(t):
+        scan("sgo sgr neg2", "pp", T.pp[:, 1:C + 1], T.sg[:], T.neg2[:], 24.0, mul, mul)
+        ac("sgo sgr", "dy", T.dy[:], T.sg[:], 767.0, -1151.5)
+        scan("sgo sgr neg2", "pb", T.pb[:], T.sg[:], T.neg2[:], 16.0, mul, mul)
+        tt("pp pp_ pb lend", "eb", T.eb[:], ind("pp", C + 1, "lend"), T.pb[:], mul)
+        scan("eb dy", "y32", T.y32[:, 0:C], T.eb[:], T.dy[:], -4096.0, mx, add)
+        ac("y32 y32_ lpx", "xg", T.xg[:], ind("y32", CW + 8, "lpx", 25), -1.0, -1151.0, act.Relu)
+        ac("y32", "yb", T.yb[:], T.y32[:, 0:C], 1.0 / 767.5, 1151.5 / 767.5)
+        ac("yb", "oddx", T.oddx[:, 1:C + 1], T.yb[:], 1.0, 0.0, act.Abs)
+
     front(0)
-    ac("nh nh_ luph", "rb", T.rb[:], ind("nh", 392, "luph"))
-    ac("m0 lh", "nhd", T.nhd[:], ind("m0", C, "lh"))
-    ac("iot lh", "cde", T.cde[:], ind("iot", 392, "lh"), 2.0, float(C + 1 - 1024))
-    parity(0)
-    scan("nhd rb", "ra", T.ra[:], T.nhd[:], T.rb[:], 0.0, mul, mx)
-
-    def top(t):
-        tt("rp rp_ luph cde", "m1", T.m1[:], ind("rp", 392, "luph"), T.cde[:], add)
-        scan("nhd m1", "m0", T.m0[:], T.nhd[:], T.m1[:], 0.0, mul, mx)
-        ac("m0", "ma", T.ma[:], T.m0[:])
-
-    def jump(out, win, lst, other):
-        tt("%s %s %s" % (win, lst, other), out, T[out][:], ind(win, C, lst), T[other][:], mx)
-
-    fill("orow_", T.orow[:, 7:8], 0.0)
-    s = conv("ra", T.ra[:])
+    for j, m, c in [(K0, -2.0 * B, B), (KZ, 8.0, -4.0), (KP_, -2.0 * B, B - BIG - 1.0), (K6, 4.0 * B, -799.0 - 2.0 * B),
+                    (K7, -2.0 * B, B + 400.0 - 1.125)]:
+        ts("z0", "k%d" % j, cor(j), cor(Z0), m, mul, c, add)
+    ts("pr1", "lnm", T.lnm[:], sm("pr1"), 2.0, mul, float(S0 + 1), add)
+    ts("end", "lsib", T.lsib[:], sm("end"), 2.0, mul, float(S0 + 1), add)
+    fill("rd_", T.rd[:, 0:1], BIG)
+    fill("oddx_", T.oddx[:, 0:1], 1.0)
+    fill("orow_", T.orow[:, 7:8], -400.0)
     fill("go_", T.go[:, A:4 * 208:208], 0.0)
-    ts("sc k1", "lj1", T.lj1[:], s, cor(1), add, -1.0, mul)
-    ac("ra lj1", "rb", T.rb[:], ind("ra", C, "lj1"))
-    top(0)
-    ac("rb lj1", "rc", T.rc[:], ind("rb", C, "lj1"))
-    s = conv("rb", T.rb[:])
-    tt("iot ld ndf0", "ndf", T.ndf[:], ind("iot", 392, "ld"), T.yy[:], sub)
-    jump("m1", "m0", "lj1", "ma")
-    ts("sc k1", "lj2", T.lj2[:], s, cor(1), add, -1.0, mul)
-    s = conv("rc", T.rc[:], "sc2")
-    jump("mb", "m1", "lj1", "m0")
-    ts("sc2 k1", "lj3", T.lj3[:], s, cor(1), add, -1.0, mul)
-    ac("tb0 tb1 lca", "dv", T.dv[:, C + 1:3 * C:2], ind("tb", 896, "lca"))
+
+    def statics():
+        ac("nd1", "dw0", T.dw[:, 0:C], T.nd1[:], -1.0, -399.0)
+        ac("nd1", "dw1", T.dw[:, S0:S0 + 2 * C:2], T.nd1[:], -1.0, -399.0)
+        ac("iot iot2 ldw", "dw2", T.dw[:, S0 + 1:S0 + 2 * C:2], ind("iot", 776, "ldw"), 1.0, -385.0)
+        ac("iot iot2 lca", "ca", T.ca[:], ind("iot", 776, "lca"), -1.0, -797.0)
 
     def unpack(t):
         for b in range(4):
@@ -366,56 +341,67 @@ def rank_program(g, core, T, topo):
         for b in range(4):
             ac("pd%d" % b, "yp%d" % b, T.yp[:, P * b + 16:P * b + P], T.pd[:, 512 * b:512 * b + C])
 
-    for t in range(NR):
-        lst, ll = T["lst%d" % t], T["ll%d" % t]
-        if t:
-            front(t)
-            top(t)
-            parity(t)
-            jump("m1", "m0", "lj1", "ma")
-            jump("mb", "m1", "lj1", "m0")
-        ac("nb2", "bt", T.bt[:, C:3 * C:2], T.nb2[:], -1.0)
-        jump("m0", "mb", "lj2", "m1")
-        jump("m1", "m0", "lj3", "mb")
-        for b in range(4):
+    def planes(t, bs):
+        for b in bs:
             if t:
                 ac("xpo%d xpr%d" % (b, b), "xq%d" % b, T.xq[:, P * b + 16:P * b + P], T.xp[:, C * b:C * b + C], 0.0078125)
             else:
                 ac("x0", "xq%d" % b, T.xq[:, P * b + 16:P * b + P], T.x0[:, b:4 * C:4])
-        tt("m1 lhinv qq", "m0", T.m0[:], ind("m1", C, "lhinv"), T.qq[:], mul)
-        s = conv("m0", T.m0[:], "sc", "cv2")
-        tt("sc i1c", "l1g", sm("l1g"), s, sm("i1c"), mx)
-        ts("sc k5", "l2a", sm("l2a"), s, -1.0, mul, cor(5), add)
-        ts("l1g k4", "l1", T.l1[:], sm("l1g"), cor(4), add, 1.0 / 2048, mul)
-        tt("l1g l2a", "l2g", sm("l2g"), sm("l2a"), sm("l1g"), mx)
-        tt("dv l1 ndf", "m1", T.m1[:], ind("dv", W, "l1"), T.ndf[:], add)
-        ts("l2g k4", "l2", T.l2[:], sm("l2g"), cor(4), add, 1.0 / 2048, mul)
-        cp("m1 l1", "bt", ind("bt", W, "l1"), T.m1[:])
-        tt("dw0 dw1 dw2 l2 ndf", "nr", T.nr[:], ind("dw", W, "l2"), T.ndf[:], sub)
-        ac("bt lnm", "ma", T.ma[:], ind("bt", W, "lnm"))
-        ac("nr", "mb", T.mb[:], T.nr[:], 1.0, -LAM / 2, act.Abs)
-        tt("bt lsib ca", "aw", T.aw[:, C + 1:3 * C:2], ind("bt", W, "lsib"), T.ca[:], add)
+
+    for t in range(NR):
+        lst, ll = T["lst%d" % t], T["ll%d" % t]
+        if t:
+            front(t)
+        else:
+            tt("iot ld yy", "vv", T.vv[:], ind("iot", CW, "ld"), T.yy[:], add)
+        scan("xg kc", "nv", T.nv[:], T.xg[:], T.kc[:], 0.0, mx, sub)
+        ac("nd1", "bt", T.bt[:, S0:S0 + 2 * C:2], T.nd1[:], -1.0)
+        if t == 0:
+            statics()
+            ac("vv", "v2", T.v2[:], T.vv[:], 1.0, 400.0)
+        scan("keep1 nv", "pa", T.pa[:, 0:CW], T.keep1[:], T.nv[:], 0.0, mul, mn)
+        scan("yb cvb", "scb", T.scb[:], T.yb[:], T.cvb[:], 8.0, mn, add)
+        tt("pa pa0 lpr keepb", "hh", T.hh[:], ind("pa", CW + 8, "lpr", 25), T.keepb[:], add)
+        ts("scb k%d" % KZ, "zn", sm("zn"), T.scb[:, 15:C:16], -1.0, mul, cor(KZ), add)
+        scan("hh nv", "uu", T.uu[:], T.hh[:], T.nv[:], 0.0, mx, mn)
+        if t == 0:
+            quant("et0 et1 et2 et3", "qe", T.qe[:], T.se[:], T.et[:])
+        pe, po = classes("uu", T.uu, mn)
+        planes(t, range(4))
+        tt("pk zn", "we", sm("w", 0, 24, 2), pe, sm("zn", 0, 24, 2), mul)
+        tt("pk zn", "wo", sm("w", 1, 24, 2), po, sm("zn", 1, 24, 2), mul)
+        tt("we wo n", "l1f", sm("l1f"), sm("w"), sm("n"), mx)
+        ts("we wo", "wn", sm("wn"), sm("w"), -1.0, mul)
+        cp("l1f", "l1", T.l1[:], sm("l1f"))
+        tt("wn l1f", "l2f", sm("l2f"), sm("wn"), sm("l1f"), mx)
+        cp("l2f", "l2", T.l2[:], sm("l2f"))
+        cp("vv l1", "bt", ind("bt", W, "l1"), T.vv[:])
+        ac("dw0 dw1 dw2 l2", "dwg", T.dwg[:], ind("dw", W, "l2"), 1.0, 400.0)
+        tt("bt lsib ca", "aw aw_", T.aw[:, S0 + 1:S0 + 2 * C:2], ind("bt", W, "lsib"), T.ca[:], add)
+        ac("bt lnm", "ma", T.ma[:], ind("bt", W, "lnm"), 1.0, -784.0)
+        scan("dwg v2", "nr", T.nr[:], T.dwg[:], T.v2[:], 0.0, mx, sub)
+        tt("aw aw_ l1 nd1", "yy", T.yy[:], ind("aw", W, "l1"), T.nd1[:], mx)
+        ac("nr", "mb", T.mb[:], T.nr[:], 1.0, 399.0, act.Abs)
         s = conv("ma", T.ma[:])
-        tt("aw l1 nb2", "yy ndf0", T.yy[:], ind("aw", W, "l1"), T.nb2[:], mx)
-        ts("sc k0", "wi", T.wi[:], s, cor(0), add, -2048.0, mul)
-        scan("bt yy", "rd", T.rd[:, 1:C + 1], T.bt[:, C:3 * C:2], T.yy[:], 0.0, add, add)
-        ts("wi", "oi", T.oi[:], T.wi[:], 2047, op_.bitwise_and)
-        ac("rd rd_", "base0", T.base[:, C:3 * C:2], T.rd[:, 0:C])
+        scan("bt yy", "rd", T.rd[:, 1:C + 1], T.bt[:, S0:S0 + 2 * C:2], T.yy[:], BIG, add, add)
+        ts("sc k%d" % K0, "wi", T.wi[:], s, cor(K0), add, -2048.0, mul)
+        ac("rd rd_", "base0", T.base[:, S0:S0 + 2 * C:2], T.rd[:, 0:C])
         unpack(t)
-        cp("oi", "lb", T.lb[:], T.oi[:])
         scan("rd oddx oddx_ ones", "base1", T.base[:, 0:C], T.ones[:, 0:C], T.oddx[:, 0:C], T.rd[:, C:C + 1], add, sub)
-        tt("rd rd_ lb ma", "base2", T.base[:, C + 1:3 * C:2], ind("rd", C + 1, "lb"), T.ma[:], add)
+        ts("wi", "oi", T.oi[:], T.wi[:], 2047, op_.bitwise_and)
+        cp("oi", "lb", T.lb[:], T.oi[:])
+        tt("rd rd_ lb ma", "base2", T.base[:, S0 + 1:S0 + 2 * C:2], ind("rd", C + 1, "lb"), T.ma[:], add)
         tt("base0 base1 base2 l2 mb", "m0", T.m0[:], ind("base", W, "l2"), T.mb[:], add)
-        s = conv("m0", T.m0[:])
-        ts("sc k3", "lpos", T.lpos[:], s, cor(3), add, MAGIC, sub)
+        s = conv("m0", T.m0[:], "sc", BIG + 2.0 * B)
+        ts("sc k%d" % KP_, "lpos", T.lpos[:], s, cor(KP_), add)
         cp("nr lpos", "orow", T.orow[:, 8:8 + C].indirect(T.lpos[:]), T.nr[:])
         s = conv("orow", T.orow[:, 8:8 + C])
         s2 = conv("orow orow_", T.orow[:, 7:7 + C], "sc2")
-        ts("sc k6", "f1", sm("f1"), s, -1.0, mul, cor(6), add)
-        ts("sc k0", "wi", T.wi[:], s, cor(0), add, 2048.0, mul)
+        ts("sc k%d" % K6, "f1", sm("f1"), s, -1.0, mul, cor(K6), add)
+        ts("sc k%d" % K0, "wi", T.wi[:], s, cor(K0), add, 2048.0, mul)
         tt("sc2 f1", "f2", sm("f2"), s2, sm("f1"), mx)
         ts("wi", "oi", T.oi[:], T.wi[:], 2047, op_.bitwise_and)
-        ts("f2 k7", "f3", sm("f3"), sm("f2"), cor(7), add, 1024.0, mul)
+        ts("f2 k%d" % K7, "f3", sm("f3"), sm("f2"), cor(K7), add, 1024.0, mul)
         ts("oi", "lsto%d" % t, lst[:, 0:24], T.oi[:], 16.0, add)
         tt("f3 oi", "f4", sm("f4"), sm("f3"), T.oi[:], mn)
         ts("f4", "lstf%d" % t, lst[:, 24:48], sm("f4"), 16.0, add)
@@ -481,7 +467,7 @@ def rank_program(g, core, T, topo):
         for b in range(4):
             big(b, True)
         if t == NR - 1:
-            ac("iot lsto%d" % t, "otr", T.otr[:], T.iot[:, 0:408].indirect(lst[:, 0:24]), 1.0, -16.0)
+            ac("iot lsto%d" % t, "otr", T.otr[:], T.iot[:, 0:CW].indirect(lst[:, 0:24]), 1.0, -16.0)
             dmas("s", "out", "otr", "", [(T.ot[k:k + 1, :], T.otr[16 * k:16 * k + 1, :]) for k in range(8)])
         product(True)
         if t == NR - 1:

@@ -3,8 +3,11 @@ from concourse.mybir import dt, AluOpType, ActivationFunctionType
 C, A, NR = 384, 192, 3
 STEP = [1, 2, 4]
 CW = C + 16
-S0 = 1544
-W = S0 + 776
+KEY = 801
+OFF = 1159
+S0 = KEY + OFF
+S1 = S0 + 2 * C
+W = S1 + C
 B = 2560.0
 BIG = 8388608.0
 P = C + 16
@@ -18,18 +21,17 @@ def _sb(dtype, **kw):
         SCRATCH[k] = ("sbuf", [128, kw[k]], dtype)
 
 
-_sb(H, x0=4 * C, xt=4 * C, xp=4 * C, xq=4 * P, yp=4 * P, zt=4 * C, z128=4 * C, ut=512, vt=512, et=2048,
-    sg=C, pp=C + 16, pb=C, eb=C, oddx=C + 16, neg2=C, ones=512, go=4 * 208, gr=4 * 208, yb=C, cvb=C, scb=C, xg=CW,
-    iotb=CW, nl=CW, nh=CW, tk=CW, ti=CW, szr=CW + 16, szp=CW, keep1=CW, keepb=CW, inc=CW, kp=C)
-_sb(G, kc=CW, nv=CW, hh=CW, uu=CW, tr=2 * C, seg=C)
+_sb(H, x0=4 * C, xt=4 * C, xp=4 * C, xq=4 * P, yp=4 * P, zt=4 * C, z128=4 * C, ut=512, vt=512, et=528,
+    sg=C, pp=C + 16, pb=C, eb=C, oddx=C + 16, neg2=C, ones=2 * C, go=4 * 208, gr=4 * 208, yq=C, rb=C, xg=CW, dj=CW,
+    iotb=CW, nl=CW, nh=CW, tk=CW, ti=CW, szr=CW + 16, szp=CW, keep1=CW, keepb=CW, inc=CW, kp=2 * C, s3=C, c3=C, ub=C, sig=C)
+_sb(G, kc=CW, nv=CW, nv2=CW, hh=CW, uu=CW, tr=2 * C, seg=2 * C, id16=C, val=C)
 _sb(Q, qu=128, qur=128, qv=128, qe=512, qw=512, qz=C, qx0=C, qx1=C, qx2=C, qx3=C, ql0=C, ql1=C, ql2=C)
 _sb(S, su=128, sur=128, sv=128, se=512, sw=512, szz=C, sx0=C, sx1=C, sx2=C, sx3=C, sl0=C, sl1=C, sl2=C)
-_sb(I, tz=32, tp=24, i1=24, i2=24, i3=24, wi=24, oi=24)
-_sb(U, lend=24, lsz=26, lpx=26, lpr=26, ld=24, ldw=24, lca=24, lb=24, lsib=24, lnm=24, lp16=24, lu=8, l1=24, l2=24, lpos=24,
-    lst0=48, lst1=48, lst2=48, ll0=48, ll1=48, ll2=48)
-_sb(F, iot=776, sm=32 * 40, c16=64, c48=48, pk=48, pws=64, cor=24, cv1=C, krow=CW, pa=CW + 8, y32=CW + 8, dy=C,
-    rd=392, sc=C, sc2=C, nd1=C, vv=C, v2=C, ca=C, dw=W, aw=W, bt=W, base=W, dwg=C,
-    m0=C, ma=C, mb=C, nr=C, yy=C, orow=392, otr=C, yo=C)
+_sb(I, tz=64, i1=24, i2=26, i3=24, wi=24, oi=24)
+_sb(U, ls=26 * 16, lu=8, lst0=48, lst1=48, lst2=48, ll0=48, ll1=48, ll2=48)
+_sb(F, iot=776, sm=64 * 24, c16=64, c48=48, pk=96, pws=64, cor=32, cv1=C, krow=CW, pa=CW + 8, y32=C + 8, dy=C,
+    rd=392, sc=C, nd1=C, vv=C, v2=C, ca=C, dw=W, aw=W, bt=W, base=W, dwg=C,
+    m0=C, ma=C, mb=C, nr=C, yy=C, orow=C, otr=C, yo=C)
 SCRATCH["pd"] = ("psum", [128, 2048], F)
 SCRATCH["pq"] = ("psum", [128, 2048], F)
 
@@ -134,33 +136,50 @@ def rank_program(g, core, T, topo):
     def mm(r, w, out, lq, ls, rq, rs):
         run("p", r, w, lambda: g.tensor.matmul_mx(out, lq, ls, rq, rs, True, True))
 
-    slot = {}
+    slot, lslot, cslot = {}, {}, {}
 
     def sm(name, a=0, b=24, step=1):
         if name not in slot:
             slot[name] = len(slot)
-        return T.sm[:, 32 * slot[name] + a:32 * slot[name] + b:step]
+        return T.sm[:, 64 * slot[name] + a:64 * slot[name] + b:step]
 
-    def cor(j):
-        return T.cor[:, j:j + 1]
+    def li(name, a=0, b=24, step=1):
+        if name not in lslot:
+            lslot[name] = len(lslot)
+        return T.ls[:, 26 * lslot[name] + a:26 * lslot[name] + b:step]
+
+    def cor(name):
+        if name not in cslot:
+            cslot[name] = len(cslot)
+        return T.cor[:, cslot[name]:cslot[name] + 1]
 
     def ind(buf, n, lst, k=24):
-        return T[buf][:, 0:n].indirect(T[lst][:, 0:k])
+        return T[buf][:, 0:n].indirect(li(lst, 0, k))
 
     add, sub, mul, mx, mn = op_.add, op_.subtract, op_.mult, op_.max, op_.min
 
-    def conv(r, src, dst="sc", init=2.0 * B):
-        scan(r + " cv1", dst, T[dst][:, 0:C], src, T.cv1[:, 0:C], init, mn, add)
-        return T[dst][:, 15:C:16]
+    def lin(e, name, src, m, c):
+        if e == "v":
+            ts(src, name, cor(name), cor(src), m, mul, c, add)
+        else:
+            ac(src, name, cor(name), cor(src), m, c)
 
-    def classes(r, src, o):
-        run("v", r, "tr0", lambda: V.transpose(T.tr[:, 0:C], src[:, 0:C]))
-        run("v", r, "tr1", lambda: V.transpose(T.tr[:, C:2 * C], src[:, 16:CW]))
-        scan("kp tr0 tr1", "seg", T.seg[:], T.kp[:], T.tr[:, 0:2 * C:2], 0.0, mul, o)
-        scan("seg c48a c48b", "pk", T.pk[:], T.seg[:, 7:C:8], T.c48[:], -4096.0, mx, add)
-        return T.pk[:, 1:24:2], T.pk[:, 25:48:2]
+    def conv(r, src, init=2.0 * B):
+        scan(r + " cv1", "sc", T.sc[:], src, T.cv1[:], init, mn, add)
+        return T.sc[:, 15:C:16]
 
-    dmas("a", "ltree", "", "tz tp", [(T.tz[:, 4:28], T.sz[:]), (T.tp[:], T.pr[:])])
+    def turn():
+        run("v", "uu", "tr0", lambda: V.transpose(T.tr[:, 0:C], T.uu[:, 0:C]))
+        run("v", "uu", "tr1", lambda: V.transpose(T.tr[:, C:2 * C], T.uu[:, 16:CW]))
+
+    def join(o):
+        scan("kp tr0 tr1", "seg", T.seg[:], T.kp[:], T.tr[:], 0.0, mul, o)
+
+    def pick(j, k):
+        scan("seg c48a c48b", "pk%d" % k, T.pk[:, 48 * k:48 * k + 48], T.seg[:, j:2 * C:16], T.c48[:], -4096.0, mx, add)
+        return T.pk[:, 48 * k + 1:48 * k + 24:2], T.pk[:, 48 * k + 25:48 * k + 48:2]
+
+    dmas("a", "ltree", "", "tz", [(T.tz[:, 4:28], T.sz[:]), (T.tz[:, 36:60], T.pr[:])])
     dmas("s", "lx", "", "x0", [(T.x0[:], T.x[:])])
     dmas("a", "lu_", "", "ut", [(T.ut[:], T.u[:])])
     dmas("s", "lw", "x0", "qw", [(T.qw[:].bitcast(dt.uint8), T.wc[:]), (T.sw[:], T.ws[:])])
@@ -168,85 +187,68 @@ def rank_program(g, core, T, topo):
 
     iota("i1", T.i1[:], [[0, 24]], 0, 1, False)
     iota("i3", T.i3[:, 0:16], [[1, 16]], 128, -1, False)
-    iota("pw", T.pws[:, 48:64], [[0, 8], [-1, 2]], 2, 0, True)
-    iota("i2", T.i2[:], [[16, 24]], 0, 0, False)
+    iota("iotb", T.iotb[:], [[1, CW]], 0, 0, True)
+    iota("i2", T.i2[:], [[16, 26]], 0, 0, False)
     iota("iot", T.iot[:, 0:CW], [[1, CW]], 0, 0, True)
+    fill("pw", T.pws[:, 48:64], 2.0)
     fill("ones", T.ones[:], 1.0)
-    run("g", "ones", "kp", lambda: g.affine_select(T.kp[:], T.ones[:, 0:C], [[0, 48], [1, 8]], op_.is_gt, 0.0, 0, 0))
+    run("g", "ones", "kp", lambda: g.affine_select(T.kp[:], T.ones[:], [[0, 48], [1, 16]], op_.is_gt, 0.0, 0, 0))
     iota("iot2", T.iot[:, CW:776], [[1, 776 - CW]], CW, 0, True)
-    for b in range(4):
-        run("g", "ones", "et%d" % b, lambda: g.affine_select(T.et[:, 512 * b:512 * b + 512], T.ones[:], [[1, 512]], op_.is_equal, 0.0, -b, -4))
-    iota("bt", T.bt[:, S0:W], [[0, W - S0]], 0, 0, True)
+    run("g", "ones", "et", lambda: g.affine_select(T.et[:], T.ones[:, 0:528], [[1, 528]], op_.is_equal, 0.0, -3, -4))
+    iota("bt", T.bt[:, S0:S1 + 8], [[0, S1 + 8 - S0]], 0, 0, True)
 
-    HI, LO, THR, TH2, THL, RT, K0, KZ, KR, KP_, K6, K7, H16, Z0 = range(14)
-    fill("tz_", T.tz[:, 0:4], 0)
-    fill("tze", T.tz[:, 28:32], 0)
-    fill("prc_", sm("prc", 0, 32), 0.0)
-    fill("neg2", T.neg2[:], -2.0)
+    scan("pw", "pw2", T.pws[:, 0:16], T.pws[:, 48:64], T.pws[:, 48:64], 1.0, mul, mx)
+    fill("tz0", T.tz[:, 0:4], 0)
+    fill("tz1", T.tz[:, 28:32], 0)
+    fill("tz3", T.tz[:, 32:36], -1)
+    fill("tz2", T.tz[:, 60:64], 0)
     ts("i1", "ih", T.i3[:, 16:17], T.i1[:, 0:1], 4, op_.arith_shift_right, 1, op_.bitwise_and)
     ts("i3", "i3", T.i3[:, 0:16], T.i3[:, 0:16], 15, op_.bitwise_and)
-    scan("pw", "pw2", T.pws[:, 0:16], T.pws[:, 48:64], T.pws[:, 48:64], 1.0, mul, mx)
     ts("i1 ih", "i1", T.i1[:], T.i1[:], 15, op_.bitwise_and)
+    cp("ih", "hi", cor("hi"), T.i3[:, 16:17])
     ts("i3", "c16m", T.c16[:, 48:64], T.i3[:, 0:16], 0.0, op_.is_equal)
-    cp("ih", "hi", cor(HI), T.i3[:, 16:17])
+    ts("i1", "z0", cor("z0"), T.i1[:, 0:1], 0.0, op_.is_equal)
+    ts("i1", "a8", cor("a8"), T.i1[:, 0:1], 8.0, op_.is_ge)
     tt("c16m pw2", "pw3", T.pws[:, 16:32], T.c16[:, 48:64], T.pws[:, 0:16], mul)
-    tt("i1 i2", "n", sm("n"), T.i1[:], T.i2[:], add)
+    lin("v", "lo", "hi", -1.0, 1.0)
+    ts("i1", "e9", cor("e9"), T.i1[:, 0:1], 9.0, op_.is_equal)
     scan("pw3", "thr", T.pws[:, 32:48], T.pws[:, 16:32], T.pws[:, 16:32], 0.0, add, mx)
     thr = T.pws[:, 47:48]
-    ts("hi", "lo", cor(LO), cor(HI), -1.0, mul, 1.0, add)
-    ts("thr", "th2", cor(TH2), thr, 2.0, mul)
-    ts("thr", "thl0", cor(THR), thr, 2.0, op_.is_equal)
-    ac("iot", "iotb", T.iotb[:], T.iot[:, 0:CW])
-    ts("hi", "kr", cor(KR), cor(HI), -32.0, mul, 777.0, add)
-    tt("thr thl0", "thl", cor(THL), thr, cor(THR), sub)
-    ac("iot kr", "krow", T.krow[:], T.iot[:, 0:CW], 2.0, cor(KR))
-    ts("hi", "rt", cor(RT), cor(HI), -16.0, mul, float(CW + 1), add)
-    ts("hi", "h16", cor(H16), cor(HI), 16.0, mul)
-    ts("iotb thl", "nl", T.nl[:], T.iotb[:], cor(THL), op_.is_ge, 1.0, add)
-    ts("iotb th2", "nh", T.nh[:], T.iotb[:], cor(TH2), op_.is_lt, -2.0, add)
-    ac("nl", "tk", T.tk[:], T.nl[:], 4096.0, -3324.0)
-    ts("n rt", "root", sm("root"), sm("n"), 0.0, op_.is_equal, cor(RT), mul)
+    lin("v", "h17", "hi", 16.0, 1.0)
+    lin("a", "tkb", "a8", 4096.0, 800.0 - 4096.0)
+    lin("a", "ks", "a8", -1.0, 2.0)
+    lin("v", "k1", "a8", 2.0 * C - 1.0, KEY + 1.0)
+    ts("thr", "th2", cor("th2"), thr, 2.0, mul)
+    tt("thr z0", "thl", cor("thl"), thr, cor("z0"), sub)
+    ts("hi ks", "k2", cor("k2"), cor("hi"), -16.0, mul, cor("ks"), mul)
+    ts("iotb th2", "nh", T.nh[:], T.iotb[:], cor("th2"), op_.is_lt, -2.0, add)
+    ts("iotb thl", "nl", T.nl[:], T.iotb[:], cor("thl"), op_.is_ge, 1.0, add)
+    tt("k1 k2", "kr", cor("kr"), cor("k1"), cor("k2"), add)
+    ac("nl tkb", "tk", T.tk[:], T.nl[:], 4096.0, cor("tkb"))
     scan("nl nh", "ti", T.ti[:], T.nl[:], T.nh[:], 0.0, mx, add)
-    cp("i1", "lp16", T.lp16[:], T.i1[:])
-    ts("c16m", "c16a", T.c16[:, 16:32], T.c16[:, 48:64], -B, mul)
-    ts("i3", "c16b", T.c16[:, 32:48], T.i3[:, 0:16], 15.0, op_.is_equal, 2.0 * B, mul)
 
-    ts("tz tze lo", "za", sm("za", 0, 26), T.tz[:, 4:30], cor(LO), mul)
-    ts("tz tz_ tze hi", "zb", sm("zb", 0, 26), T.tz[:, 3:29], cor(HI), mul)
-    tt("tp root prc_", "prc", sm("prc", 4, 28), T.tp[:], sm("root"), add)
-    tt("za zb", "zc", sm("zc", 0, 26), sm("za", 0, 26), sm("zb", 0, 26), add)
-    ts("prc lo", "pa_", sm("pa_", 0, 26), sm("prc", 4, 30), cor(LO), mul)
-    cp("zc", "lsz", T.lsz[:], sm("zc", 0, 26))
-    ts("prc hi", "pb_", sm("pb_", 0, 26), sm("prc", 3, 29), cor(HI), mul)
-    ac("iot lsz", "szr", T.szr[:, 0:CW], ind("iot", CW, "lsz", 25))
-    fill("szr_", T.szr[:, CW:CW + 16], 1024.0)
-    tt("pa_ pb_", "pc", sm("pc", 0, 26), sm("pa_", 0, 26), sm("pb_", 0, 26), add)
+    ts("tz tz1 tz2 tz3 lo", "za", sm("za", 0, 58), T.tz[:, 4:62], cor("lo"), mul)
+    ts("tz tz0 tz1 tz2 tz3 hi", "zb", sm("zb", 0, 58), T.tz[:, 3:61], cor("hi"), mul)
+    tt("i1 i2", "n", sm("n"), T.i1[:], T.i2[:, 0:24], add)
+    tt("za zb", "zc", sm("zc", 0, 58), sm("za", 0, 58), sm("zb", 0, 58), add)
+    fill("szr_", T.szr[:, 0:1], 0.0)
+    cp("zc", "lsz", li("lsz", 0, 26), sm("zc", 0, 26))
+    ts("zc h17", "lpr", li("lpr", 0, 26), sm("zc", 32, 58), cor("h17"), add)
+    ac("iotb lsz", "szr", T.szr[:, 1:CW + 1], ind("iotb", CW, "lsz", 25))
+    ac("szr szr_ lpr", "szp", T.szp[:], ind("szr", CW + 1, "lpr", 25))
+    ac("iot ks kr", "krow", T.krow[:], T.iot[:, 0:CW], cor("ks"), cor("kr"))
     tt("tz n", "end", sm("end"), T.tz[:, 4:28], sm("n"), add)
-    ts("pc h16", "lpr", T.lpr[:], sm("pc", 0, 26), cor(H16), add)
     cp("ti lsz", "inc", T.inc[:], ind("ti", CW, "lsz", 25))
-    ac("szr szr_ lpr", "szp", T.szp[:], ind("szr", CW + 16, "lpr", 25))
-    cp("pc", "lpx", T.lpx[:], sm("pc", 0, 26))
-    cp("end", "lend", T.lend[:], sm("end"))
-    tt("c16a c16b", "c16", T.c16[:, 0:16], T.c16[:, 16:32], T.c16[:, 32:48], add)
-    ts("i1", "z0", cor(Z0), T.i1[:, 0:1], 0.0, op_.is_equal)
-    ac("c16 lp16", "cv1", T.cv1[:], ind("c16", 16, "lp16"))
-    ac("cv1", "cvb", T.cvb[:], T.cv1[:], 4.0 / B)
+    lin("v", "kb", "a8", 6144.0, -2048.0)
     cp("i2", "lu", T.lu[:], T.i2[:, 0:8])
-    fill("pa0", T.pa[:, CW:CW + 8], 0.0)
-    ts("ones hi", "c48x", sm("c48x"), T.ones[:, 0:24], cor(HI), mul)
-    ts("tp", "pr1", sm("pr1"), T.tp[:], 1.0, add)
-    ts("c48x", "c48a", T.c48[:, 0:48:2], sm("c48x"), -4096.0, mul, 2048.0, add)
-    ts("c48x", "c48b", T.c48[:, 1:48:2], sm("c48x"), 2048.0, mul, -2816.0, add)
-    ts("szp th2", "keep1", T.keep1[:], T.szp[:], cor(TH2), op_.is_lt)
-    ts("szp thr", "keepb", T.keepb[:], T.szp[:], thr, op_.is_lt, -2048.0, mul)
-
-    scan("keep1 inc", "pa", T.pa[:, 0:CW], T.keep1[:], T.inc[:], 0.0, mul, sub)
     quant("ut", "qu", T.qu[:], T.su[:], T.ut[:])
-    tt("pa pa0 lpr keepb", "hh", T.hh[:], ind("pa", CW + 8, "lpr", 25), T.keepb[:], add)
+    cp("end", "lend", li("lend"), sm("end"))
+    ts("zc", "lpx", li("lpx", 0, 26), sm("zc", 32, 58), 1.0, add)
     cp("qu lu", "qur", T.qur[:].bitcast(dt.uint32), T.qu[:].bitcast(dt.uint32).indirect(T.lu[:]))
     run("a", "qu lu", "sur", lambda: g.scalar.activation(T.sur[:], T.su[:].indirect(T.lu[:]), act.Copy))
-    scan("hh inc", "uu", T.uu[:], T.hh[:], T.inc[:], 0.0, mx, sub)
-    quant("x0", "qxo0 qxr0", T.qx0[:], T.sx0[:], T.x0[:])
+    fill("pa0", T.pa[:, 0:1], 0.0)
+    ts("szp th2", "keep1", T.keep1[:], T.szp[:], cor("th2"), op_.is_lt)
+    ts("szp thr kb", "keepb", T.keepb[:], T.szp[:], thr, op_.is_lt, cor("kb"), mul)
 
     def send(t, what):
         dst = T.cores[(rank + STEP[t]) % n_ranks]
@@ -278,65 +280,104 @@ def rank_program(g, core, T, topo):
         h, c0, bank = ("o", A, 0) if own else ("r", 0, 1)
         ts("pd%d" % bank, "sg" + h, T.sg[:, c0:c0 + A], T.pd[:, 512 * bank:512 * bank + A], 0.0, op_.is_gt, 0.5, sub)
 
+    def parity():
+        scan("sgo sgr neg2", "pp", T.pp[:, 1:C + 1], T.sg[:], T.neg2[:], 20.0, mul, mul)
+        ac("sgo sgr", "dy", T.dy[:], T.sg[:], 799.0, -1199.5)
+        scan("sgo sgr neg2", "pb", T.pb[:], T.sg[:], T.neg2[:], 20.0, mul, mul)
+
+    def ends():
+        tt("pp pp_ pb lend", "eb", T.eb[:], ind("pp", C + 1, "lend"), T.pb[:], mul)
+
+    def kinds():
+        scan("eb dy", "y32", T.y32[:, 1:C + 1], T.eb[:], T.dy[:], -4096.0, mx, add)
+        y = T.y32[:, 1:C + 1]
+        ac("y32 y32_ lpx xs xb", "xg", T.xg[:], ind("y32", C + 1, "lpx", 25), cor("xs"), cor("xb"), act.Relu)
+        ac("y32 yb", "yq", T.yq[:], y, 1.0 / 799.5, cor("yb"), act.Abs)
+        ac("yq lid js jb", "dj", T.dj[:], ind("yq", C, "lid", 25), cor("js"), cor("jb"), act.Relu)
+        ac("y32", "oddx", T.oddx[:, 1:C + 1], y, 1.0 / 799.5, 1199.5 / 799.5, act.Abs)
+        ac("y32", "rb", T.rb[:], y, 1.0 / 799.5, 1199.5 / 799.5, act.Relu)
+
+    scan("keep1 inc", "pa", T.pa[:, 1:CW + 1], T.keep1[:], T.inc[:], 0.0, mul, sub)
+    quant("x0", "qxo0 qxr0", T.qx0[:], T.sx0[:], T.x0[:])
     score(0, True)
     score(0, False)
     send(0, "codes")
-    iota("aw", T.aw[:, 0:C], [[0, C]], -2048, 0, True)
-    iota("aw_", T.aw[:, S0:W], [[0, W - S0]], -2048, 0, True)
+    iota("aw aw_", T.aw[:, S0:W], [[0, W - S0]], -2048, 0, True)
     for b in range(4):
         iota("xq_%d" % b, T.xq[:, P * b:P * b + 16], [[0, 16]], 0, 0, True)
         iota("yp_%d" % b, T.yp[:, P * b:P * b + 16], [[0, 16]], 0, 0, True)
-
-    pe, po = classes("uu", T.uu, add)
-    tt("n pr1", "b", sm("b"), sm("n"), sm("pr1"), sub)
-    ts("pk", "de", sm("d", 0, 24, 2), pe, -1.0, mul, -769.0, add)
-    ts("pk", "do", sm("d", 1, 24, 2), po, -1.0, mul, -769.0, add)
-    ts("b", "s1", sm("s1"), sm("b"), 0.0, op_.is_gt, 775.0, mul)
-    cp("de do", "ld", T.ld[:], sm("d"))
-    ts("de do", "d2", sm("d2"), sm("d"), 2.0, mul)
-    ts("b", "s0", sm("s0"), sm("b"), 0.0, op_.is_equal, 771.0, mul)
-    ac("iot ld", "nd1", T.nd1[:], ind("iot", CW, "ld"), -1.0, -399.0)
-    tt("d2 s1", "t10", sm("t10"), sm("d2"), sm("s1"), mx)
-    tt("d2 s0", "t11", sm("t11"), sm("d2"), sm("s0"), mx)
-    fill("pp_", T.pp[:, 0:1], 24.0)
-    cp("t10", "lca", T.lca[:], sm("t10"))
-    cp("t11", "ldw", T.ldw[:], sm("t11"))
+    tt("pa pa0 lpr keepb", "hh", T.hh[:], ind("pa", CW + 1, "lpr", 25), T.keepb[:], add)
+    fill("neg2", T.neg2[:], -2.0)
+    lin("a", "xs", "a8", 1.0, -1.0)
+    lin("a", "xb", "a8", 1199.0, -1199.0)
+    lin("a", "yb", "e9", 1.0, 1199.5 / 799.5)
+    lin("a", "js", "a8", 1538.0, 0.0)
+    scan("hh inc", "uu", T.uu[:], T.hh[:], T.inc[:], 0.0, mx, sub)
     signs(True)
     signs(False)
+    turn()
+    fill("pp_", T.pp[:, 0:1], 20.0)
+    parity()
+    join(add)
+    ts("ones hi", "c48a", T.c48[:, 0:48:2], T.ones[:, 0:24], cor("hi"), mul, -4096.0, mul)
+    ts("ones hi", "c48b", T.c48[:, 1:48:2], T.ones[:, 0:24], cor("hi"), mul, 2048.0, mul)
+    ts("i2 h17", "lid0", sm("lid0", 0, 26), T.i2[:], cor("h17"), sub, 1.0, add)
+    ts("c48a", "c48a", T.c48[:, 0:48:2], T.c48[:, 0:48:2], 2048.0, add)
+    ts("c48b", "c48b", T.c48[:, 1:48:2], T.c48[:, 1:48:2], -2048.0 - OFF, add)
+    cp("i1", "j16", cor("j16"), T.i1[:, 0:1])
+    ends()
+    pe, po = pick(7, 0)
+    ts("lid0 j16", "lid", li("lid", 0, 26), sm("lid0", 0, 26), cor("j16"), add, C - 1.0, mn)
+    ts("e9 a8", "jb", cor("jb"), cor("e9"), -1538.0, mul, -2.0, add)
+    fill("y32_", T.y32[:, 0:1], -1200.0)
+    kinds()
+    ts("pk0", "de", sm("d", 0, 24, 2), pe, -1.0, mul, -OFF - 1.0, add)
+    ts("pk0", "do", sm("d", 1, 24, 2), po, -1.0, mul, -OFF - 1.0, add)
+    tt("n tz", "b", sm("b"), sm("n"), T.tz[:, 36:60], sub)
+    cp("de do", "ld", li("ld"), sm("d"))
     tt("tk lsz krow", "kc", T.kc[:], ind("tk", CW, "lsz", 25), T.krow[:], mn)
-    fill("y32_", T.y32[:, C:CW + 8], -1152.0)
-    ac("iot", "yy", T.yy[:], T.iot[:, 0:C], -1.0 / 2048, 400.0)
+    ts("de do", "d2", sm("d2"), sm("d"), 2.0, mul)
+    ts("b", "s1", sm("s1"), sm("b"), 1.0, op_.is_gt, 775.0, mul)
+    ts("b", "s0", sm("s0"), sm("b"), 1.0, op_.is_equal, 771.0, mul)
+    tt("d2 s1", "t10", sm("t10"), sm("d2"), sm("s1"), mx)
+    tt("d2 s0", "t11", sm("t11"), sm("d2"), sm("s0"), mx)
 
-    def front(t):
-        scan("sgo sgr neg2", "pp", T.pp[:, 1:C + 1], T.sg[:], T.neg2[:], 24.0, mul, mul)
-        ac("sgo sgr", "dy", T.dy[:], T.sg[:], 767.0, -1151.5)
-        scan("sgo sgr neg2", "pb", T.pb[:], T.sg[:], T.neg2[:], 16.0, mul, mul)
-        tt("pp pp_ pb lend", "eb", T.eb[:], ind("pp", C + 1, "lend"), T.pb[:], mul)
-        scan("eb dy", "y32", T.y32[:, 0:C], T.eb[:], T.dy[:], -4096.0, mx, add)
-        ac("y32 y32_ lpx", "xg", T.xg[:], ind("y32", CW + 8, "lpx", 25), -1.0, -1151.0, act.Relu)
-        ac("y32", "yb", T.yb[:], T.y32[:, 0:C], 1.0 / 767.5, 1151.5 / 767.5)
-        ac("yb", "oddx", T.oddx[:, 1:C + 1], T.yb[:], 1.0, 0.0, act.Abs)
-
-    front(0)
-    for j, m, c in [(K0, -2.0 * B, B), (KZ, 8.0, -4.0), (KP_, -2.0 * B, B - BIG - 1.0), (K6, 4.0 * B, -799.0 - 2.0 * B),
-                    (K7, -2.0 * B, B + 400.0 - 1.125)]:
-        ts("z0", "k%d" % j, cor(j), cor(Z0), m, mul, c, add)
-    ts("pr1", "lnm", T.lnm[:], sm("pr1"), 2.0, mul, float(S0 + 1), add)
-    ts("end", "lsib", T.lsib[:], sm("end"), 2.0, mul, float(S0 + 1), add)
-    fill("rd_", T.rd[:, 0:1], BIG)
-    fill("oddx_", T.oddx[:, 0:1], 1.0)
-    fill("orow_", T.orow[:, 7:8], -400.0)
-    fill("go_", T.go[:, A:4 * 208:208], 0.0)
-
-    def statics():
-        ac("nd1", "dw0", T.dw[:, 0:C], T.nd1[:], -1.0, -399.0)
-        ac("nd1", "dw1", T.dw[:, S0:S0 + 2 * C:2], T.nd1[:], -1.0, -399.0)
-        ac("iot iot2 ldw", "dw2", T.dw[:, S0 + 1:S0 + 2 * C:2], ind("iot", 776, "ldw"), 1.0, -385.0)
-        ac("iot iot2 lca", "ca", T.ca[:], ind("iot", 776, "lca"), -1.0, -797.0)
+    def statics(k):
+        if k == 0:
+            cp("t10", "lca", li("lca"), sm("t10"))
+            cp("t11", "ldw", li("ldw"), sm("t11"))
+            ac("iot ld", "nd1", T.nd1[:], ind("iot", CW, "ld"), -1.0, -399.0)
+            ac("iot", "yy", T.yy[:], T.iot[:, 0:C], -1.0 / 2048, 400.0)
+        if k == 1:
+            ts("c16m", "c16a", T.c16[:, 16:32], T.c16[:, 48:64], -B, mul)
+            ts("i3", "c16b", T.c16[:, 32:48], T.i3[:, 0:16], 15.0, op_.is_equal, 2.0 * B, mul)
+            cp("i1", "lp16", li("lp16"), T.i1[:])
+            tt("c16a c16b", "c16", T.c16[:, 0:16], T.c16[:, 16:32], T.c16[:, 32:48], add)
+        if k == 2:
+            tt("iot ld yy", "vv", T.vv[:], ind("iot", CW, "ld"), T.yy[:], add)
+            ac("nd1", "dw0", T.dw[:, S1:W], T.nd1[:], -1.0, -399.0)
+            ac("nd1", "dw1", T.dw[:, S0:S1:2], T.nd1[:], -1.0, -399.0)
+            ac("iot iot2 ldw", "dw2", T.dw[:, S0 + 1:S1:2], ind("iot", 776, "ldw"), 1.0, -385.0)
+            ac("iot iot2 lca", "ca", T.ca[:], ind("iot", 776, "lca"), -1.0, -797.0)
+        if k == 3:
+            ts("tz", "lnm", li("lnm"), T.tz[:, 36:60], 2.0, mul, float(S0 + 3), add)
+            ts("end", "lsib", li("lsib"), sm("end"), 2.0, mul, float(S0 + 1), add)
+            ac("nd1", "v2", T.v2[:], T.nd1[:], -1.0, 401.0)
+            ac("c16 lp16", "cv1", T.cv1[:], ind("c16", 16, "lp16"))
+        if k == 4:
+            lin("v", "k0", "z0", -2.0 * B, B)
+            lin("v", "kp_", "z0", -2.0 * B, B - BIG - 1.0)
+            fill("rd_", T.rd[:, 0:1], BIG)
+            fill("oddx_", T.oddx[:, 0:1], 1.0)
+            fill("go_", T.go[:, A:4 * 208:208], 0.0)
+            for b in range(4):
+                quant("et", "qe%d" % b, T.qe[:, 128 * b:128 * b + 128], T.se[:, 128 * b:128 * b + 128], T.et[:, 3 - b:515 - b])
+        if k == 5:
+            cp("iot", "id16", T.id16[:], T.iot[:, 16:CW])
 
     def unpack(t):
         for b in range(4):
-            mm("qe ac%d" % t, "pd%d" % b, T.pd[:, 512 * b:512 * b + C], T.qe[:, 128 * b:128 * b + 128], T.se[:, 128 * b:128 * b + 128],
+            mm("qe%d ac%d" % (b, t), "pd%d" % b, T.pd[:, 512 * b:512 * b + C], T.qe[:, 128 * b:128 * b + 128], T.se[:, 128 * b:128 * b + 128],
                T["ql%d" % t][:], T["sl%d" % t][:])
         for b in range(4):
             ac("pd%d" % b, "yp%d" % b, T.yp[:, P * b + 16:P * b + P], T.pd[:, 512 * b:512 * b + C])
@@ -350,61 +391,66 @@ def rank_program(g, core, T, topo):
 
     for t in range(NR):
         lst, ll = T["lst%d" % t], T["ll%d" % t]
+
+        def once(k):
+            if t == 0:
+                statics(k)
+
         if t:
-            front(t)
-        else:
-            tt("iot ld yy", "vv", T.vv[:], ind("iot", CW, "ld"), T.yy[:], add)
+            parity()
+            ends()
+            kinds()
         scan("xg kc", "nv", T.nv[:], T.xg[:], T.kc[:], 0.0, mx, sub)
-        ac("nd1", "bt", T.bt[:, S0:S0 + 2 * C:2], T.nd1[:], -1.0)
-        if t == 0:
-            statics()
-            ac("vv", "v2", T.v2[:], T.vv[:], 1.0, 400.0)
-        scan("keep1 nv", "pa", T.pa[:, 0:CW], T.keep1[:], T.nv[:], 0.0, mul, mn)
-        scan("yb cvb", "scb", T.scb[:], T.yb[:], T.cvb[:], 8.0, mn, add)
-        tt("pa pa0 lpr keepb", "hh", T.hh[:], ind("pa", CW + 8, "lpr", 25), T.keepb[:], add)
-        ts("scb k%d" % KZ, "zn", sm("zn"), T.scb[:, 15:C:16], -1.0, mul, cor(KZ), add)
-        scan("hh nv", "uu", T.uu[:], T.hh[:], T.nv[:], 0.0, mx, mn)
-        if t == 0:
-            quant("et0 et1 et2 et3", "qe", T.qe[:], T.se[:], T.et[:])
-        pe, po = classes("uu", T.uu, mn)
-        planes(t, range(4))
-        tt("pk zn", "we", sm("w", 0, 24, 2), pe, sm("zn", 0, 24, 2), mul)
-        tt("pk zn", "wo", sm("w", 1, 24, 2), po, sm("zn", 1, 24, 2), mul)
-        tt("we wo n", "l1f", sm("l1f"), sm("w"), sm("n"), mx)
-        ts("we wo", "wn", sm("wn"), sm("w"), -1.0, mul)
-        cp("l1f", "l1", T.l1[:], sm("l1f"))
-        tt("wn l1f", "l2f", sm("l2f"), sm("wn"), sm("l1f"), mx)
-        cp("l2f", "l2", T.l2[:], sm("l2f"))
-        cp("vv l1", "bt", ind("bt", W, "l1"), T.vv[:])
-        ac("dw0 dw1 dw2 l2", "dwg", T.dwg[:], ind("dw", W, "l2"), 1.0, 400.0)
-        tt("bt lsib ca", "aw aw_", T.aw[:, S0 + 1:S0 + 2 * C:2], ind("bt", W, "lsib"), T.ca[:], add)
+        once(0)
+        scan("keep1 nv", "pa", T.pa[:, 1:CW + 1], T.keep1[:], T.nv[:], 0.0, mul, mn)
+        once(1)
+        tt("pa pa0 lpr keepb", "hh", T.hh[:], ind("pa", CW + 1, "lpr", 25), T.keepb[:], add)
+        scan("dj nv", "nv2", T.nv2[:], T.dj[:], T.nv[:], 0.0, mx, add)
+        scan("hh nv2", "uu", T.uu[:], T.hh[:], T.nv2[:], 0.0, mx, mn)
+        ac("nd1", "bt", T.bt[:, S0:S1:2], T.nd1[:], -1.0)
+        once(2)
+        turn()
+        once(3)
+        join(mn)
+        pe, po = pick(9, 0)
+        qe_, qo = pick(8, 1)
+        ts("pk0", "l1e", li("l1", 0, 24, 2), pe, -1.0, mul)
+        ts("pk0", "l1o", li("l1", 1, 24, 2), po, -1.0, mul)
+        ts("pk1", "l2e", li("l2", 0, 24, 2), qe_, -1.0, mul)
+        ts("pk1", "l2o", li("l2", 1, 24, 2), qo, -1.0, mul)
+        cp("vv l1e l1o", "bt", ind("bt", W, "l1"), T.vv[:])
+        ac("dw0 dw1 dw2 l2e l2o", "dwg", T.dwg[:], ind("dw", W, "l2"), 1.0, 400.0)
+        planes(t, range(2))
+        once(4)
+        tt("bt lsib ca", "aw aw_", T.aw[:, S0 + 1:S1:2], ind("bt", W, "lsib"), T.ca[:], add)
         ac("bt lnm", "ma", T.ma[:], ind("bt", W, "lnm"), 1.0, -784.0)
         scan("dwg v2", "nr", T.nr[:], T.dwg[:], T.v2[:], 0.0, mx, sub)
-        tt("aw aw_ l1 nd1", "yy", T.yy[:], ind("aw", W, "l1"), T.nd1[:], mx)
+        tt("aw aw_ l1e l1o nd1", "yy", T.yy[:], ind("aw", W, "l1"), T.nd1[:], mx)
+        ac("nr", "s3", T.s3[:], T.nr[:], 1.0, 400.0, act.Sign)
+        ac("s3", "c3", T.c3[:], T.s3[:], 2.5, -1.0, act.Abs)
         ac("nr", "mb", T.mb[:], T.nr[:], 1.0, 399.0, act.Abs)
         s = conv("ma", T.ma[:])
-        scan("bt yy", "rd", T.rd[:, 1:C + 1], T.bt[:, S0:S0 + 2 * C:2], T.yy[:], BIG, add, add)
-        ts("sc k%d" % K0, "wi", T.wi[:], s, cor(K0), add, -2048.0, mul)
-        ac("rd rd_", "base0", T.base[:, S0:S0 + 2 * C:2], T.rd[:, 0:C])
+        scan("bt yy", "rd", T.rd[:, 1:C + 1], T.bt[:, S0:S1:2], T.yy[:], BIG, add, add)
+        ts("sc k0", "wi", T.wi[:], s, cor("k0"), add, -2048.0, mul)
+        ac("rd rd_", "base0", T.base[:, S0:S1:2], T.rd[:, 0:C])
+        scan("rb c3", "ub", T.ub[:], T.rb[:], T.c3[:], 0.0, mx, sub)
+        ts("wi", "oi", T.oi[:], T.wi[:], 2047, op_.bitwise_and)
+        ac("ub", "sig", T.sig[:], T.ub[:], -1.0, -1.25, act.Sign)
+        planes(t, range(2, 4))
         unpack(t)
-        scan("rd oddx oddx_ ones", "base1", T.base[:, 0:C], T.ones[:, 0:C], T.oddx[:, 0:C], T.rd[:, C:C + 1], add, sub)
-        ts("wi", "oi", T.oi[:], T.wi[:], 2047, op_.bitwise_and)
-        cp("oi", "lb", T.lb[:], T.oi[:])
-        tt("rd rd_ lb ma", "base2", T.base[:, S0 + 1:S0 + 2 * C:2], ind("rd", C + 1, "lb"), T.ma[:], add)
-        tt("base0 base1 base2 l2 mb", "m0", T.m0[:], ind("base", W, "l2"), T.mb[:], add)
-        s = conv("m0", T.m0[:], "sc", BIG + 2.0 * B)
-        ts("sc k%d" % KP_, "lpos", T.lpos[:], s, cor(KP_), add)
-        cp("nr lpos", "orow", T.orow[:, 8:8 + C].indirect(T.lpos[:]), T.nr[:])
-        s = conv("orow", T.orow[:, 8:8 + C])
-        s2 = conv("orow orow_", T.orow[:, 7:7 + C], "sc2")
-        ts("sc k%d" % K6, "f1", sm("f1"), s, -1.0, mul, cor(K6), add)
-        ts("sc k%d" % K0, "wi", T.wi[:], s, cor(K0), add, 2048.0, mul)
-        tt("sc2 f1", "f2", sm("f2"), s2, sm("f1"), mx)
-        ts("wi", "oi", T.oi[:], T.wi[:], 2047, op_.bitwise_and)
-        ts("f2 k%d" % K7, "f3", sm("f3"), sm("f2"), cor(K7), add, 1024.0, mul)
-        ts("oi", "lsto%d" % t, lst[:, 0:24], T.oi[:], 16.0, add)
-        tt("f3 oi", "f4", sm("f4"), sm("f3"), T.oi[:], mn)
-        ts("f4", "lstf%d" % t, lst[:, 24:48], sm("f4"), 16.0, add)
+        scan("rd oddx oddx_ ones", "base1", T.base[:, S1:W], T.ones[:, 0:C], T.oddx[:, 0:C], T.rd[:, C:C + 1], add, sub)
+        cp("oi", "lb", li("lb"), T.oi[:])
+        once(5)
+        tt("rd rd_ lb ma", "base2", T.base[:, S0 + 1:S1:2], ind("rd", C + 1, "lb"), T.ma[:], add)
+        scan("id16 sig", "val", T.val[:], T.id16[:], T.sig[:], 0.0, mx, mul)
+        tt("base0 base1 base2 l2e l2o mb", "m0", T.m0[:], ind("base", W, "l2"), T.mb[:], add)
+        s = conv("m0", T.m0[:], BIG + 2.0 * B)
+        ts("sc kp_", "lpos", li("lpos"), s, cor("kp_"), add)
+        cp("val lpos", "orow", ind("orow", C, "lpos"), T.val[:])
+        s = conv("orow", T.orow[:])
+        ac("sc k0", "lof", sm("lof"), s, 1.0, cor("k0"), act.Abs)
+        ts("sc k0", "lstf%d" % t, lst[:, 24:48], s, cor("k0"), add)
+        cp("lof", "lsto%d" % t, lst[:, 0:24], sm("lof"))
         send(t, "lists")
 
         qn, sn = T["qx%d" % (t + 1)], T["sx%d" % (t + 1)]

@@ -10,7 +10,7 @@ S1 = S0 + 2 * C
 W = S1 + C
 B = 2560.0
 BIG = 8388608.0
-P = C + 16
+P = 4 * C
 
 F, H, G, I, U, Q, S = "float32", "bfloat16", "float16", "int32", "uint16", "float8_e4m3fn_x4", "uint8"
 SCRATCH = {}
@@ -21,21 +21,21 @@ def _sb(dtype, **kw):
         SCRATCH[k] = ("sbuf", [128, kw[k]], dtype)
 
 
-_sb(H, x0=4 * C, xt=4 * C, xp=4 * C, xq=4 * P, yp=4 * P, zt=4 * C, z128=4 * C, ut=512, vt=512, et=528,
-    sg=C, pp=C + 16, pb=C, eb=C, oddx=C + 16, neg2=C, ones=2 * C, go=4 * 208, gr=4 * 208, yq=C, rb=C, xg=CW, dj=CW,
-    iotb=CW, nl=CW, nh=CW, tk=CW, ti=CW, szr=CW + 16, szp=CW, keep1=CW, keepb=CW, inc=CW, kp=2 * C, s3=C, c3=C, ub=C, sig=C)
+_sb(H, x0=4 * C, xt=4 * C, xp=4 * C, xq=3 * P, yp=3 * P, zt=4 * C, z128=4 * C, ut=512, vt=512, et=528,
+    sg=C, pp=C + 16, pb=C + 16, eb=C, oddx=C + 16, neg2=A, ones=528, go=4 * 208, gr=4 * 208, yq=C, rb=C, yk=C, dy=C, dj=CW,
+    iotb=CW, nl=CW, nh=CW, tk=CW, ti=CW, szr=CW + 16, szp=CW, keep1=CW, keepb=CW, inc=CW, kp=A, s3=C, c3=C, ub=C, sig=C)
 _sb(G, kc=CW, nv=CW, nv2=CW, hh=CW, uu=CW, tr=2 * C, seg=2 * C, id16=C, val=C)
 _sb(Q, qu=128, qur=128, qv=128, qe=512, qw=512, qz=C, qx0=C, qx1=C, qx2=C, qx3=C, ql0=C, ql1=C, ql2=C)
 _sb(S, su=128, sur=128, sv=128, se=512, sw=512, szz=C, sx0=C, sx1=C, sx2=C, sx3=C, sl0=C, sl1=C, sl2=C)
 _sb(I, tz=64, i1=24, i2=26, i3=24, wi=24, oi=24)
-_sb(U, ls=26 * 16, lu=8, lst0=48, lst1=48, lst2=48, ll0=48, ll1=48, ll2=48)
-_sb(F, iot=776, sm=64 * 24, c16=64, c48=48, pk=96, pws=64, cor=32, cv1=C, krow=CW, pa=CW + 8, y32=C + 8, dy=C,
+_sb(U, ls=26 * 20, lu=8, lst0=24, lst1=24, lst2=24, ll0=16, ll1=16, ll2=16)
+_sb(F, iot=776, sm=64 * 24, c16=64, c48=48, pk=96, pws=64, cor=32, cv1=C, krow=CW, pa=CW + 8, rp=C + 8, dx=C,
     rd=392, sc=C, nd1=C, vv=C, v2=C, ca=C, dw=W, aw=W, bt=W, base=W, dwg=C,
-    m0=C, ma=C, mb=C, nr=C, yy=C, orow=C, otr=C, yo=C)
+    m0=C, ma=C, mb=C, nr=C, yy=C, orow=C, otr=C, yo=C, otab=P + C)
 SCRATCH["pd"] = ("psum", [128, 2048], F)
 SCRATCH["pq"] = ("psum", [128, 2048], F)
 
-SEMAPHORES = (["v0", "a0", "p0", "g0", "ltree", "lu_", "lx", "lw", "lv", "sent", "out"]
+SEMAPHORES = (["v0", "a0", "p0", "g0", "ltree", "lu_", "lx", "lw", "lv", "sent", "out", "dupx", "dupy"]
               + ["ac%d" % t for t in range(NR)] + ["al%d" % t for t in range(NR)])
 
 
@@ -165,18 +165,42 @@ def rank_program(g, core, T, topo):
             ac(src, name, cor(name), cor(src), m, c)
 
     def conv(r, src, init=2.0 * B):
-        scan(r + " cv1", "sc", T.sc[:], src, T.cv1[:], init, mn, add)
+        scan(r + " cv1", "sc sc0 sc1", T.sc[:], src, T.cv1[:], init, mn, add)
         return T.sc[:, 15:C:16]
 
+    def half(r, src, h, init=2.0 * B):
+        scan(r + " cv1", "sc sc%d" % h if h == 0 else "sc1", T.sc[:, A * h:A * h + A], src[:, A * h:A * h + A], T.cv1[:, 0:A], init, mn, add)
+
+    cut = [0, A + 16, CW]
+
+    def parents():
+        for h in range(2):
+            tt("pa pa0 lpr lpr2 keepb", "hh%d" % h, T.hh[:, cut[h]:cut[h + 1]],
+               T.pa[:, 0:CW + 1].indirect(li("lpr2", 0, 12) if h else li("lpr", 0, 13)), T.keepb[:, cut[h]:cut[h + 1]], add)
+
+    def down(h, row, r, o):
+        a, b = cut[h], cut[h + 1]
+        scan("hh%d uu0 %s" % (h, r), "uu%d" % h, T.uu[:, a:b], T.hh[:, a:b], row[:, a:b], T.uu[:, a - 1:a] if h else 0.0, mx, o)
+
     def turn():
-        run("v", "uu", "tr0", lambda: V.transpose(T.tr[:, 0:C], T.uu[:, 0:C]))
-        run("v", "uu", "tr1", lambda: V.transpose(T.tr[:, C:2 * C], T.uu[:, 16:CW]))
+        for h in range(2):
+            for k in range(2):
+                run("v", "uu0 uu%d" % h, "tr%d%d" % (h, k),
+                    lambda: V.transpose(T.tr[:, C * k + A * h:C * k + A * h + A], T.uu[:, 16 * k + A * h:16 * k + A * h + A]))
 
     def join(o):
-        scan("kp tr0 tr1", "seg", T.seg[:], T.kp[:], T.tr[:], 0.0, mul, o)
+        for h in range(2):
+            for k in range(2):
+                a = C * k + A * h
+                scan("kp tr%d%d" % (h, k), "seg%d%d" % (h, k), T.seg[:, a:a + A], T.kp[:], T.tr[:, a:a + A], 0.0, mul, o)
+
+    def evens(h):
+        back = slice(S1 + A * h + A - 1, S1 + A * h - 1, -1)
+        scan("oddx oddx_ ones base11", "base1%d" % h, T.base[:, back], T.oddx[:, A * h + A + 1:A * h + 1:-1], T.ones[:, 0:A],
+             BIG + C if h else T.base[:, S1 + A:S1 + A + 1], add, sub)
 
     def pick(j, k):
-        scan("seg c48a c48b", "pk%d" % k, T.pk[:, 48 * k:48 * k + 48], T.seg[:, j:2 * C:16], T.c48[:], -4096.0, mx, add)
+        scan("seg00 seg01 seg10 seg11 c48a c48b", "pk%d" % k, T.pk[:, 48 * k:48 * k + 48], T.seg[:, j:2 * C:16], T.c48[:], -4096.0, mx, add)
         return T.pk[:, 48 * k + 1:48 * k + 24:2], T.pk[:, 48 * k + 25:48 * k + 48:2]
 
     dmas("a", "ltree", "", "tz", [(T.tz[:, 4:28], T.sz[:]), (T.tz[:, 36:60], T.pr[:])])
@@ -192,7 +216,7 @@ def rank_program(g, core, T, topo):
     iota("iot", T.iot[:, 0:CW], [[1, CW]], 0, 0, True)
     fill("pw", T.pws[:, 48:64], 2.0)
     fill("ones", T.ones[:], 1.0)
-    run("g", "ones", "kp", lambda: g.affine_select(T.kp[:], T.ones[:], [[0, 48], [1, 16]], op_.is_gt, 0.0, 0, 0))
+    run("g", "ones", "kp", lambda: g.affine_select(T.kp[:], T.ones[:, 0:A], [[0, 12], [1, 16]], op_.is_gt, 0.0, 0, 0))
     iota("iot2", T.iot[:, CW:776], [[1, 776 - CW]], CW, 0, True)
     run("g", "ones", "et", lambda: g.affine_select(T.et[:], T.ones[:, 0:528], [[1, 528]], op_.is_equal, 0.0, -3, -4))
     iota("bt", T.bt[:, S0:S1 + 8], [[0, S1 + 8 - S0]], 0, 0, True)
@@ -215,9 +239,9 @@ def rank_program(g, core, T, topo):
     scan("pw3", "thr", T.pws[:, 32:48], T.pws[:, 16:32], T.pws[:, 16:32], 0.0, add, mx)
     thr = T.pws[:, 47:48]
     lin("v", "h17", "hi", 16.0, 1.0)
-    lin("a", "tkb", "a8", 4096.0, 800.0 - 4096.0)
+    lin("a", "tkb", "a8", 4096.0, 400.0 - 4096.0)
     lin("a", "ks", "a8", -1.0, 2.0)
-    lin("v", "k1", "a8", 2.0 * C - 1.0, KEY + 1.0)
+    lin("v", "k1", "a8", 2.0 * C - 1.0, KEY + 1.0 - 400.0)
     ts("thr", "th2", cor("th2"), thr, 2.0, mul)
     tt("thr z0", "thl", cor("thl"), thr, cor("z0"), sub)
     ts("hi ks", "k2", cor("k2"), cor("hi"), -16.0, mul, cor("ks"), mul)
@@ -244,6 +268,7 @@ def rank_program(g, core, T, topo):
     quant("ut", "qu", T.qu[:], T.su[:], T.ut[:])
     cp("end", "lend", li("lend"), sm("end"))
     ts("zc", "lpx", li("lpx", 0, 26), sm("zc", 32, 58), 1.0, add)
+    ts("zc h17", "lpr2", li("lpr2", 0, 12), sm("zc", 45, 57), cor("h17"), add)
     cp("qu lu", "qur", T.qur[:].bitcast(dt.uint32), T.qu[:].bitcast(dt.uint32).indirect(T.lu[:]))
     run("a", "qu lu", "sur", lambda: g.scalar.activation(T.sur[:], T.su[:].indirect(T.lu[:]), act.Copy))
     fill("pa0", T.pa[:, 0:1], 0.0)
@@ -260,8 +285,8 @@ def rank_program(g, core, T, topo):
             pairs = [(T["ql%d" % t][:].bitcast(dt.uint8), T["qx%d" % t][:].bitcast(dt.uint8)), (T["sl%d" % t][:], T["sx%d" % t][:])]
             sem = "ac%d" % t
         else:
-            r = ["lsto%d" % t, "lstf%d" % t]
-            pairs = [(T["ll%d" % t][:, 0:38], T["lst%d" % t][:, 0:38])]
+            r = ["lst%d" % t]
+            pairs = [(T["ll%d" % t][:, 0:14], T["lst%d" % t][:, 0:14])]
             sem = "al%d" % t
         before("g", r, [])
         for o, i in pairs:
@@ -280,22 +305,33 @@ def rank_program(g, core, T, topo):
         h, c0, bank = ("o", A, 0) if own else ("r", 0, 1)
         ts("pd%d" % bank, "sg" + h, T.sg[:, c0:c0 + A], T.pd[:, 512 * bank:512 * bank + A], 0.0, op_.is_gt, 0.5, sub)
 
-    def parity():
-        scan("sgo sgr neg2", "pp", T.pp[:, 1:C + 1], T.sg[:], T.neg2[:], 20.0, mul, mul)
-        ac("sgo sgr", "dy", T.dy[:], T.sg[:], 799.0, -1199.5)
-        scan("sgo sgr neg2", "pb", T.pb[:], T.sg[:], T.neg2[:], 20.0, mul, mul)
+    def parity(own):
+        h, c0 = ("o", A) if own else ("r", 0)
+        back = slice(c0 + A - 1, c0 - 1 if c0 else None, -1)
+        scan("neg2 ppo sg" + h, "pp" + h, T.pp[:, back], T.sg[:, back], T.neg2[:, 0:A], 20.0 if own else T.pp[:, A:A + 1], mul, mul)
+        ac("xs xb sg" + h, "dx" + h, T.dx[:, c0:c0 + A], T.sg[:, c0:c0 + A], cor("xs"), cor("xb"))
+        scan("neg2 pbo sg" + h, "pb" + h, T.pb[:, back], T.sg[:, back], T.neg2[:, 0:A], -20.0 if own else T.pb[:, A:A + 1], mul, mul)
+        ac("sg" + h, "dy" + h, T.dy[:, c0:c0 + A], T.sg[:, c0:c0 + A], -800.0, -1200.0)
 
-    def ends():
-        tt("pp pp_ pb lend", "eb", T.eb[:], ind("pp", C + 1, "lend"), T.pb[:], mul)
+    def ends(own):
+        if own:
+            tt("ppo pp_ pbo pb_ lendo", "ebo", T.eb[:, A:C], T.pp[:, A:C + 1].indirect(li("lendo", 0, 12)), T.pb[:, A + 1:C + 1], mul)
+        else:
+            tt("ppo ppr pp_ pbo pbr lend", "ebr", T.eb[:, 0:A], ind("pp", C + 1, "lend", 12), T.pb[:, 1:A + 1], mul)
+
+    def role(own):
+        h, c0 = ("o", A) if own else ("r", 0)
+        tt("eb%s dx%s" % (h, h), "rp" + h, T.rp[:, 1 + c0:1 + c0 + A], T.eb[:, c0:c0 + A], T.dx[:, c0:c0 + A], mn)
+
+    def kind(own):
+        h, c0 = ("o", A) if own else ("r", 0)
+        scan("eb%s dy%s" % (h, h), "yk" + h, T.yk[:, c0:c0 + A], T.eb[:, c0:c0 + A], T.dy[:, c0:c0 + A], -4096.0, mx, add)
+        ac("yb yk" + h, "yq" + h, T.yq[:, c0:c0 + A], T.yk[:, c0:c0 + A], -1.0 / 800, cor("yb"), act.Abs)
 
     def kinds():
-        scan("eb dy", "y32", T.y32[:, 1:C + 1], T.eb[:], T.dy[:], -4096.0, mx, add)
-        y = T.y32[:, 1:C + 1]
-        ac("y32 y32_ lpx xs xb", "xg", T.xg[:], ind("y32", C + 1, "lpx", 25), cor("xs"), cor("xb"), act.Relu)
-        ac("y32 yb", "yq", T.yq[:], y, 1.0 / 799.5, cor("yb"), act.Abs)
-        ac("yq lid js jb", "dj", T.dj[:], ind("yq", C, "lid", 25), cor("js"), cor("jb"), act.Relu)
-        ac("y32", "oddx", T.oddx[:, 1:C + 1], y, 1.0 / 799.5, 1199.5 / 799.5, act.Abs)
-        ac("y32", "rb", T.rb[:], y, 1.0 / 799.5, 1199.5 / 799.5, act.Relu)
+        ac("yqo yqr lid js jb", "dj", T.dj[:], ind("yq", C, "lid", 25), cor("js"), cor("jb"), act.Relu)
+        ac("yko ykr", "oddx", T.oddx[:, 1:C + 1], T.yk[:], -1.0 / 800, -1.5, act.Abs)
+        ac("yko ykr", "rb", T.rb[:], T.yk[:], -1.0 / 800, -1.5, act.Relu)
 
     scan("keep1 inc", "pa", T.pa[:, 1:CW + 1], T.keep1[:], T.inc[:], 0.0, mul, sub)
     quant("x0", "qxo0 qxr0", T.qx0[:], T.sx0[:], T.x0[:])
@@ -303,56 +339,67 @@ def rank_program(g, core, T, topo):
     score(0, False)
     send(0, "codes")
     iota("aw aw_", T.aw[:, S0:W], [[0, W - S0]], -2048, 0, True)
-    for b in range(4):
-        iota("xq_%d" % b, T.xq[:, P * b:P * b + 16], [[0, 16]], 0, 0, True)
-        iota("yp_%d" % b, T.yp[:, P * b:P * b + 16], [[0, 16]], 0, 0, True)
-    tt("pa pa0 lpr keepb", "hh", T.hh[:], ind("pa", CW + 1, "lpr", 25), T.keepb[:], add)
+    iota("xq_", T.xq[:, 2 * P:3 * P], [[0, P]], 0, 0, True)
+    iota("yp_", T.yp[:, 2 * P:3 * P], [[0, P]], 0, 0, True)
+    iota("otab", T.otab[:], [[0, 5], [1, C]], 0, 0, True)
+    parents()
     fill("neg2", T.neg2[:], -2.0)
-    lin("a", "xs", "a8", 1.0, -1.0)
-    lin("a", "xb", "a8", 1199.0, -1199.0)
-    lin("a", "yb", "e9", 1.0, 1199.5 / 799.5)
+    fill("oddx_", T.oddx[:, C + 1:C + 2], 0.0)
+    lin("a", "xs", "a8", 799.0, -799.0)
+    lin("a", "xb", "a8", -400.5, 0.5)
+    lin("a", "yb", "e9", 1.0, -1.5)
     lin("a", "js", "a8", 1538.0, 0.0)
-    scan("hh inc", "uu", T.uu[:], T.hh[:], T.inc[:], 0.0, mx, sub)
+    lin("a", "jb", "e9", -1538.0, -2.0)
+    lin("a", "ca0", "hi", -4096.0, 2048.0)
+    lin("a", "ca1", "hi", 2048.0, -2048.0 - OFF)
+    ac("a8", "rp_", T.rp[:, 0:1], cor("a8"), -1.0, -399.0)
+    ac("ones ca0", "c48a", T.c48[:, 0:48:2], T.ones[:, 0:24], cor("ca0"))
+    ac("ones ca1", "c48b", T.c48[:, 1:48:2], T.ones[:, 0:24], cor("ca1"))
+    down(0, T.inc, "inc", sub)
     signs(True)
+    down(1, T.inc, "inc", sub)
     signs(False)
     turn()
-    fill("pp_", T.pp[:, 0:1], 20.0)
-    parity()
+    parity(True)
     join(add)
-    ts("ones hi", "c48a", T.c48[:, 0:48:2], T.ones[:, 0:24], cor("hi"), mul, -4096.0, mul)
-    ts("ones hi", "c48b", T.c48[:, 1:48:2], T.ones[:, 0:24], cor("hi"), mul, 2048.0, mul)
-    ts("i2 h17", "lid0", sm("lid0", 0, 26), T.i2[:], cor("h17"), sub, 1.0, add)
-    ts("c48a", "c48a", T.c48[:, 0:48:2], T.c48[:, 0:48:2], 2048.0, add)
-    ts("c48b", "c48b", T.c48[:, 1:48:2], T.c48[:, 1:48:2], -2048.0 - OFF, add)
-    cp("i1", "j16", cor("j16"), T.i1[:, 0:1])
-    ends()
+    parity(False)
+    fill("pp_", T.pp[:, C:C + 1], 20.0)
+    fill("pb_", T.pb[:, C:C + 1], -20.0)
+    ts("end", "lendo", li("lendo", 0, 12), sm("end", 12, 24), -float(A), add)
     pe, po = pick(7, 0)
-    ts("lid0 j16", "lid", li("lid", 0, 26), sm("lid0", 0, 26), cor("j16"), add, C - 1.0, mn)
-    ts("e9 a8", "jb", cor("jb"), cor("e9"), -1538.0, mul, -2.0, add)
-    fill("y32_", T.y32[:, 0:1], -1200.0)
-    kinds()
+    ts("i2 h17", "lid0", sm("lid0", 0, 26), T.i2[:], cor("h17"), sub, 1.0, add)
+    cp("i1", "j16", cor("j16"), T.i1[:, 0:1])
+    ends(False)
+    ends(True)
     ts("pk0", "de", sm("d", 0, 24, 2), pe, -1.0, mul, -OFF - 1.0, add)
     ts("pk0", "do", sm("d", 1, 24, 2), po, -1.0, mul, -OFF - 1.0, add)
-    tt("n tz", "b", sm("b"), sm("n"), T.tz[:, 36:60], sub)
+    ts("lid0 j16", "lid", li("lid", 0, 26), sm("lid0", 0, 26), cor("j16"), add, C - 1.0, mn)
+    kind(False)
+    kind(True)
     cp("de do", "ld", li("ld"), sm("d"))
+    kinds()
+    role(False)
+    role(True)
     tt("tk lsz krow", "kc", T.kc[:], ind("tk", CW, "lsz", 25), T.krow[:], mn)
+    tt("n tz", "b", sm("b"), sm("n"), T.tz[:, 36:60], sub)
     ts("de do", "d2", sm("d2"), sm("d"), 2.0, mul)
-    ts("b", "s1", sm("s1"), sm("b"), 1.0, op_.is_gt, 775.0, mul)
-    ts("b", "s0", sm("s0"), sm("b"), 1.0, op_.is_equal, 771.0, mul)
-    tt("d2 s1", "t10", sm("t10"), sm("d2"), sm("s1"), mx)
-    tt("d2 s0", "t11", sm("t11"), sm("d2"), sm("s0"), mx)
 
     def statics(k):
         if k == 0:
-            cp("t10", "lca", li("lca"), sm("t10"))
-            cp("t11", "ldw", li("ldw"), sm("t11"))
+            ts("b", "s1", sm("s1"), sm("b"), 1.0, op_.is_gt, 775.0, mul)
+            ts("b", "s0", sm("s0"), sm("b"), 1.0, op_.is_equal, 771.0, mul)
+            ts("c16m", "c16a", T.c16[:, 16:32], T.c16[:, 48:64], -B, mul)
+            ts("i3", "c16b", T.c16[:, 32:48], T.i3[:, 0:16], 15.0, op_.is_equal, 2.0 * B, mul)
             ac("iot ld", "nd1", T.nd1[:], ind("iot", CW, "ld"), -1.0, -399.0)
             ac("iot", "yy", T.yy[:], T.iot[:, 0:C], -1.0 / 2048, 400.0)
         if k == 1:
-            ts("c16m", "c16a", T.c16[:, 16:32], T.c16[:, 48:64], -B, mul)
-            ts("i3", "c16b", T.c16[:, 32:48], T.i3[:, 0:16], 15.0, op_.is_equal, 2.0 * B, mul)
+            tt("d2 s1", "t10", sm("t10"), sm("d2"), sm("s1"), mx)
+            tt("d2 s0", "t11", sm("t11"), sm("d2"), sm("s0"), mx)
             cp("i1", "lp16", li("lp16"), T.i1[:])
             tt("c16a c16b", "c16", T.c16[:, 0:16], T.c16[:, 16:32], T.c16[:, 32:48], add)
+        if k == 6:
+            cp("t10", "lca", li("lca"), sm("t10"))
+            cp("t11", "ldw", li("ldw"), sm("t11"))
         if k == 2:
             tt("iot ld yy", "vv", T.vv[:], ind("iot", CW, "ld"), T.yy[:], add)
             ac("nd1", "dw0", T.dw[:, S1:W], T.nd1[:], -1.0, -399.0)
@@ -367,27 +414,29 @@ def rank_program(g, core, T, topo):
         if k == 4:
             lin("v", "k0", "z0", -2.0 * B, B)
             lin("v", "kp_", "z0", -2.0 * B, B - BIG - 1.0)
+            lin("v", "kl", "z0", -2.0 * B, B + P)
             fill("rd_", T.rd[:, 0:1], BIG)
-            fill("oddx_", T.oddx[:, 0:1], 1.0)
             fill("go_", T.go[:, A:4 * 208:208], 0.0)
             for b in range(4):
                 quant("et", "qe%d" % b, T.qe[:, 128 * b:128 * b + 128], T.se[:, 128 * b:128 * b + 128], T.et[:, 3 - b:515 - b])
         if k == 5:
-            cp("iot", "id16", T.id16[:], T.iot[:, 16:CW])
+            cp("iot", "id16", T.id16[:], T.iot[:, 0:C])
 
     def unpack(t):
         for b in range(4):
             mm("qe%d ac%d" % (b, t), "pd%d" % b, T.pd[:, 512 * b:512 * b + C], T.qe[:, 128 * b:128 * b + 128], T.se[:, 128 * b:128 * b + 128],
                T["ql%d" % t][:], T["sl%d" % t][:])
         for b in range(4):
-            ac("pd%d" % b, "yp%d" % b, T.yp[:, P * b + 16:P * b + P], T.pd[:, 512 * b:512 * b + C])
+            ac("pd%d" % b, "yp%d" % b + (" yp" if b in (0, 3) else ""), T.yp[:, P + C * b:P + C * b + C], T.pd[:, 512 * b:512 * b + C])
+        dmas("s", "dupy", "yp yp0 yp1 yp2 yp3", "ypa", [(T.yp[:, 0:P], T.yp[:, P:2 * P])])
 
-    def planes(t, bs):
-        for b in bs:
-            if t:
-                ac("xpo%d xpr%d" % (b, b), "xq%d" % b, T.xq[:, P * b + 16:P * b + P], T.xp[:, C * b:C * b + C], 0.0078125)
-            else:
-                ac("x0", "xq%d" % b, T.xq[:, P * b + 16:P * b + P], T.x0[:, b:4 * C:4])
+    def planes(t):
+        if t:
+            ac(" ".join("xp%s%d" % (h, b) for h in "or" for b in range(4)), "xq", T.xq[:, P:2 * P], T.xp[:], 0.0078125)
+        else:
+            for b in range(4):
+                ac("x0", "xq%d xq" % b if b == 3 else "xq%d" % b, T.xq[:, P + C * b:P + C * b + C], T.x0[:, b:4 * C:4])
+        dmas("s", "dupx", "xq xq0 xq1 xq2 xq3", "xqa", [(T.xq[:, 0:P], T.xq[:, P:2 * P])])
 
     for t in range(NR):
         lst, ll = T["lst%d" % t], T["ll%d" % t]
@@ -397,21 +446,29 @@ def rank_program(g, core, T, topo):
                 statics(k)
 
         if t:
-            parity()
-            ends()
+            parity(False)
+            ends(False)
+            kind(False)
             kinds()
-        scan("xg kc", "nv", T.nv[:], T.xg[:], T.kc[:], 0.0, mx, sub)
+            role(False)
+        tt("rpo rpr rp_ lpx kc", "nv", T.nv[:], ind("rp", C + 1, "lpx", 25), T.kc[:], sub)
         once(0)
         scan("keep1 nv", "pa", T.pa[:, 1:CW + 1], T.keep1[:], T.nv[:], 0.0, mul, mn)
         once(1)
-        tt("pa pa0 lpr keepb", "hh", T.hh[:], ind("pa", CW + 1, "lpr", 25), T.keepb[:], add)
         scan("dj nv", "nv2", T.nv2[:], T.dj[:], T.nv[:], 0.0, mx, add)
-        scan("hh nv2", "uu", T.uu[:], T.hh[:], T.nv2[:], 0.0, mx, mn)
+        parents()
+        once(6)
+        down(0, T.nv2, "nv2", mn)
+        evens(1)
+        down(1, T.nv2, "nv2", mn)
         ac("nd1", "bt", T.bt[:, S0:S1:2], T.nd1[:], -1.0)
+        if t:
+            planes(t)
         once(2)
         turn()
         once(3)
         join(mn)
+        evens(0)
         pe, po = pick(9, 0)
         qe_, qo = pick(8, 1)
         ts("pk0", "l1e", li("l1", 0, 24, 2), pe, -1.0, mul)
@@ -420,55 +477,59 @@ def rank_program(g, core, T, topo):
         ts("pk1", "l2o", li("l2", 1, 24, 2), qo, -1.0, mul)
         cp("vv l1e l1o", "bt", ind("bt", W, "l1"), T.vv[:])
         ac("dw0 dw1 dw2 l2e l2o", "dwg", T.dwg[:], ind("dw", W, "l2"), 1.0, 400.0)
-        planes(t, range(2))
+        if t == 0:
+            planes(t)
         once(4)
-        tt("bt lsib ca", "aw aw_", T.aw[:, S0 + 1:S1:2], ind("bt", W, "lsib"), T.ca[:], add)
         ac("bt lnm", "ma", T.ma[:], ind("bt", W, "lnm"), 1.0, -784.0)
         scan("dwg v2", "nr", T.nr[:], T.dwg[:], T.v2[:], 0.0, mx, sub)
-        tt("aw aw_ l1e l1o nd1", "yy", T.yy[:], ind("aw", W, "l1"), T.nd1[:], mx)
+        tt("bt lsib ca", "aw aw_", T.aw[:, S0 + 1:S1:2], ind("bt", W, "lsib"), T.ca[:], add)
         ac("nr", "s3", T.s3[:], T.nr[:], 1.0, 400.0, act.Sign)
         ac("s3", "c3", T.c3[:], T.s3[:], 2.5, -1.0, act.Abs)
         ac("nr", "mb", T.mb[:], T.nr[:], 1.0, 399.0, act.Abs)
         s = conv("ma", T.ma[:])
-        scan("bt yy", "rd", T.rd[:, 1:C + 1], T.bt[:, S0:S1:2], T.yy[:], BIG, add, add)
+        tt("aw aw_ l1e l1o nd1", "yy", T.yy[:], ind("aw", W, "l1"), T.nd1[:], mx)
         ts("sc k0", "wi", T.wi[:], s, cor("k0"), add, -2048.0, mul)
-        ac("rd rd_", "base0", T.base[:, S0:S1:2], T.rd[:, 0:C])
         scan("rb c3", "ub", T.ub[:], T.rb[:], T.c3[:], 0.0, mx, sub)
         ts("wi", "oi", T.oi[:], T.wi[:], 2047, op_.bitwise_and)
-        ac("ub", "sig", T.sig[:], T.ub[:], -1.0, -1.25, act.Sign)
-        planes(t, range(2, 4))
-        unpack(t)
-        scan("rd oddx oddx_ ones", "base1", T.base[:, S1:W], T.ones[:, 0:C], T.oddx[:, 0:C], T.rd[:, C:C + 1], add, sub)
+        scan("bt yy", "rd", T.rd[:, 1:C + 1], T.bt[:, S0:S1:2], T.yy[:], BIG, add, add)
         cp("oi", "lb", li("lb"), T.oi[:])
+        ac("ub", "s3", T.s3[:], T.ub[:], -1.0, -1.25, act.Sign)
+        ac("rd rd_", "base0", T.base[:, S0:S1:2], T.rd[:, 0:C])
+        ac("s3", "sig", T.sig[:], T.s3[:], P / 2.0, P / 2.0)
+        unpack(t)
         once(5)
         tt("rd rd_ lb ma", "base2", T.base[:, S0 + 1:S1:2], ind("rd", C + 1, "lb"), T.ma[:], add)
-        scan("id16 sig", "val", T.val[:], T.id16[:], T.sig[:], 0.0, mx, mul)
-        tt("base0 base1 base2 l2e l2o mb", "m0", T.m0[:], ind("base", W, "l2"), T.mb[:], add)
-        s = conv("m0", T.m0[:], BIG + 2.0 * B)
-        ts("sc kp_", "lpos", li("lpos"), s, cor("kp_"), add)
-        cp("val lpos", "orow", ind("orow", C, "lpos"), T.val[:])
+        scan("id16 sig", "val", T.val[:], T.id16[:], T.sig[:], 0.0, mx, sub)
+        for h in range(2):
+            tt("base0 base10 base11 base2 l2e l2o mb", "m0%d" % h, T.m0[:, A * h:A * h + A], T.base[:, 0:W].indirect(li("l2", 12 * h, 12 * h + 12)),
+               T.mb[:, A * h:A * h + A], add)
+        for h in range(2):
+            half("m0%d" % h, T.m0, h, BIG + 2.0 * B)
+        for h in range(2):
+            ts("sc%d kp_" % h, "lpos%d" % h, li("lpos", 12 * h, 12 * h + 12), T.sc[:, A * h + 15:A * h + A:16], cor("kp_"), add)
+        cp("val lpos0 lpos1", "orow", ind("orow", C, "lpos"), T.val[:])
         s = conv("orow", T.orow[:])
-        ac("sc k0", "lof", sm("lof"), s, 1.0, cor("k0"), act.Abs)
-        ts("sc k0", "lstf%d" % t, lst[:, 24:48], s, cor("k0"), add)
-        cp("lof", "lsto%d" % t, lst[:, 0:24], sm("lof"))
+        ts("sc kl", "lst%d" % t, lst[:, 0:24], s, cor("kl"), add)
         send(t, "lists")
 
         qn, sn = T["qx%d" % (t + 1)], T["sx%d" % (t + 1)]
 
         def gath(b, own):
-            call = ac if b else cp
+            call = cp if own and b == 0 else ac
+            a = P + C * b
             if own:
-                call("xq%d xq_%d lstf%d" % (b, b, t), "go%d" % b, T.go[:, 208 * b:208 * b + A], T.xq[:, P * b:P * b + P].indirect(lst[:, 36:48]))
+                call("xq xq_ lst%d" % t, "go%d" % b, T.go[:, 208 * b:208 * b + A], T.xq[:, a:a + P + C].indirect(lst[:, 12:24]))
             else:
-                call("yp%d yp_%d al%d" % (b, b, t), "gr%d" % b, T.gr[:, 208 * b:208 * b + 208], T.yp[:, P * b:P * b + P].indirect(ll[:, 24:37]))
+                call("yp yp_ al%d" % t, "gr%d" % b, T.gr[:, 208 * b:208 * b + 208], T.yp[:, a:a + P + C].indirect(ll[:, 0:13]))
 
         def diff(b, own):
+            a = C * b
             if own:
-                tt("xq%d xq_%d go%d go_ lsto%d" % (b, b, b, t), "zo%d" % b, T.zt[:, 4 * A + b:4 * C:4],
-                   T.xq[:, P * b:P * b + P].indirect(lst[:, 12:24]), T.go[:, 208 * b + 1:208 * b + 1 + A], sub)
+                tt("xq xqa go%d go_ lst%d" % (b, t), "zo%d" % b, T.zt[:, 4 * A + b:4 * C:4],
+                   T.xq[:, a:a + P + C].indirect(lst[:, 12:24]), T.go[:, 208 * b + 1:208 * b + 1 + A], sub)
             else:
-                tt("yp%d yp_%d gr%d al%d" % (b, b, b, t), "zr%d" % b, T.zt[:, b:4 * A:4],
-                   T.yp[:, P * b:P * b + P].indirect(ll[:, 0:12]), T.gr[:, 208 * b + 1:208 * b + 1 + A], sub)
+                tt("yp ypa gr%d al%d" % (b, t), "zr%d" % b, T.zt[:, b:4 * A:4],
+                   T.yp[:, a:a + P + C].indirect(ll[:, 0:12]), T.gr[:, 208 * b + 1:208 * b + 1 + A], sub)
 
         def big(b, own):
             h, c0 = ("o", A) if own else ("r", 0)
@@ -513,36 +574,40 @@ def rank_program(g, core, T, topo):
         for b in range(4):
             big(b, True)
         if t == NR - 1:
-            ac("iot lsto%d" % t, "otr", T.otr[:], T.iot[:, 0:CW].indirect(lst[:, 0:24]), 1.0, -16.0)
+            ac("otab lst%d" % t, "otr", T.otr[:], T.otab[:].indirect(lst[:, 0:24]))
             dmas("s", "out", "otr", "", [(T.ot[k:k + 1, :], T.otr[16 * k:16 * k + 1, :]) for k in range(8)])
         product(True)
         if t == NR - 1:
             quant("vt", "qv", T.qv[:], T.sv[:], T.vt[:])
         for b in range(4):
-            state(b, True)
-        for b in range(3):
-            tile(b, True)
-        for b in range(4):
             gath(b, False)
         for b in range(4):
+            state(b, True)
+        for b in range(4):
+            tile(b, True)
+        for b in range(4):
             diff(b, False)
-        big(0, False)
-        tile(3, True)
-        for b in range(1, 4):
+        for b in range(4):
             big(b, False)
-        product(False)
         pack(True)
         if t == NR - 1:
             outputs(True)
         else:
             score(t + 1, True)
-        for b in range(4):
+        product(False)
+        if t < NR - 1:
+            signs(True)
+            state(0, False)
+            parity(True)
+        else:
+            result(True)
+            state(0, False)
+        tile(0, False)
+        for b in range(1, 4):
             state(b, False)
             tile(b, False)
         if t < NR - 1:
-            signs(True)
-        else:
-            result(True)
+            ends(True)
         pack(False)
         if t == NR - 1:
             outputs(False)
@@ -550,7 +615,9 @@ def rank_program(g, core, T, topo):
         else:
             score(t + 1, False)
             send(t + 1, "codes")
+            role(True)
             signs(False)
+            kind(True)
 
     for sem in [k for k in count if k != "out"] + ["out"]:
         if max(known[e].get(sem, 0) for e in eng) < count[sem]:

@@ -21,15 +21,15 @@ def _sb(dtype, **kw):
         SCRATCH[k] = ("sbuf", [128, kw[k]], dtype)
 
 
-_sb(H, x0=4 * C, xt=4 * C, xp=4 * C, xq=3 * P, yp=3 * P, zt=4 * C, z128=4 * C, ut=512, vt=512, et=528,
+_sb(H, x0=P, xt=P, xp=P, xq=3 * P, yp=3 * P, zt=P, z128=P, ut=512, vt=512, et=528,
     sg=C, pp=C + 16, pb=C + 16, eb=C, oddx=C + 16, neg2=A, ones=528, go=4 * 208, gr=4 * 208, yq=C, rb=C, yk=C, dy=C, dj=CW,
-    iotb=CW, nl=CW, nh=CW, tk=CW, ti=CW, szr=CW + 16, szp=CW, keep1=CW, keepb=CW, inc=CW, kp=A, s3=C, c3=C, ub=C, sig=C)
+    iotb=CW, nl=CW, nh=CW, tk=CW, szr=CW + 16, szp=CW, keep1=CW, keepb=CW, inc=CW, kp=A, s3=C, c3=C, ub=C, sig=C)
 _sb(G, kc=CW, nv=CW, nv2=CW, hh=CW, uu=CW, tr=2 * C, seg=2 * C, id16=C, val=C)
 _sb(Q, qu=128, qur=128, qv=128, qe=512, qw=512, qz=C, qx0=C, qx1=C, qx2=C, qx3=C, ql0=C, ql1=C, ql2=C)
 _sb(S, su=128, sur=128, sv=128, se=512, sw=512, szz=C, sx0=C, sx1=C, sx2=C, sx3=C, sl0=C, sl1=C, sl2=C)
 _sb(I, tz=64, i1=24, i2=26, i3=24, wi=24, oi=24)
 _sb(U, ls=26 * 20, lu=8, lst0=24, lst1=24, lst2=24, ll0=16, ll1=16, ll2=16)
-_sb(F, iot=776, sm=64 * 24, c16=64, c48=48, pk=96, pws=64, cor=32, cv1=C, krow=CW, pa=CW + 8, rp=C + 8, dx=C,
+_sb(F, iot=776, sm=64 * 24, c16=64, c48=48, pk=96, pws=64, cor=40, cv1=C, krow=CW, pa=CW + 8, rp=C + 8, dx=C,
     rd=392, sc=C, nd1=C, vv=C, v2=C, ca=C, dw=W, aw=W, bt=W, base=W, dwg=C,
     m0=C, ma=C, mb=C, nr=C, yy=C, orow=C, otr=C, yo=C, otab=P + C)
 SCRATCH["pd"] = ("psum", [128, 2048], F)
@@ -153,127 +153,53 @@ def rank_program(g, core, T, topo):
             cslot[name] = len(cslot)
         return T.cor[:, cslot[name]:cslot[name] + 1]
 
-    def ind(buf, n, lst, k=24):
-        return T[buf][:, 0:n].indirect(li(lst, 0, k))
+    def ind(buf, n, lst, k=24, a=0):
+        return T[buf][:, 0:n].indirect(li(lst, a, a + k))
 
     add, sub, mul, mx, mn = op_.add, op_.subtract, op_.mult, op_.max, op_.min
 
-    def lin(e, name, src, m, c):
-        if e == "v":
-            ts(src, name, cor(name), cor(src), m, mul, c, add)
-        else:
-            ac(src, name, cor(name), cor(src), m, c)
+    def lin(name, src, m, c):
+        names = [k for k in (m, c) if isinstance(k, str)]
+        ac(" ".join([src] + names), name, cor(name), cor(src), cor(m) if m in names else m, cor(c) if c in names else c)
 
     def conv(r, src, init=2.0 * B):
         scan(r + " cv1", "sc sc0 sc1", T.sc[:], src, T.cv1[:], init, mn, add)
         return T.sc[:, 15:C:16]
 
     def half(r, src, h, init=2.0 * B):
-        scan(r + " cv1", "sc sc%d" % h if h == 0 else "sc1", T.sc[:, A * h:A * h + A], src[:, A * h:A * h + A], T.cv1[:, 0:A], init, mn, add)
+        scan(r + " cv1", "sc1" if h else "sc sc0", T.sc[:, A * h:A * h + A], src[:, A * h:A * h + A], T.cv1[:, 0:A], init, mn, add)
 
     cut = [0, A + 16, CW]
 
-    def parents():
-        for h in range(2):
-            tt("pa pa0 lpr lpr2 keepb", "hh%d" % h, T.hh[:, cut[h]:cut[h + 1]],
-               T.pa[:, 0:CW + 1].indirect(li("lpr2", 0, 12) if h else li("lpr", 0, 13)), T.keepb[:, cut[h]:cut[h + 1]], add)
+    def along(row, r, o):
+        scan("keep1 " + r, "pa", T.pa[:, 1:CW + 1], T.keep1[:], row[:], 0.0, mul, o)
+
+    def parents(h):
+        tt("pa pa0 lpr lpr2 keepb", "hh%d" % h, T.hh[:, cut[h]:cut[h + 1]],
+           ind("pa", CW + 1, "lpr2", 12) if h else ind("pa", CW + 1, "lpr", 13), T.keepb[:, cut[h]:cut[h + 1]], add)
 
     def down(h, row, r, o):
         a, b = cut[h], cut[h + 1]
         scan("hh%d uu0 %s" % (h, r), "uu%d" % h, T.uu[:, a:b], T.hh[:, a:b], row[:, a:b], T.uu[:, a - 1:a] if h else 0.0, mx, o)
 
-    def turn():
-        for h in range(2):
-            for k in range(2):
-                run("v", "uu0 uu%d" % h, "tr%d%d" % (h, k),
-                    lambda: V.transpose(T.tr[:, C * k + A * h:C * k + A * h + A], T.uu[:, 16 * k + A * h:16 * k + A * h + A]))
+    def turn(h):
+        for k in range(2):
+            run("v", "uu0 uu%d" % h, "tr%d%d" % (h, k),
+                lambda: V.transpose(T.tr[:, C * k + A * h:C * k + A * h + A], T.uu[:, 16 * k + A * h:16 * k + A * h + A]))
 
-    def join(o):
-        for h in range(2):
-            for k in range(2):
-                a = C * k + A * h
-                scan("kp tr%d%d" % (h, k), "seg%d%d" % (h, k), T.seg[:, a:a + A], T.kp[:], T.tr[:, a:a + A], 0.0, mul, o)
-
-    def evens(h):
-        back = slice(S1 + A * h + A - 1, S1 + A * h - 1, -1)
-        scan("oddx oddx_ ones base11", "base1%d" % h, T.base[:, back], T.oddx[:, A * h + A + 1:A * h + 1:-1], T.ones[:, 0:A],
-             BIG + C if h else T.base[:, S1 + A:S1 + A + 1], add, sub)
+    def join(h, o):
+        for k in range(2):
+            a = C * k + A * h
+            scan("kp tr%d%d" % (h, k), "seg%d%d" % (h, k), T.seg[:, a:a + A], T.kp[:], T.tr[:, a:a + A], 0.0, mul, o)
 
     def pick(j, k):
         scan("seg00 seg01 seg10 seg11 c48a c48b", "pk%d" % k, T.pk[:, 48 * k:48 * k + 48], T.seg[:, j:2 * C:16], T.c48[:], -4096.0, mx, add)
         return T.pk[:, 48 * k + 1:48 * k + 24:2], T.pk[:, 48 * k + 25:48 * k + 48:2]
 
-    dmas("a", "ltree", "", "tz", [(T.tz[:, 4:28], T.sz[:]), (T.tz[:, 36:60], T.pr[:])])
-    dmas("s", "lx", "", "x0", [(T.x0[:], T.x[:])])
-    dmas("a", "lu_", "", "ut", [(T.ut[:], T.u[:])])
-    dmas("s", "lw", "x0", "qw", [(T.qw[:].bitcast(dt.uint8), T.wc[:]), (T.sw[:], T.ws[:])])
-    dmas("s", "lv", "", "vt", [(T.vt[:], T.v[:])])
-
-    iota("i1", T.i1[:], [[0, 24]], 0, 1, False)
-    iota("i3", T.i3[:, 0:16], [[1, 16]], 128, -1, False)
-    iota("iotb", T.iotb[:], [[1, CW]], 0, 0, True)
-    iota("i2", T.i2[:], [[16, 26]], 0, 0, False)
-    iota("iot", T.iot[:, 0:CW], [[1, CW]], 0, 0, True)
-    fill("pw", T.pws[:, 48:64], 2.0)
-    fill("ones", T.ones[:], 1.0)
-    run("g", "ones", "kp", lambda: g.affine_select(T.kp[:], T.ones[:, 0:A], [[0, 12], [1, 16]], op_.is_gt, 0.0, 0, 0))
-    iota("iot2", T.iot[:, CW:776], [[1, 776 - CW]], CW, 0, True)
-    run("g", "ones", "et", lambda: g.affine_select(T.et[:], T.ones[:, 0:528], [[1, 528]], op_.is_equal, 0.0, -3, -4))
-    iota("bt", T.bt[:, S0:S1 + 8], [[0, S1 + 8 - S0]], 0, 0, True)
-
-    scan("pw", "pw2", T.pws[:, 0:16], T.pws[:, 48:64], T.pws[:, 48:64], 1.0, mul, mx)
-    fill("tz0", T.tz[:, 0:4], 0)
-    fill("tz1", T.tz[:, 28:32], 0)
-    fill("tz3", T.tz[:, 32:36], -1)
-    fill("tz2", T.tz[:, 60:64], 0)
-    ts("i1", "ih", T.i3[:, 16:17], T.i1[:, 0:1], 4, op_.arith_shift_right, 1, op_.bitwise_and)
-    ts("i3", "i3", T.i3[:, 0:16], T.i3[:, 0:16], 15, op_.bitwise_and)
-    ts("i1 ih", "i1", T.i1[:], T.i1[:], 15, op_.bitwise_and)
-    cp("ih", "hi", cor("hi"), T.i3[:, 16:17])
-    ts("i3", "c16m", T.c16[:, 48:64], T.i3[:, 0:16], 0.0, op_.is_equal)
-    ts("i1", "z0", cor("z0"), T.i1[:, 0:1], 0.0, op_.is_equal)
-    ts("i1", "a8", cor("a8"), T.i1[:, 0:1], 8.0, op_.is_ge)
-    tt("c16m pw2", "pw3", T.pws[:, 16:32], T.c16[:, 48:64], T.pws[:, 0:16], mul)
-    lin("v", "lo", "hi", -1.0, 1.0)
-    ts("i1", "e9", cor("e9"), T.i1[:, 0:1], 9.0, op_.is_equal)
-    scan("pw3", "thr", T.pws[:, 32:48], T.pws[:, 16:32], T.pws[:, 16:32], 0.0, add, mx)
-    thr = T.pws[:, 47:48]
-    lin("v", "h17", "hi", 16.0, 1.0)
-    lin("a", "tkb", "a8", 4096.0, 400.0 - 4096.0)
-    lin("a", "ks", "a8", -1.0, 2.0)
-    lin("v", "k1", "a8", 2.0 * C - 1.0, KEY + 1.0 - 400.0)
-    ts("thr", "th2", cor("th2"), thr, 2.0, mul)
-    tt("thr z0", "thl", cor("thl"), thr, cor("z0"), sub)
-    ts("hi ks", "k2", cor("k2"), cor("hi"), -16.0, mul, cor("ks"), mul)
-    ts("iotb th2", "nh", T.nh[:], T.iotb[:], cor("th2"), op_.is_lt, -2.0, add)
-    ts("iotb thl", "nl", T.nl[:], T.iotb[:], cor("thl"), op_.is_ge, 1.0, add)
-    tt("k1 k2", "kr", cor("kr"), cor("k1"), cor("k2"), add)
-    ac("nl tkb", "tk", T.tk[:], T.nl[:], 4096.0, cor("tkb"))
-    scan("nl nh", "ti", T.ti[:], T.nl[:], T.nh[:], 0.0, mx, add)
-
-    ts("tz tz1 tz2 tz3 lo", "za", sm("za", 0, 58), T.tz[:, 4:62], cor("lo"), mul)
-    ts("tz tz0 tz1 tz2 tz3 hi", "zb", sm("zb", 0, 58), T.tz[:, 3:61], cor("hi"), mul)
-    tt("i1 i2", "n", sm("n"), T.i1[:], T.i2[:, 0:24], add)
-    tt("za zb", "zc", sm("zc", 0, 58), sm("za", 0, 58), sm("zb", 0, 58), add)
-    fill("szr_", T.szr[:, 0:1], 0.0)
-    cp("zc", "lsz", li("lsz", 0, 26), sm("zc", 0, 26))
-    ts("zc h17", "lpr", li("lpr", 0, 26), sm("zc", 32, 58), cor("h17"), add)
-    ac("iotb lsz", "szr", T.szr[:, 1:CW + 1], ind("iotb", CW, "lsz", 25))
-    ac("szr szr_ lpr", "szp", T.szp[:], ind("szr", CW + 1, "lpr", 25))
-    ac("iot ks kr", "krow", T.krow[:], T.iot[:, 0:CW], cor("ks"), cor("kr"))
-    tt("tz n", "end", sm("end"), T.tz[:, 4:28], sm("n"), add)
-    cp("ti lsz", "inc", T.inc[:], ind("ti", CW, "lsz", 25))
-    lin("v", "kb", "a8", 6144.0, -2048.0)
-    cp("i2", "lu", T.lu[:], T.i2[:, 0:8])
-    quant("ut", "qu", T.qu[:], T.su[:], T.ut[:])
-    cp("end", "lend", li("lend"), sm("end"))
-    ts("zc", "lpx", li("lpx", 0, 26), sm("zc", 32, 58), 1.0, add)
-    ts("zc h17", "lpr2", li("lpr2", 0, 12), sm("zc", 45, 57), cor("h17"), add)
-    cp("qu lu", "qur", T.qur[:].bitcast(dt.uint32), T.qu[:].bitcast(dt.uint32).indirect(T.lu[:]))
-    run("a", "qu lu", "sur", lambda: g.scalar.activation(T.sur[:], T.su[:].indirect(T.lu[:]), act.Copy))
-    fill("pa0", T.pa[:, 0:1], 0.0)
-    ts("szp th2", "keep1", T.keep1[:], T.szp[:], cor("th2"), op_.is_lt)
-    ts("szp thr kb", "keepb", T.keepb[:], T.szp[:], thr, op_.is_lt, cor("kb"), mul)
+    def evens(h):
+        back = slice(S1 + A * h + A - 1, S1 + A * h - 1, -1)
+        scan("oddx oddx_ ones base11", "base1%d" % h, T.base[:, back], T.oddx[:, A * h + A + 1:A * h + 1:-1], T.ones[:, 0:A],
+             BIG + C if h else T.base[:, S1 + A:S1 + A + 1], add, sub)
 
     def send(t, what):
         dst = T.cores[(rank + STEP[t]) % n_ranks]
@@ -308,119 +234,30 @@ def rank_program(g, core, T, topo):
     def parity(own):
         h, c0 = ("o", A) if own else ("r", 0)
         back = slice(c0 + A - 1, c0 - 1 if c0 else None, -1)
-        scan("neg2 ppo sg" + h, "pp" + h, T.pp[:, back], T.sg[:, back], T.neg2[:, 0:A], 20.0 if own else T.pp[:, A:A + 1], mul, mul)
+        scan("neg2 ppo sg" + h, "pp" + h, T.pp[:, back], T.sg[:, back], T.neg2[:], 20.0 if own else T.pp[:, A:A + 1], mul, mul)
         ac("xs xb sg" + h, "dx" + h, T.dx[:, c0:c0 + A], T.sg[:, c0:c0 + A], cor("xs"), cor("xb"))
-        scan("neg2 pbo sg" + h, "pb" + h, T.pb[:, back], T.sg[:, back], T.neg2[:, 0:A], -20.0 if own else T.pb[:, A:A + 1], mul, mul)
+        scan("neg2 pbo sg" + h, "pb" + h, T.pb[:, back], T.sg[:, back], T.neg2[:], -20.0 if own else T.pb[:, A:A + 1], mul, mul)
         ac("sg" + h, "dy" + h, T.dy[:, c0:c0 + A], T.sg[:, c0:c0 + A], -800.0, -1200.0)
 
-    def ends(own):
-        if own:
+    def ends(q):
+        if q == "o":
             tt("ppo pp_ pbo pb_ lendo", "ebo", T.eb[:, A:C], T.pp[:, A:C + 1].indirect(li("lendo", 0, 12)), T.pb[:, A + 1:C + 1], mul)
         else:
-            tt("ppo ppr pp_ pbo pbr lend", "ebr", T.eb[:, 0:A], ind("pp", C + 1, "lend", 12), T.pb[:, 1:A + 1], mul)
+            a = 96 * q
+            tt("ppo ppr pp_ pbo pbr lend", "eb%d" % q, T.eb[:, a:a + 96], ind("pp", C + 1, "lend", 6, 6 * q), T.pb[:, a + 1:a + 97], mul)
 
-    def role(own):
-        h, c0 = ("o", A) if own else ("r", 0)
-        tt("eb%s dx%s" % (h, h), "rp" + h, T.rp[:, 1 + c0:1 + c0 + A], T.eb[:, c0:c0 + A], T.dx[:, c0:c0 + A], mn)
+    def role(q):
+        a = 96 * q
+        tt("ebo dxo" if q > 1 else "eb%d dxr" % q, "rp%d" % q, T.rp[:, 1 + a:97 + a], T.eb[:, a:a + 96], T.dx[:, a:a + 96], mn)
 
     def kind(own):
-        h, c0 = ("o", A) if own else ("r", 0)
-        scan("eb%s dy%s" % (h, h), "yk" + h, T.yk[:, c0:c0 + A], T.eb[:, c0:c0 + A], T.dy[:, c0:c0 + A], -4096.0, mx, add)
+        h, c0, e = ("o", A, "ebo") if own else ("r", 0, "eb0 eb1")
+        scan("%s dy%s" % (e, h), "yk" + h, T.yk[:, c0:c0 + A], T.eb[:, c0:c0 + A], T.dy[:, c0:c0 + A], -4096.0, mx, add)
         ac("yb yk" + h, "yq" + h, T.yq[:, c0:c0 + A], T.yk[:, c0:c0 + A], -1.0 / 800, cor("yb"), act.Abs)
 
     def kinds():
         ac("yqo yqr lid js jb", "dj", T.dj[:], ind("yq", C, "lid", 25), cor("js"), cor("jb"), act.Relu)
         ac("yko ykr", "oddx", T.oddx[:, 1:C + 1], T.yk[:], -1.0 / 800, -1.5, act.Abs)
-        ac("yko ykr", "rb", T.rb[:], T.yk[:], -1.0 / 800, -1.5, act.Relu)
-
-    scan("keep1 inc", "pa", T.pa[:, 1:CW + 1], T.keep1[:], T.inc[:], 0.0, mul, sub)
-    quant("x0", "qxo0 qxr0", T.qx0[:], T.sx0[:], T.x0[:])
-    score(0, True)
-    score(0, False)
-    send(0, "codes")
-    iota("aw aw_", T.aw[:, S0:W], [[0, W - S0]], -2048, 0, True)
-    iota("xq_", T.xq[:, 2 * P:3 * P], [[0, P]], 0, 0, True)
-    iota("yp_", T.yp[:, 2 * P:3 * P], [[0, P]], 0, 0, True)
-    iota("otab", T.otab[:], [[0, 5], [1, C]], 0, 0, True)
-    parents()
-    fill("neg2", T.neg2[:], -2.0)
-    fill("oddx_", T.oddx[:, C + 1:C + 2], 0.0)
-    lin("a", "xs", "a8", 799.0, -799.0)
-    lin("a", "xb", "a8", -400.5, 0.5)
-    lin("a", "yb", "e9", 1.0, -1.5)
-    lin("a", "js", "a8", 1538.0, 0.0)
-    lin("a", "jb", "e9", -1538.0, -2.0)
-    lin("a", "ca0", "hi", -4096.0, 2048.0)
-    lin("a", "ca1", "hi", 2048.0, -2048.0 - OFF)
-    ac("a8", "rp_", T.rp[:, 0:1], cor("a8"), -1.0, -399.0)
-    ac("ones ca0", "c48a", T.c48[:, 0:48:2], T.ones[:, 0:24], cor("ca0"))
-    ac("ones ca1", "c48b", T.c48[:, 1:48:2], T.ones[:, 0:24], cor("ca1"))
-    down(0, T.inc, "inc", sub)
-    signs(True)
-    down(1, T.inc, "inc", sub)
-    signs(False)
-    turn()
-    parity(True)
-    join(add)
-    parity(False)
-    fill("pp_", T.pp[:, C:C + 1], 20.0)
-    fill("pb_", T.pb[:, C:C + 1], -20.0)
-    ts("end", "lendo", li("lendo", 0, 12), sm("end", 12, 24), -float(A), add)
-    pe, po = pick(7, 0)
-    ts("i2 h17", "lid0", sm("lid0", 0, 26), T.i2[:], cor("h17"), sub, 1.0, add)
-    cp("i1", "j16", cor("j16"), T.i1[:, 0:1])
-    ends(False)
-    ends(True)
-    ts("pk0", "de", sm("d", 0, 24, 2), pe, -1.0, mul, -OFF - 1.0, add)
-    ts("pk0", "do", sm("d", 1, 24, 2), po, -1.0, mul, -OFF - 1.0, add)
-    ts("lid0 j16", "lid", li("lid", 0, 26), sm("lid0", 0, 26), cor("j16"), add, C - 1.0, mn)
-    kind(False)
-    kind(True)
-    cp("de do", "ld", li("ld"), sm("d"))
-    kinds()
-    role(False)
-    role(True)
-    tt("tk lsz krow", "kc", T.kc[:], ind("tk", CW, "lsz", 25), T.krow[:], mn)
-    tt("n tz", "b", sm("b"), sm("n"), T.tz[:, 36:60], sub)
-    ts("de do", "d2", sm("d2"), sm("d"), 2.0, mul)
-
-    def statics(k):
-        if k == 0:
-            ts("b", "s1", sm("s1"), sm("b"), 1.0, op_.is_gt, 775.0, mul)
-            ts("b", "s0", sm("s0"), sm("b"), 1.0, op_.is_equal, 771.0, mul)
-            ts("c16m", "c16a", T.c16[:, 16:32], T.c16[:, 48:64], -B, mul)
-            ts("i3", "c16b", T.c16[:, 32:48], T.i3[:, 0:16], 15.0, op_.is_equal, 2.0 * B, mul)
-            ac("iot ld", "nd1", T.nd1[:], ind("iot", CW, "ld"), -1.0, -399.0)
-            ac("iot", "yy", T.yy[:], T.iot[:, 0:C], -1.0 / 2048, 400.0)
-        if k == 1:
-            tt("d2 s1", "t10", sm("t10"), sm("d2"), sm("s1"), mx)
-            tt("d2 s0", "t11", sm("t11"), sm("d2"), sm("s0"), mx)
-            cp("i1", "lp16", li("lp16"), T.i1[:])
-            tt("c16a c16b", "c16", T.c16[:, 0:16], T.c16[:, 16:32], T.c16[:, 32:48], add)
-        if k == 6:
-            cp("t10", "lca", li("lca"), sm("t10"))
-            cp("t11", "ldw", li("ldw"), sm("t11"))
-        if k == 2:
-            tt("iot ld yy", "vv", T.vv[:], ind("iot", CW, "ld"), T.yy[:], add)
-            ac("nd1", "dw0", T.dw[:, S1:W], T.nd1[:], -1.0, -399.0)
-            ac("nd1", "dw1", T.dw[:, S0:S1:2], T.nd1[:], -1.0, -399.0)
-            ac("iot iot2 ldw", "dw2", T.dw[:, S0 + 1:S1:2], ind("iot", 776, "ldw"), 1.0, -385.0)
-            ac("iot iot2 lca", "ca", T.ca[:], ind("iot", 776, "lca"), -1.0, -797.0)
-        if k == 3:
-            ts("tz", "lnm", li("lnm"), T.tz[:, 36:60], 2.0, mul, float(S0 + 3), add)
-            ts("end", "lsib", li("lsib"), sm("end"), 2.0, mul, float(S0 + 1), add)
-            ac("nd1", "v2", T.v2[:], T.nd1[:], -1.0, 401.0)
-            ac("c16 lp16", "cv1", T.cv1[:], ind("c16", 16, "lp16"))
-        if k == 4:
-            lin("v", "k0", "z0", -2.0 * B, B)
-            lin("v", "kp_", "z0", -2.0 * B, B - BIG - 1.0)
-            lin("v", "kl", "z0", -2.0 * B, B + P)
-            fill("rd_", T.rd[:, 0:1], BIG)
-            fill("go_", T.go[:, A:4 * 208:208], 0.0)
-            for b in range(4):
-                quant("et", "qe%d" % b, T.qe[:, 128 * b:128 * b + 128], T.se[:, 128 * b:128 * b + 128], T.et[:, 3 - b:515 - b])
-        if k == 5:
-            cp("iot", "id16", T.id16[:], T.iot[:, 0:C])
 
     def unpack(t):
         for b in range(4):
@@ -438,6 +275,163 @@ def rank_program(g, core, T, topo):
                 ac("x0", "xq%d xq" % b if b == 3 else "xq%d" % b, T.xq[:, P + C * b:P + C * b + C], T.x0[:, b:4 * C:4])
         dmas("s", "dupx", "xq xq0 xq1 xq2 xq3", "xqa", [(T.xq[:, 0:P], T.xq[:, P:2 * P])])
 
+    dmas("a", "ltree", "", "tz", [(T.tz[:, 4:28], T.sz[:]), (T.tz[:, 36:60], T.pr[:])])
+    dmas("s", "lx", "", "x0", [(T.x0[:], T.x[:])])
+    dmas("a", "lu_", "", "ut", [(T.ut[:], T.u[:])])
+    dmas("s", "lw", "x0", "qw", [(T.qw[:].bitcast(dt.uint8), T.wc[:]), (T.sw[:], T.ws[:])])
+    dmas("s", "lv", "", "vt", [(T.vt[:], T.v[:])])
+
+    iota("i1", T.i1[:], [[0, 24]], 0, 1, False)
+    iota("i3", T.i3[:, 0:16], [[1, 16]], 128, -1, False)
+    iota("i2", T.i2[:], [[16, 26]], 0, 0, False)
+    iota("iotb", T.iotb[:], [[1, CW]], 0, 0, True)
+    iota("iot", T.iot[:, 0:CW], [[1, CW]], 0, 0, True)
+    fill("pw", T.pws[:, 48:64], 2.0)
+    fill("ones", T.ones[:], 1.0)
+    run("g", "ones", "kp", lambda: g.affine_select(T.kp[:], T.ones[:, 0:A], [[0, 12], [1, 16]], op_.is_gt, 0.0, 0, 0))
+    run("g", "ones", "et", lambda: g.affine_select(T.et[:], T.ones[:], [[1, 528]], op_.is_equal, 0.0, -3, -4))
+    iota("iot2", T.iot[:, CW:776], [[1, 776 - CW]], CW, 0, True)
+
+    scan("pw", "pw2", T.pws[:, 0:16], T.pws[:, 48:64], T.pws[:, 48:64], 1.0, mul, mx)
+    ts("i1", "ih", T.i3[:, 16:17], T.i1[:, 0:1], 4, op_.arith_shift_right, 1, op_.bitwise_and)
+    fill("tz0", T.tz[:, 0:4], -1)
+    ts("i3", "i3", T.i3[:, 0:16], T.i3[:, 0:16], 15, op_.bitwise_and)
+    fill("tz1", T.tz[:, 28:36], -1)
+    ts("i1 ih", "i1", T.i1[:], T.i1[:], 15, op_.bitwise_and)
+    cp("ih", "hi", cor("hi"), T.i3[:, 16:17])
+    fill("tz2", T.tz[:, 60:64], -1)
+    ts("i3", "c16m", T.c16[:, 48:64], T.i3[:, 0:16], 0.0, op_.is_equal)
+    fill("neg2", T.neg2[:], -2.0)
+    ts("i1", "a8", cor("a8"), T.i1[:, 0:1], 8.0, op_.is_ge)
+    ts("i1", "z0", cor("z0"), T.i1[:, 0:1], 0.0, op_.is_equal)
+    tt("c16m pw2", "pw3", T.pws[:, 16:32], T.c16[:, 48:64], T.pws[:, 0:16], mul)
+    ts("i1", "e9", cor("e9"), T.i1[:, 0:1], 9.0, op_.is_equal)
+    tt("i1 i2", "n", sm("n"), T.i1[:], T.i2[:, 0:24], add)
+    cp("i1", "j16", cor("j16"), T.i1[:, 0:1])
+    scan("pw3", "thr", T.pws[:, 32:48], T.pws[:, 16:32], T.pws[:, 16:32], 0.0, add, mx)
+    thr = T.pws[:, 47:48]
+    for name, src, m, c in [("lo", "hi", -1.0, 1.0), ("h17", "hi", 16.0, 1.0), ("ks", "a8", -1.0, 2.0), ("k1", "a8", 2.0 * C - 1.0, KEY - 399.0),
+                            ("k2", "hi", "ks", 0.0), ("tkb", "a8", 4096.0, 400.0), ("kr", "k2", -16.0, "k1")]:
+        lin(name, src, m, c)
+    fill("szr_", T.szr[:, 0:1], 0.0)
+    fill("pa0", T.pa[:, 0:1], 0.0)
+    cp("i2", "lu", T.lu[:], T.i2[:, 0:8])
+    tt("thr z0", "thl", cor("thl"), thr, cor("z0"), sub)
+    ts("thr", "th2", cor("th2"), thr, 2.0, mul)
+    fill("pp_", T.pp[:, C:C + 1], 20.0)
+    fill("pb_", T.pb[:, C:C + 1], -20.0)
+    ts("iotb thl", "nl", T.nl[:], T.iotb[:], cor("thl"), op_.is_ge, 4096.0, mul)
+    ac("nl tkb", "tk", T.tk[:], T.nl[:], 1.0, cor("tkb"))
+    ac("iot ks kr", "krow", T.krow[:], T.iot[:, 0:CW], cor("ks"), cor("kr"))
+
+    ts("tz tz1 tz2 lo", "za", sm("za", 0, 58), T.tz[:, 4:62], cor("lo"), mul)
+    ts("tz tz0 tz1 tz2 hi", "zb", sm("zb", 0, 58), T.tz[:, 3:61], cor("hi"), mul)
+    tt("tz n", "end", sm("end"), T.tz[:, 4:28], sm("n"), add)
+    tt("n tz", "b", sm("b"), sm("n"), T.tz[:, 36:60], sub)
+    ts("i2 h17", "lid0", sm("lid0", 0, 26), T.i2[:], cor("h17"), sub, 1.0, add)
+    tt("za zb", "zc", sm("zc", 0, 58), sm("za", 0, 58), sm("zb", 0, 58), add)
+    cp("end", "lend", li("lend"), sm("end"))
+    ts("end", "lendo", li("lendo", 0, 12), sm("end", 12, 24), -float(A), add)
+    ts("lid0 j16", "lid", li("lid", 0, 26), sm("lid0", 0, 26), cor("j16"), add, C - 1.0, mn)
+    fill("oddx_", T.oddx[:, C + 1:C + 2], 0.0)
+    cp("zc", "lsz", li("lsz", 0, 26), sm("zc", 0, 26))
+    ts("zc h17", "lpr", li("lpr", 0, 26), sm("zc", 32, 58), cor("h17"), add)
+    ac("iotb lsz", "szr", T.szr[:, 1:CW + 1], ind("iotb", CW, "lsz", 25))
+    ac("szr szr_ lpr", "szp", T.szp[:], ind("szr", CW + 1, "lpr", 25))
+    quant("ut", "qu", T.qu[:], T.su[:], T.ut[:])
+    ts("zc", "lpx", li("lpx", 0, 26), sm("zc", 32, 58), 1.0, add)
+    ts("zc h17", "lpr2", li("lpr2", 0, 12), sm("zc", 45, 57), cor("h17"), add)
+    cp("qu lu", "qur", T.qur[:].bitcast(dt.uint32), T.qu[:].bitcast(dt.uint32).indirect(T.lu[:]))
+    cp("qu lu", "sur", T.sur[:], T.su[:].indirect(T.lu[:]))
+    ts("szr thl", "nl", T.nl[:], T.szr[:, 1:CW + 1], cor("thl"), op_.is_ge, 1.0, add)
+    ts("szr th2", "nh", T.nh[:], T.szr[:, 1:CW + 1], cor("th2"), op_.is_lt, -2.0, add)
+    quant("x0", "qxo0 qxr0", T.qx0[:], T.sx0[:], T.x0[:])
+    score(0, True)
+    score(0, False)
+    send(0, "codes")
+    iota("bt", T.bt[:, S0:S1 + 8], [[0, S1 + 8 - S0]], 0, 0, True)
+    iota("aw aw_", T.aw[:, S0:W], [[0, W - S0]], -2048, 0, True)
+    iota("xq_", T.xq[:, 2 * P:3 * P], [[0, P]], 0, 0, True)
+    iota("yp_", T.yp[:, 2 * P:3 * P], [[0, P]], 0, 0, True)
+    iota("otab", T.otab[:], [[0, 5], [1, C]], 0, 0, True)
+    for name, src, m, c in [("kb", "a8", 6144.0, -2048.0), ("xs", "a8", 799.0, -799.0), ("xb", "a8", -400.5, 0.5), ("yb", "e9", 1.0, -1.5),
+                            ("js", "a8", 1538.0, 0.0), ("jb", "e9", -1538.0, -2.0), ("ca0", "hi", -4096.0, 2048.0),
+                            ("ca1", "hi", 2048.0, -2048.0 - OFF), ("k0", "z0", -2.0 * B, B), ("kp_", "z0", -2.0 * B, B - BIG - 1.0),
+                            ("kl", "z0", -2.0 * B, B + P)]:
+        lin(name, src, m, c)
+    ac("a8", "rp_", T.rp[:, 0:1], cor("a8"), -1.0, -399.0)
+    ac("ones ca0", "c48a", T.c48[:, 0:48:2], T.ones[:, 0:24], cor("ca0"))
+    ac("ones ca1", "c48b", T.c48[:, 1:48:2], T.ones[:, 0:24], cor("ca1"))
+    ac("iot", "yy", T.yy[:], T.iot[:, 0:C], -1.0 / 2048, 1.0)
+
+    scan("nl nh", "inc", T.inc[:], T.nl[:], T.nh[:], 0.0, mx, add)
+    ts("szp th2", "keep1", T.keep1[:], T.szp[:], cor("th2"), op_.is_lt)
+    ts("szp thr kb", "keepb", T.keepb[:], T.szp[:], thr, op_.is_lt, cor("kb"), mul)
+    along(T.inc, "inc", sub)
+    signs(True)
+    signs(False)
+    parents(0)
+    parity(True)
+    parents(1)
+    parity(False)
+    planes(0)
+    down(0, T.inc, "inc", sub)
+    ends("o")
+    down(1, T.inc, "inc", sub)
+    ends(0)
+    ends(1)
+    turn(0)
+    turn(1)
+    kind(True)
+    kind(False)
+    kinds()
+    join(0, add)
+    join(1, add)
+    role(3)
+    pe, po = pick(7, 0)
+    role(2)
+    role(0)
+    role(1)
+    ts("pk0", "de", sm("d", 0, 24, 2), pe, -1.0, mul, -OFF - 1.0, add)
+    ts("pk0", "do", sm("d", 1, 24, 2), po, -1.0, mul, -OFF - 1.0, add)
+    ts("b", "s1", sm("s1"), sm("b"), 1.0, op_.is_gt, 775.0, mul)
+    ts("b", "s0", sm("s0"), sm("b"), 1.0, op_.is_equal, 771.0, mul)
+    ts("i3", "c16b", T.c16[:, 32:48], T.i3[:, 0:16], 15.0, op_.is_equal, 2.0 * B, mul)
+    cp("de do", "ld", li("ld"), sm("d"))
+    ts("de do", "d2", sm("d2"), sm("d"), 2.0, mul)
+    ac("iot ld", "nd1", T.nd1[:], ind("iot", CW, "ld"), -1.0, -399.0)
+    tt("tk lsz krow", "kc", T.kc[:], ind("tk", CW, "lsz", 25), T.krow[:], mn)
+    tt("d2 s1", "t10", sm("t10"), sm("d2"), sm("s1"), mx)
+    tt("d2 s0", "t11", sm("t11"), sm("d2"), sm("s0"), mx)
+    ts("c16m", "c16a", T.c16[:, 16:32], T.c16[:, 48:64], -B, mul)
+    cp("i1", "lp16", li("lp16"), T.i1[:])
+
+    def statics(k):
+        if k == 0:
+            cp("t10", "lca", li("lca"), sm("t10"))
+            cp("t11", "ldw", li("ldw"), sm("t11"))
+            tt("c16a c16b", "c16", T.c16[:, 0:16], T.c16[:, 16:32], T.c16[:, 32:48], add)
+            ts("tz", "lnm", li("lnm"), T.tz[:, 36:60], 2.0, mul, float(S0 + 3), add)
+            ac("nd1", "dw0", T.dw[:, S1:W], T.nd1[:], -1.0, -399.0)
+            ac("nd1", "dw1", T.dw[:, S0:S1:2], T.nd1[:], -1.0, -399.0)
+            ac("iot iot2 ldw", "dw2", T.dw[:, S0 + 1:S1:2], ind("iot", 776, "ldw"), 1.0, -385.0)
+        if k == 1:
+            scan("yy nd1", "vv", T.vv[:], T.yy[:], T.nd1[:], 2.0, mn, sub)
+        if k == 2:
+            ac("iot iot2 lca", "ca", T.ca[:], ind("iot", 776, "lca"), -1.0, -797.0)
+            ac("nd1", "v2", T.v2[:], T.nd1[:], -1.0, 401.0)
+        if k == 3:
+            ts("end", "lsib", li("lsib"), sm("end"), 2.0, mul, float(S0 + 1), add)
+            fill("rd_", T.rd[:, 0:1], BIG)
+            fill("go_", T.go[:, A:4 * 208:208], 0.0)
+        if k == 4:
+            ac("c16 lp16", "cv1", T.cv1[:], ind("c16", 16, "lp16"))
+        if k in (5, 6):
+            for b in range(2 * k - 10, 2 * k - 8):
+                quant("et", "qe%d" % b, T.qe[:, 128 * b:128 * b + 128], T.se[:, 128 * b:128 * b + 128], T.et[:, 3 - b:515 - b])
+        if k == 7:
+            cp("iot", "id16", T.id16[:], T.iot[:, 0:C])
+
     for t in range(NR):
         lst, ll = T["lst%d" % t], T["ll%d" % t]
 
@@ -447,38 +441,42 @@ def rank_program(g, core, T, topo):
 
         if t:
             parity(False)
-            ends(False)
+            kind(True)
+            ends(0)
+            ends(1)
+            role(0)
             kind(False)
             kinds()
-            role(False)
-        tt("rpo rpr rp_ lpx kc", "nv", T.nv[:], ind("rp", C + 1, "lpx", 25), T.kc[:], sub)
+            role(1)
+        tt("rp0 rp1 rp2 rp3 rp_ lpx kc", "nv", T.nv[:], ind("rp", C + 1, "lpx", 25), T.kc[:], sub)
         once(0)
-        scan("keep1 nv", "pa", T.pa[:, 1:CW + 1], T.keep1[:], T.nv[:], 0.0, mul, mn)
+        along(T.nv, "nv", mn)
         once(1)
         scan("dj nv", "nv2", T.nv2[:], T.dj[:], T.nv[:], 0.0, mx, add)
-        parents()
-        once(6)
+        parents(0)
+        parents(1)
+        ac("nd1", "bt", T.bt[:, S0:S1:2], T.nd1[:], -1.0)
+        ac("yko ykr", "rb", T.rb[:], T.yk[:], -1.0 / 800, -1.5, act.Relu)
+        once(2)
         down(0, T.nv2, "nv2", mn)
         evens(1)
         down(1, T.nv2, "nv2", mn)
-        ac("nd1", "bt", T.bt[:, S0:S1:2], T.nd1[:], -1.0)
         if t:
             planes(t)
-        once(2)
-        turn()
-        once(3)
-        join(mn)
+        turn(0)
+        turn(1)
+        join(0, mn)
+        join(1, mn)
         evens(0)
         pe, po = pick(9, 0)
         qe_, qo = pick(8, 1)
+        once(3)
         ts("pk0", "l1e", li("l1", 0, 24, 2), pe, -1.0, mul)
         ts("pk0", "l1o", li("l1", 1, 24, 2), po, -1.0, mul)
         ts("pk1", "l2e", li("l2", 0, 24, 2), qe_, -1.0, mul)
         ts("pk1", "l2o", li("l2", 1, 24, 2), qo, -1.0, mul)
         cp("vv l1e l1o", "bt", ind("bt", W, "l1"), T.vv[:])
         ac("dw0 dw1 dw2 l2e l2o", "dwg", T.dwg[:], ind("dw", W, "l2"), 1.0, 400.0)
-        if t == 0:
-            planes(t)
         once(4)
         ac("bt lnm", "ma", T.ma[:], ind("bt", W, "lnm"), 1.0, -784.0)
         scan("dwg v2", "nr", T.nr[:], T.dwg[:], T.v2[:], 0.0, mx, sub)
@@ -496,17 +494,19 @@ def rank_program(g, core, T, topo):
         ac("ub", "s3", T.s3[:], T.ub[:], -1.0, -1.25, act.Sign)
         ac("rd rd_", "base0", T.base[:, S0:S1:2], T.rd[:, 0:C])
         ac("s3", "sig", T.sig[:], T.s3[:], P / 2.0, P / 2.0)
-        unpack(t)
         once(5)
         tt("rd rd_ lb ma", "base2", T.base[:, S0 + 1:S1:2], ind("rd", C + 1, "lb"), T.ma[:], add)
-        scan("id16 sig", "val", T.val[:], T.id16[:], T.sig[:], 0.0, mx, sub)
+        once(6)
+        unpack(t)
         for h in range(2):
-            tt("base0 base10 base11 base2 l2e l2o mb", "m0%d" % h, T.m0[:, A * h:A * h + A], T.base[:, 0:W].indirect(li("l2", 12 * h, 12 * h + 12)),
+            tt("base0 base10 base11 base2 l2e l2o mb", "m0%d" % h, T.m0[:, A * h:A * h + A], ind("base", W, "l2", 12, 12 * h),
                T.mb[:, A * h:A * h + A], add)
         for h in range(2):
             half("m0%d" % h, T.m0, h, BIG + 2.0 * B)
         for h in range(2):
             ts("sc%d kp_" % h, "lpos%d" % h, li("lpos", 12 * h, 12 * h + 12), T.sc[:, A * h + 15:A * h + A:16], cor("kp_"), add)
+            if h == 0:
+                scan("id16 sig", "val", T.val[:], T.id16[:] if t else T.iot[:, 0:C], T.sig[:], 0.0, mx, sub)
         cp("val lpos0 lpos1", "orow", ind("orow", C, "lpos"), T.val[:])
         s = conv("orow", T.orow[:])
         ts("sc kl", "lst%d" % t, lst[:, 0:24], s, cor("kl"), add)
@@ -573,10 +573,8 @@ def rank_program(g, core, T, topo):
             diff(b, True)
         for b in range(4):
             big(b, True)
-        if t == NR - 1:
-            ac("otab lst%d" % t, "otr", T.otr[:], T.otab[:].indirect(lst[:, 0:24]))
-            dmas("s", "out", "otr", "", [(T.ot[k:k + 1, :], T.otr[16 * k:16 * k + 1, :]) for k in range(8)])
         product(True)
+        once(7)
         if t == NR - 1:
             quant("vt", "qv", T.qv[:], T.sv[:], T.vt[:])
         for b in range(4):
@@ -589,25 +587,23 @@ def rank_program(g, core, T, topo):
             diff(b, False)
         for b in range(4):
             big(b, False)
+        if t == NR - 1:
+            ac("otab lst%d" % t, "otr", T.otr[:], T.otab[:].indirect(lst[:, 0:24]))
+            dmas("s", "out", "otr", "", [(T.ot[k:k + 1, :], T.otr[16 * k:16 * k + 1, :]) for k in range(8)])
+        product(False)
         pack(True)
         if t == NR - 1:
             outputs(True)
         else:
             score(t + 1, True)
-        product(False)
-        if t < NR - 1:
-            signs(True)
-            state(0, False)
-            parity(True)
-        else:
-            result(True)
-            state(0, False)
-        tile(0, False)
-        for b in range(1, 4):
+        for b in range(4):
             state(b, False)
             tile(b, False)
         if t < NR - 1:
-            ends(True)
+            signs(True)
+            parity(True)
+        else:
+            result(True)
         pack(False)
         if t == NR - 1:
             outputs(False)
@@ -615,9 +611,10 @@ def rank_program(g, core, T, topo):
         else:
             score(t + 1, False)
             send(t + 1, "codes")
-            role(True)
+            ends("o")
+            role(2)
             signs(False)
-            kind(True)
+            role(3)
 
     for sem in [k for k in count if k != "out"] + ["out"]:
         if max(known[e].get(sem, 0) for e in eng) < count[sem]:

@@ -22,20 +22,20 @@ def _sb(dtype, **kw):
 
 
 _sb(H, x0=P, xt=P, xp=P, xq=3 * P, yp=3 * P, zt=P, z128=P, ut=512, vt=512, et=528,
-    sg=C, pp=C + 16, pb=C + 16, eb=C, oddx=C + 16, neg2=A, ones=528, go=4 * 208, gr=4 * 208, yq=C, rb=C, yk=C, dy=C, dj=CW,
-    iotb=CW, nl=CW, nh=CW, tk=CW, szr=CW + 16, szp=CW, keep1=CW, keepb=CW, inc=CW, kp=A, s3=C, c3=C, ub=C, sig=C)
-_sb(G, kc=CW, nv=CW, nv2=CW, hh=CW, uu=CW, tr=2 * C, seg=2 * C, id16=C, val=C)
+    sg=C + 16, pp=C + 16, pb=C + 16, eb=C + 16, oddx=C + 16, neg2=A, ones=528, go=4 * 208, gr=4 * 208, rb=C, yk=C, dy=C, dj=CW,
+    iotb=CW, nl=CW, nh=CW, tk=CW, szr=CW + 16, szp=CW, keep1=CW, keepb=CW, inc=CW, kp=A, kq=A, ev=C, cvb=C, s3=C, c3=C, ub=C, sig=C)
+_sb(G, rp=CW, kc=CW, nv=CW, nv2=CW, hh=CW, uu=CW, tr=2 * C, seg=2 * C, id16=C, val=C, m0=C, sd=C)
 _sb(Q, qu=128, qur=128, qv=128, qe=512, qw=512, qz=C, qx0=C, qx1=C, qx2=C, qx3=C, ql0=C, ql1=C, ql2=C)
 _sb(S, su=128, sur=128, sv=128, se=512, sw=512, szz=C, sx0=C, sx1=C, sx2=C, sx3=C, sl0=C, sl1=C, sl2=C)
 _sb(I, tz=64, i1=24, i2=26, i3=24, wi=24, oi=24)
 _sb(U, ls=26 * 20, lu=8, lst0=24, lst1=24, lst2=24, ll0=16, ll1=16, ll2=16)
-_sb(F, iot=776, sm=64 * 24, c16=64, c48=48, pk=96, pws=64, cor=40, cv1=C, krow=CW, pa=CW + 8, rp=C + 8, dx=C,
+_sb(F, iot=776, sm=64 * 24, c16=64, c48=48, pk=96, pws=64, cor=40, cv1=C, krow=CW + 8, pa=CW + 8, dx=CW, lw=CW + 8, kabs=CW,
     rd=392, sc=C, nd1=C, vv=C, v2=C, ca=C, dw=W, aw=W, bt=W, base=W, dwg=C,
-    m0=C, ma=C, mb=C, nr=C, yy=C, orow=C, otr=C, yo=C, otab=P + C)
+    ma=C, mc=C, mb=C, nr=C, yy=C, orow=C, otr=C, yo=C, otab=P + C)
 SCRATCH["pd"] = ("psum", [128, 2048], F)
 SCRATCH["pq"] = ("psum", [128, 2048], F)
 
-SEMAPHORES = (["v0", "a0", "p0", "g0", "ltree", "lu_", "lx", "lw", "lv", "sent", "out", "dupx", "dupy"]
+SEMAPHORES = (["v0", "a0", "p0", "g0", "ltree", "lu_", "lx", "lw", "lv", "sent", "out", "dupx", "dupy", "sum"]
               + ["ac%d" % t for t in range(NR)] + ["al%d" % t for t in range(NR)])
 
 
@@ -163,20 +163,20 @@ def rank_program(g, core, T, topo):
         ac(" ".join([src] + names), name, cor(name), cor(src), cor(m) if m in names else m, cor(c) if c in names else c)
 
     def conv(r, src, init=2.0 * B):
-        scan(r + " cv1", "sc sc0 sc1", T.sc[:], src, T.cv1[:], init, mn, add)
+        scan(r + " cv1", "sc sc2", T.sc[:], src, T.cv1[:], init, mn, add)
         return T.sc[:, 15:C:16]
 
-    def half(r, src, h, init=2.0 * B):
-        scan(r + " cv1", "sc1" if h else "sc sc0", T.sc[:, A * h:A * h + A], src[:, A * h:A * h + A], T.cv1[:, 0:A], init, mn, add)
+    def small(h, a, b):
+        scan("m0%d cvb" % h, "sd%d" % h, T.sd[:, a:b], T.m0[:, a:b], T.cvb[:, 0:b - a], 1024.0, mn, add)
 
     cut = [0, A + 16, CW]
 
     def along(row, r, o):
         scan("keep1 " + r, "pa", T.pa[:, 1:CW + 1], T.keep1[:], row[:], 0.0, mul, o)
 
-    def parents(h):
-        tt("pa pa0 lpr lpr2 keepb", "hh%d" % h, T.hh[:, cut[h]:cut[h + 1]],
-           ind("pa", CW + 1, "lpr2", 12) if h else ind("pa", CW + 1, "lpr", 13), T.keepb[:, cut[h]:cut[h + 1]], add)
+    def parents(h, row="keepb"):
+        tt("pa pa0 lpr lpr2 " + row, "hh%d" % h, T.hh[:, cut[h]:cut[h + 1]],
+           ind("pa", CW + 1, "lpr2", 12) if h else ind("pa", CW + 1, "lpr", 13), T[row][:, cut[h]:cut[h + 1]], add)
 
     def down(h, row, r, o):
         a, b = cut[h], cut[h + 1]
@@ -187,19 +187,25 @@ def rank_program(g, core, T, topo):
             run("v", "uu0 uu%d" % h, "tr%d%d" % (h, k),
                 lambda: V.transpose(T.tr[:, C * k + A * h:C * k + A * h + A], T.uu[:, 16 * k + A * h:16 * k + A * h + A]))
 
-    def join(h, o):
+    def join(h, least):
         for k in range(2):
             a = C * k + A * h
-            scan("kp tr%d%d" % (h, k), "seg%d%d" % (h, k), T.seg[:, a:a + A], T.kp[:], T.tr[:, a:a + A], 0.0, mul, o)
+            if least:
+                scan("kq9 kq25 kq15 kq31 tr%d%d" % (h, k), "seg%d%d" % (h, k), T.seg[:, a:a + A], T.tr[:, a:a + A], T.kq[:], 0.0, mn, add)
+            else:
+                scan("kp tr%d%d" % (h, k), "seg%d%d" % (h, k), T.seg[:, a:a + A], T.kp[:], T.tr[:, a:a + A], 0.0, mul, add)
 
     def pick(j, k):
         scan("seg00 seg01 seg10 seg11 c48a c48b", "pk%d" % k, T.pk[:, 48 * k:48 * k + 48], T.seg[:, j:2 * C:16], T.c48[:], -4096.0, mx, add)
         return T.pk[:, 48 * k + 1:48 * k + 24:2], T.pk[:, 48 * k + 25:48 * k + 48:2]
 
     def evens(h):
-        back = slice(S1 + A * h + A - 1, S1 + A * h - 1, -1)
-        scan("oddx oddx_ ones base11", "base1%d" % h, T.base[:, back], T.oddx[:, A * h + A + 1:A * h + 1:-1], T.ones[:, 0:A],
-             BIG + C if h else T.base[:, S1 + A:S1 + A + 1], add, sub)
+        back = slice(A * h + A - 1, A * h - 1 if h else None, -1)
+        scan("oddx oddx_ ones", "ev%d" % h, T.ev[:, back], T.oddx[:, A * h + A + 1:A * h + 1:-1], T.ones[:, 0:A], 0.0, add, sub)
+
+    def places(h):
+        ac("ev%d base11" % h, "base1%d" % h, T.base[:, S1 + A * h:S1 + A * h + A], T.ev[:, A * h:A * h + A], 1.0,
+           BIG + C if h else T.base[:, S1 + A:S1 + A + 1])
 
     def send(t, what):
         dst = T.cores[(rank + STEP[t]) % n_ranks]
@@ -229,35 +235,37 @@ def rank_program(g, core, T, topo):
 
     def signs(own):
         h, c0, bank = ("o", A, 0) if own else ("r", 0, 1)
-        ts("pd%d" % bank, "sg" + h, T.sg[:, c0:c0 + A], T.pd[:, 512 * bank:512 * bank + A], 0.0, op_.is_gt, 0.5, sub)
+        ts("pd%d" % bank, "sg" + h, T.sg[:, 1 + c0:1 + c0 + A], T.pd[:, 512 * bank:512 * bank + A], 0.0, op_.is_gt, 0.5, sub)
+
+    def defects(own):
+        h, c0 = ("o", A) if own else ("r", 0)
+        ac("sg" + h, "dy" + h, T.dy[:, c0:c0 + A], T.sg[:, 1 + c0:1 + c0 + A], -1.0, -1.5)
 
     def parity(own):
         h, c0 = ("o", A) if own else ("r", 0)
         back = slice(c0 + A - 1, c0 - 1 if c0 else None, -1)
-        scan("neg2 ppo sg" + h, "pp" + h, T.pp[:, back], T.sg[:, back], T.neg2[:], 20.0 if own else T.pp[:, A:A + 1], mul, mul)
-        ac("xs xb sg" + h, "dx" + h, T.dx[:, c0:c0 + A], T.sg[:, c0:c0 + A], cor("xs"), cor("xb"))
-        scan("neg2 pbo sg" + h, "pb" + h, T.pb[:, back], T.sg[:, back], T.neg2[:], -20.0 if own else T.pb[:, A:A + 1], mul, mul)
-        ac("sg" + h, "dy" + h, T.dy[:, c0:c0 + A], T.sg[:, c0:c0 + A], -800.0, -1200.0)
+        sg = T.sg[:, c0 + A:c0:-1]
+        scan("neg2 ppo sg" + h, "pp" + h, T.pp[:, back], sg, T.neg2[:], 1.0 if own else T.pp[:, A:A + 1], mul, mul)
+        scan("neg2 pbo sg" + h, "pb" + h, T.pb[:, back], sg, T.neg2[:], 1.0 if own else T.pb[:, A:A + 1], mul, mul)
+        if not own:
+            ac("sgo sgr sg_ lpx xs xb", "dx", T.dx[:], ind("sg", C + 1, "lpx", 25), cor("xs"), cor("xb"))
 
-    def ends(q):
-        if q == "o":
-            tt("ppo pp_ pbo pb_ lendo", "ebo", T.eb[:, A:C], T.pp[:, A:C + 1].indirect(li("lendo", 0, 12)), T.pb[:, A + 1:C + 1], mul)
+    def ends(own):
+        if own:
+            tt("ppo pp_ pbo pb_ lendo", "ebo", T.eb[:, A + 1:C + 1], T.pp[:, A:C + 1].indirect(li("lendo", 0, 12)), T.pb[:, A + 1:C + 1], op_.not_equal)
         else:
-            a = 96 * q
-            tt("ppo ppr pp_ pbo pbr lend", "eb%d" % q, T.eb[:, a:a + 96], ind("pp", C + 1, "lend", 6, 6 * q), T.pb[:, a + 1:a + 97], mul)
+            tt("ppo ppr pp_ pbo pbr lend", "ebr", T.eb[:, 1:A + 1], ind("pp", C + 1, "lend", 12), T.pb[:, 1:A + 1], op_.not_equal)
 
-    def role(q):
-        a = 96 * q
-        tt("ebo dxo" if q > 1 else "eb%d dxr" % q, "rp%d" % q, T.rp[:, 1 + a:97 + a], T.eb[:, a:a + 96], T.dx[:, a:a + 96], mn)
+    def role():
+        tt("ebo ebr eb_ lpx dx", "rp", T.rp[:], ind("eb", C + 1, "lpx", 25), T.dx[:], mul)
 
     def kind(own):
-        h, c0, e = ("o", A, "ebo") if own else ("r", 0, "eb0 eb1")
-        scan("%s dy%s" % (e, h), "yk" + h, T.yk[:, c0:c0 + A], T.eb[:, c0:c0 + A], T.dy[:, c0:c0 + A], -4096.0, mx, add)
-        ac("yb yk" + h, "yq" + h, T.yq[:, c0:c0 + A], T.yk[:, c0:c0 + A], -1.0 / 800, cor("yb"), act.Abs)
+        h, c0 = ("o", A) if own else ("r", 0)
+        scan("eb%s dy%s" % (h, h), "yk" + h, T.yk[:, c0:c0 + A], T.eb[:, 1 + c0:1 + c0 + A], T.dy[:, c0:c0 + A], 0.0, mx, add)
 
     def kinds():
-        ac("yqo yqr lid js jb", "dj", T.dj[:], ind("yq", C, "lid", 25), cor("js"), cor("jb"), act.Relu)
-        ac("yko ykr", "oddx", T.oddx[:, 1:C + 1], T.yk[:], -1.0 / 800, -1.5, act.Abs)
+        ac("yko ykr lid js jb", "dj", T.dj[:], ind("yk", C, "lid", 25), cor("js"), cor("jb"), act.Abs)
+        ac("yko ykr", "oddx", T.oddx[:, 1:C + 1], T.yk[:], -1.0, -1.0, act.Abs)
 
     def unpack(t):
         for b in range(4):
@@ -292,6 +300,8 @@ def rank_program(g, core, T, topo):
     run("g", "ones", "et", lambda: g.affine_select(T.et[:], T.ones[:], [[1, 528]], op_.is_equal, 0.0, -3, -4))
     iota("iot2", T.iot[:, CW:776], [[1, 776 - CW]], CW, 0, True)
 
+    ac("ones", "bt", T.bt[:, S0 + 1:S1 + 2:2], T.ones[:, 0:C + 1], 0.0)
+    ac("ones", "aw", T.aw[:, S0:S1:2], T.ones[:, 0:C], -2048.0)
     scan("pw", "pw2", T.pws[:, 0:16], T.pws[:, 48:64], T.pws[:, 48:64], 1.0, mul, mx)
     ts("i1", "ih", T.i3[:, 16:17], T.i1[:, 0:1], 4, op_.arith_shift_right, 1, op_.bitwise_and)
     fill("tz0", T.tz[:, 0:4], -1)
@@ -301,7 +311,6 @@ def rank_program(g, core, T, topo):
     cp("ih", "hi", cor("hi"), T.i3[:, 16:17])
     fill("tz2", T.tz[:, 60:64], -1)
     ts("i3", "c16m", T.c16[:, 48:64], T.i3[:, 0:16], 0.0, op_.is_equal)
-    fill("neg2", T.neg2[:], -2.0)
     ts("i1", "a8", cor("a8"), T.i1[:, 0:1], 8.0, op_.is_ge)
     ts("i1", "z0", cor("z0"), T.i1[:, 0:1], 0.0, op_.is_equal)
     tt("c16m pw2", "pw3", T.pws[:, 16:32], T.c16[:, 48:64], T.pws[:, 0:16], mul)
@@ -310,127 +319,145 @@ def rank_program(g, core, T, topo):
     cp("i1", "j16", cor("j16"), T.i1[:, 0:1])
     scan("pw3", "thr", T.pws[:, 32:48], T.pws[:, 16:32], T.pws[:, 16:32], 0.0, add, mx)
     thr = T.pws[:, 47:48]
-    for name, src, m, c in [("lo", "hi", -1.0, 1.0), ("h17", "hi", 16.0, 1.0), ("ks", "a8", -1.0, 2.0), ("k1", "a8", 2.0 * C - 1.0, KEY - 399.0),
-                            ("k2", "hi", "ks", 0.0), ("tkb", "a8", 4096.0, 400.0), ("kr", "k2", -16.0, "k1")]:
+    for name, src, m, c in [("lo", "hi", -1.0, 1.0), ("h17", "hi", 16.0, 1.0), ("ks", "a8", -1.0, 2.0), ("k1", "a8", 2.0 * C - 1.0, KEY + 1.0),
+                            ("k2", "hi", "ks", 0.0), ("tkb", "a8", 4096.0, 800.0), ("kb", "a8", 6144.0, -2048.0),
+                            ("kr", "k2", -16.0, "k1")]:
         lin(name, src, m, c)
     fill("szr_", T.szr[:, 0:1], 0.0)
-    fill("pa0", T.pa[:, 0:1], 0.0)
     cp("i2", "lu", T.lu[:], T.i2[:, 0:8])
-    tt("thr z0", "thl", cor("thl"), thr, cor("z0"), sub)
-    ts("thr", "th2", cor("th2"), thr, 2.0, mul)
-    fill("pp_", T.pp[:, C:C + 1], 20.0)
-    fill("pb_", T.pb[:, C:C + 1], -20.0)
-    ts("iotb thl", "nl", T.nl[:], T.iotb[:], cor("thl"), op_.is_ge, 4096.0, mul)
-    ac("nl tkb", "tk", T.tk[:], T.nl[:], 1.0, cor("tkb"))
-    ac("iot ks kr", "krow", T.krow[:], T.iot[:, 0:CW], cor("ks"), cor("kr"))
+    ac("ones", "neg2", T.neg2[:], T.ones[:, 0:A], -2.0)
+    cp("i1", "lp16", li("lp16"), T.i1[:])
+    ts("i3", "c16b", T.c16[:, 32:48], T.i3[:, 0:16], 15.0, op_.is_equal, 2.0 * B, mul)
+    ac("c16m", "c16a", T.c16[:, 16:32], T.c16[:, 48:64], -B)
+    ac("ones", "kq", T.kq[:], T.ones[:, 0:A], 0.0)
+    ac("ones", "aw_", T.aw[:, S1:W], T.ones[:, 0:C], -2048.0)
 
     ts("tz tz1 tz2 lo", "za", sm("za", 0, 58), T.tz[:, 4:62], cor("lo"), mul)
     ts("tz tz0 tz1 tz2 hi", "zb", sm("zb", 0, 58), T.tz[:, 3:61], cor("hi"), mul)
     tt("tz n", "end", sm("end"), T.tz[:, 4:28], sm("n"), add)
-    tt("n tz", "b", sm("b"), sm("n"), T.tz[:, 36:60], sub)
-    ts("i2 h17", "lid0", sm("lid0", 0, 26), T.i2[:], cor("h17"), sub, 1.0, add)
+    tt("thr z0", "thl", cor("thl"), thr, cor("z0"), sub)
+    ts("thr", "th2", cor("th2"), thr, 2.0, mul)
     tt("za zb", "zc", sm("zc", 0, 58), sm("za", 0, 58), sm("zb", 0, 58), add)
     cp("end", "lend", li("lend"), sm("end"))
     ts("end", "lendo", li("lendo", 0, 12), sm("end", 12, 24), -float(A), add)
-    ts("lid0 j16", "lid", li("lid", 0, 26), sm("lid0", 0, 26), cor("j16"), add, C - 1.0, mn)
-    fill("oddx_", T.oddx[:, C + 1:C + 2], 0.0)
+    ts("i2 h17", "lid0", sm("lid0", 0, 26), T.i2[:], cor("h17"), sub, 1.0, add)
+    tt("n tz", "b", sm("b"), sm("n"), T.tz[:, 36:60], sub)
     cp("zc", "lsz", li("lsz", 0, 26), sm("zc", 0, 26))
     ts("zc h17", "lpr", li("lpr", 0, 26), sm("zc", 32, 58), cor("h17"), add)
     ac("iotb lsz", "szr", T.szr[:, 1:CW + 1], ind("iotb", CW, "lsz", 25))
     ac("szr szr_ lpr", "szp", T.szp[:], ind("szr", CW + 1, "lpr", 25))
+    ts("iotb thl", "nh", T.nh[:], T.iotb[:], cor("thl"), op_.is_ge, 4096.0, mul)
     quant("ut", "qu", T.qu[:], T.su[:], T.ut[:])
     ts("zc", "lpx", li("lpx", 0, 26), sm("zc", 32, 58), 1.0, add)
+    ts("lid0 j16", "lid", li("lid", 0, 26), sm("lid0", 0, 26), cor("j16"), add, C - 1.0, mn)
     ts("zc h17", "lpr2", li("lpr2", 0, 12), sm("zc", 45, 57), cor("h17"), add)
+    tt("c16a c16b", "c16", T.c16[:, 0:16], T.c16[:, 16:32], T.c16[:, 32:48], add)
     cp("qu lu", "qur", T.qur[:].bitcast(dt.uint32), T.qu[:].bitcast(dt.uint32).indirect(T.lu[:]))
     cp("qu lu", "sur", T.sur[:], T.su[:].indirect(T.lu[:]))
     ts("szr thl", "nl", T.nl[:], T.szr[:, 1:CW + 1], cor("thl"), op_.is_ge, 1.0, add)
-    ts("szr th2", "nh", T.nh[:], T.szr[:, 1:CW + 1], cor("th2"), op_.is_lt, -2.0, add)
+    ts("szr th2", "dj", T.dj[:], T.szr[:, 1:CW + 1], cor("th2"), op_.is_lt, -2.0, add)
+    for w, ap, c in [("pa0", T.pa[:, 0:1], 0.0), ("pp_", T.pp[:, C:C + 1], 1.0), ("pb_", T.pb[:, C:C + 1], 1.0),
+                     ("oddx_", T.oddx[:, C + 1:C + 2], 0.0), ("sg_", T.sg[:, 0:1], 0.5), ("eb_", T.eb[:, 0:1], 1.0), ("rd_", T.rd[:, 0:1], BIG)]:
+        ac("ones", w, ap, T.ones[:, 0:1], c)
     quant("x0", "qxo0 qxr0", T.qx0[:], T.sx0[:], T.x0[:])
     score(0, True)
     score(0, False)
     send(0, "codes")
-    iota("bt", T.bt[:, S0:S1 + 8], [[0, S1 + 8 - S0]], 0, 0, True)
-    iota("aw aw_", T.aw[:, S0:W], [[0, W - S0]], -2048, 0, True)
     iota("xq_", T.xq[:, 2 * P:3 * P], [[0, P]], 0, 0, True)
     iota("yp_", T.yp[:, 2 * P:3 * P], [[0, P]], 0, 0, True)
     iota("otab", T.otab[:], [[0, 5], [1, C]], 0, 0, True)
-    for name, src, m, c in [("kb", "a8", 6144.0, -2048.0), ("xs", "a8", 799.0, -799.0), ("xb", "a8", -400.5, 0.5), ("yb", "e9", 1.0, -1.5),
-                            ("js", "a8", 1538.0, 0.0), ("jb", "e9", -1538.0, -2.0), ("ca0", "hi", -4096.0, 2048.0),
-                            ("ca1", "hi", 2048.0, -2048.0 - OFF), ("k0", "z0", -2.0 * B, B), ("kp_", "z0", -2.0 * B, B - BIG - 1.0),
+    for name, src, m, c in [("xs", "a8", 799.0, -799.0), ("xb", "a8", -400.5, 400.5), ("j1", "a8", 1536.0, 0.0),
+                            ("ka", "a8", 1.0, -1.0), ("kj", "a8", 8192.0, 0.0),
+                            ("js", "e9", -752.0, "j1"), ("jb", "e9", -1536.0, "j1"), ("ca0", "hi", -4096.0, 2048.0),
+                            ("ca1", "hi", 2048.0, -2048.0 - OFF), ("k0", "z0", -2.0 * B, B), ("kp_", "z0", -1024.0, 511.0),
                             ("kl", "z0", -2.0 * B, B + P)]:
         lin(name, src, m, c)
-    ac("a8", "rp_", T.rp[:, 0:1], cor("a8"), -1.0, -399.0)
     ac("ones ca0", "c48a", T.c48[:, 0:48:2], T.ones[:, 0:24], cor("ca0"))
     ac("ones ca1", "c48b", T.c48[:, 1:48:2], T.ones[:, 0:24], cor("ca1"))
+    ac("nh tkb", "tk", T.tk[:], T.nh[:], 1.0, cor("tkb"))
+    ac("iot ks kr", "krow", T.krow[:, 1:CW + 1], T.iot[:, 0:CW], cor("ks"), cor("kr"))
+    for j, src, m, c in [(9, "lo", -4096.0, 0.0), (25, "lo", 4096.0, 0.0), (15, "hi", 8192.0, 0.0), (31, "hi", 0.0, 8192.0)]:
+        lin("q%d" % j, src, m, c)
     ac("iot", "yy", T.yy[:], T.iot[:, 0:C], -1.0 / 2048, 1.0)
+    for j in (9, 25, 15, 31):
+        ac("ones kq q%d" % j, "kq%d" % j, T.kq[:, j:A:32], T.ones[:, 0:6], cor("q%d" % j))
 
-    scan("nl nh", "inc", T.inc[:], T.nl[:], T.nh[:], 0.0, mx, add)
+    scan("nl dj", "inc", T.inc[:], T.nl[:], T.dj[:], 0.0, mx, add)
     ts("szp th2", "keep1", T.keep1[:], T.szp[:], cor("th2"), op_.is_lt)
     ts("szp thr kb", "keepb", T.keepb[:], T.szp[:], thr, op_.is_lt, cor("kb"), mul)
     along(T.inc, "inc", sub)
     signs(True)
     signs(False)
+    defects(True)
+    defects(False)
     parents(0)
     parity(True)
     parents(1)
     parity(False)
     planes(0)
     down(0, T.inc, "inc", sub)
-    ends("o")
+    ends(True)
     down(1, T.inc, "inc", sub)
-    ends(0)
-    ends(1)
+    ends(False)
     turn(0)
     turn(1)
     kind(True)
     kind(False)
     kinds()
-    join(0, add)
-    join(1, add)
-    role(3)
+    join(0, False)
+    join(1, False)
+    tt("tk lsz krow", "kc", T.kc[:], ind("tk", CW, "lsz", 25), T.krow[:, 1:CW + 1], mn)
     pe, po = pick(7, 0)
-    role(2)
-    role(0)
-    role(1)
+    role()
     ts("pk0", "de", sm("d", 0, 24, 2), pe, -1.0, mul, -OFF - 1.0, add)
     ts("pk0", "do", sm("d", 1, 24, 2), po, -1.0, mul, -OFF - 1.0, add)
     ts("b", "s1", sm("s1"), sm("b"), 1.0, op_.is_gt, 775.0, mul)
     ts("b", "s0", sm("s0"), sm("b"), 1.0, op_.is_equal, 771.0, mul)
-    ts("i3", "c16b", T.c16[:, 32:48], T.i3[:, 0:16], 15.0, op_.is_equal, 2.0 * B, mul)
     cp("de do", "ld", li("ld"), sm("d"))
     ts("de do", "d2", sm("d2"), sm("d"), 2.0, mul)
     ac("iot ld", "nd1", T.nd1[:], ind("iot", CW, "ld"), -1.0, -399.0)
-    tt("tk lsz krow", "kc", T.kc[:], ind("tk", CW, "lsz", 25), T.krow[:], mn)
+    scan("rp kc", "nv", T.nv[:], T.rp[:], T.kc[:], 0.0, mx, sub)
     tt("d2 s1", "t10", sm("t10"), sm("d2"), sm("s1"), mx)
     tt("d2 s0", "t11", sm("t11"), sm("d2"), sm("s0"), mx)
-    ts("c16m", "c16a", T.c16[:, 16:32], T.c16[:, 48:64], -B, mul)
-    cp("i1", "lp16", li("lp16"), T.i1[:])
 
     def statics(k):
         if k == 0:
             cp("t10", "lca", li("lca"), sm("t10"))
             cp("t11", "ldw", li("ldw"), sm("t11"))
-            tt("c16a c16b", "c16", T.c16[:, 0:16], T.c16[:, 16:32], T.c16[:, 32:48], add)
             ts("tz", "lnm", li("lnm"), T.tz[:, 36:60], 2.0, mul, float(S0 + 3), add)
             ac("nd1", "dw0", T.dw[:, S1:W], T.nd1[:], -1.0, -399.0)
             ac("nd1", "dw1", T.dw[:, S0:S1:2], T.nd1[:], -1.0, -399.0)
             ac("iot iot2 ldw", "dw2", T.dw[:, S0 + 1:S1:2], ind("iot", 776, "ldw"), 1.0, -385.0)
-        if k == 1:
-            scan("yy nd1", "vv", T.vv[:], T.yy[:], T.nd1[:], 2.0, mn, sub)
+        if k in (1, 11):
+            a = A * (k // 11)
+            scan("yy nd1", "vv%d" % k, T.vv[:, a:a + A], T.yy[:, a:a + A], T.nd1[:, a:a + A], 2.0, mn, sub)
         if k == 2:
             ac("iot iot2 lca", "ca", T.ca[:], ind("iot", 776, "lca"), -1.0, -797.0)
             ac("nd1", "v2", T.v2[:], T.nd1[:], -1.0, 401.0)
         if k == 3:
             ts("end", "lsib", li("lsib"), sm("end"), 2.0, mul, float(S0 + 1), add)
-            fill("rd_", T.rd[:, 0:1], BIG)
             fill("go_", T.go[:, A:4 * 208:208], 0.0)
         if k == 4:
             ac("c16 lp16", "cv1", T.cv1[:], ind("c16", 16, "lp16"))
+        if k == 5:
+            ac("cv1", "cvb", T.cvb[:], T.cv1[:], 512.0 / B)
         if k in (5, 6):
             for b in range(2 * k - 10, 2 * k - 8):
                 quant("et", "qe%d" % b, T.qe[:, 128 * b:128 * b + 128], T.se[:, 128 * b:128 * b + 128], T.et[:, 3 - b:515 - b])
         if k == 7:
             cp("iot", "id16", T.id16[:], T.iot[:, 0:C])
+            scan("nh nl", "keep1", T.keep1[:], T.nh[:], T.nl[:], 0.0, mx, mul)
+            fill("lw_", T.lw[:, 0:1], 2.0)
+            before("g", ["keep1", "lw", "lw_"], [])
+            g.dma_start(T.lw[:, 0:CW], T.keep1[:], accum_op=add).then_inc(T.sem.sum, 16)
+            count["sum"] = 16
+            after(("sum", 16, dict(known["g"])), ["keep1"], ["lw"])
+        if k == 9:
+            ac("kr", "krow_", T.krow[:, 0:1], cor("kr"))
+            ac("keep1", "nh", T.nh[:], T.keep1[:], -49152.0, 65536.0)
+            ac("nl", "lw", T.lw[:, 1:CW + 1], T.nl[:], -4096.0, 4098.0)
+            ac("nl", "nl", T.nl[:], T.nl[:], 0.25, -0.25)
+            ac("krow krow_ lpr ka kj", "kabs", T.kabs[:], ind("krow", CW + 1, "lpr", 25), cor("ka"), cor("kj"))
 
     for t in range(NR):
         lst, ll = T["lst%d" % t], T["ll%d" % t]
@@ -441,49 +468,57 @@ def rank_program(g, core, T, topo):
 
         if t:
             parity(False)
+            defects(False)
             kind(True)
-            ends(0)
-            ends(1)
-            role(0)
+            ends(False)
+            role()
             kind(False)
             kinds()
-            role(1)
-        tt("rp0 rp1 rp2 rp3 rp_ lpx kc", "nv", T.nv[:], ind("rp", C + 1, "lpx", 25), T.kc[:], sub)
-        once(0)
-        along(T.nv, "nv", mn)
-        once(1)
-        scan("dj nv", "nv2", T.nv2[:], T.dj[:], T.nv[:], 0.0, mx, add)
-        parents(0)
-        parents(1)
+        if t:
+            scan("lw rp", "pa", T.pa[:, 1:CW + 1], T.lw[:, 0:CW], T.rp[:], 4096.0, add, mn)
+            scan("rp kc", "nv", T.nv[:], T.rp[:], T.kc[:], 0.0, mx, sub)
+            parents(0, "kabs")
+            scan("dj nv", "nv2", T.nv2[:], T.dj[:], T.nv[:], 0.0, mx, add)
+            parents(1, "kabs")
+        else:
+            along(T.nv, "nv", mn)
+            once(0)
+            scan("dj nv", "nv2", T.nv2[:], T.dj[:], T.nv[:], 0.0, mx, add)
+            parents(0)
+            parents(1)
         ac("nd1", "bt", T.bt[:, S0:S1:2], T.nd1[:], -1.0)
-        ac("yko ykr", "rb", T.rb[:], T.yk[:], -1.0 / 800, -1.5, act.Relu)
+        ac("yko ykr", "rb", T.rb[:], T.yk[:], -1.0, -1.0, act.Relu)
         once(2)
         down(0, T.nv2, "nv2", mn)
         evens(1)
+        once(1)
         down(1, T.nv2, "nv2", mn)
         if t:
             planes(t)
         turn(0)
         turn(1)
-        join(0, mn)
-        join(1, mn)
+        join(0, True)
+        join(1, True)
         evens(0)
-        pe, po = pick(9, 0)
+        once(11)
         qe_, qo = pick(8, 1)
+        ts("seg00 seg10", "l1e", li("l1", 0, 24, 2), T.seg[:, 25:C:32], -1.0, mul, float(OFF), add)
+        ts("seg01 seg11", "l1o", li("l1", 1, 24, 2), T.seg[:, C + 25:2 * C:32], -1.0, mul, float(OFF), add)
         once(3)
-        ts("pk0", "l1e", li("l1", 0, 24, 2), pe, -1.0, mul)
-        ts("pk0", "l1o", li("l1", 1, 24, 2), po, -1.0, mul)
         ts("pk1", "l2e", li("l2", 0, 24, 2), qe_, -1.0, mul)
         ts("pk1", "l2o", li("l2", 1, 24, 2), qo, -1.0, mul)
-        cp("vv l1e l1o", "bt", ind("bt", W, "l1"), T.vv[:])
+        cp("vv1 vv11 l1e l1o", "bt", ind("bt", W, "l1"), T.vv[:])
         ac("dw0 dw1 dw2 l2e l2o", "dwg", T.dwg[:], ind("dw", W, "l2"), 1.0, 400.0)
         once(4)
         ac("bt lnm", "ma", T.ma[:], ind("bt", W, "lnm"), 1.0, -784.0)
         scan("dwg v2", "nr", T.nr[:], T.dwg[:], T.v2[:], 0.0, mx, sub)
         tt("bt lsib ca", "aw aw_", T.aw[:, S0 + 1:S1:2], ind("bt", W, "lsib"), T.ca[:], add)
         ac("nr", "s3", T.s3[:], T.nr[:], 1.0, 400.0, act.Sign)
+        places(1)
         ac("s3", "c3", T.c3[:], T.s3[:], 2.5, -1.0, act.Abs)
-        ac("nr", "mb", T.mb[:], T.nr[:], 1.0, 399.0, act.Abs)
+        ac("nr", "mc", T.mc[:], T.nr[:], 1.0, 399.0, act.Abs)
+        places(0)
+        ac("mc", "mb", T.mb[:], T.mc[:], 1.0, -BIG)
         s = conv("ma", T.ma[:])
         tt("aw aw_ l1e l1o nd1", "yy", T.yy[:], ind("aw", W, "l1"), T.nd1[:], mx)
         ts("sc k0", "wi", T.wi[:], s, cor("k0"), add, -2048.0, mul)
@@ -498,19 +533,19 @@ def rank_program(g, core, T, topo):
         tt("rd rd_ lb ma", "base2", T.base[:, S0 + 1:S1:2], ind("rd", C + 1, "lb"), T.ma[:], add)
         once(6)
         unpack(t)
-        for h in range(2):
-            tt("base0 base10 base11 base2 l2e l2o mb", "m0%d" % h, T.m0[:, A * h:A * h + A], ind("base", W, "l2", 12, 12 * h),
-               T.mb[:, A * h:A * h + A], add)
-        for h in range(2):
-            half("m0%d" % h, T.m0, h, BIG + 2.0 * B)
-        for h in range(2):
-            ts("sc%d kp_" % h, "lpos%d" % h, li("lpos", 12 * h, 12 * h + 12), T.sc[:, A * h + 15:A * h + A:16], cor("kp_"), add)
-            if h == 0:
-                scan("id16 sig", "val", T.val[:], T.id16[:] if t else T.iot[:, 0:C], T.sig[:], 0.0, mx, sub)
-        cp("val lpos0 lpos1", "orow", ind("orow", C, "lpos"), T.val[:])
-        s = conv("orow", T.orow[:])
-        ts("sc kl", "lst%d" % t, lst[:, 0:24], s, cor("kl"), add)
+        once(9)
+        for h, a, b in [(0, 0, 288), (1, 288, C)]:
+            tt("base0 base10 base11 base2 l2e l2o mb", "m0%d" % h, T.m0[:, a:b], ind("base", W, "l2", (b - a) // 16, a // 16), T.mb[:, a:b], add)
+        small(0, 0, 288)
+        small(1, 288, C)
+        scan("id16 sig", "val", T.val[:], T.id16[:] if t else T.iot[:, 0:C], T.sig[:], 0.0, mx, sub)
+        ts("sd0 sd1 kp_", "lpos", li("lpos"), T.sd[:, 15:C:16], cor("kp_"), add)
+        cp("val lpos", "orow", ind("orow", C, "lpos"), T.val[:])
+        scan("orow cv1", "sc", T.sc[:, 0:224], T.orow[:, 0:224], T.cv1[:, 0:224], 2.0 * B, mn, add)
+        scan("orow cv1", "sc2", T.sc[:, 224:C], T.orow[:, 224:C], T.cv1[:, 0:160], 2.0 * B, mn, add)
+        ts("sc kl", "lst%d" % t, lst[:, 0:14], T.sc[:, 15:224:16], cor("kl"), add)
         send(t, "lists")
+        ts("sc2 kl", "lsu%d" % t, lst[:, 14:24], T.sc[:, 239:C:16], cor("kl"), add)
 
         qn, sn = T["qx%d" % (t + 1)], T["sx%d" % (t + 1)]
 
@@ -518,14 +553,14 @@ def rank_program(g, core, T, topo):
             call = cp if own and b == 0 else ac
             a = P + C * b
             if own:
-                call("xq xq_ lst%d" % t, "go%d" % b, T.go[:, 208 * b:208 * b + A], T.xq[:, a:a + P + C].indirect(lst[:, 12:24]))
+                call("xq xq_ lst%d lsu%d" % (t, t), "go%d" % b, T.go[:, 208 * b:208 * b + A], T.xq[:, a:a + P + C].indirect(lst[:, 12:24]))
             else:
                 call("yp yp_ al%d" % t, "gr%d" % b, T.gr[:, 208 * b:208 * b + 208], T.yp[:, a:a + P + C].indirect(ll[:, 0:13]))
 
         def diff(b, own):
             a = C * b
             if own:
-                tt("xq xqa go%d go_ lst%d" % (b, t), "zo%d" % b, T.zt[:, 4 * A + b:4 * C:4],
+                tt("xq xqa go%d go_ lst%d lsu%d" % (b, t, t), "zo%d" % b, T.zt[:, 4 * A + b:4 * C:4],
                    T.xq[:, a:a + P + C].indirect(lst[:, 12:24]), T.go[:, 208 * b + 1:208 * b + 1 + A], sub)
             else:
                 tt("yp ypa gr%d al%d" % (b, t), "zr%d" % b, T.zt[:, b:4 * A:4],
@@ -564,7 +599,7 @@ def rank_program(g, core, T, topo):
 
         def result(own):
             h, c0, bank = ("o", A, 0) if own else ("r", 0, 1)
-            ac("pd%d" % bank, "yo" + h, T.yo[:, c0:c0 + A], T.pd[:, 512 * bank:512 * bank + A])
+            (ac if own else cp)("pd%d" % bank, "yo" + h, T.yo[:, c0:c0 + A], T.pd[:, 512 * bank:512 * bank + A])
             dmas("a", "out", "yo" + h, "", [(T.y[:, c0:c0 + A], T.yo[:, c0:c0 + A])])
 
         for b in range(4):
@@ -573,22 +608,25 @@ def rank_program(g, core, T, topo):
             diff(b, True)
         for b in range(4):
             big(b, True)
+            if b == 2:
+                gath(0, False)
         product(True)
         once(7)
         if t == NR - 1:
             quant("vt", "qv", T.qv[:], T.sv[:], T.vt[:])
-        for b in range(4):
+        for b in range(1, 4):
             gath(b, False)
+        diff(0, False)
         for b in range(4):
             state(b, True)
         for b in range(4):
             tile(b, True)
-        for b in range(4):
+        for b in range(1, 4):
             diff(b, False)
         for b in range(4):
             big(b, False)
         if t == NR - 1:
-            ac("otab lst%d" % t, "otr", T.otr[:], T.otab[:].indirect(lst[:, 0:24]))
+            ac("otab lst%d lsu%d" % (t, t), "otr", T.otr[:], T.otab[:].indirect(lst[:, 0:24]))
             dmas("s", "out", "otr", "", [(T.ot[k:k + 1, :], T.otr[16 * k:16 * k + 1, :]) for k in range(8)])
         product(False)
         pack(True)
@@ -598,12 +636,15 @@ def rank_program(g, core, T, topo):
             score(t + 1, True)
         for b in range(4):
             state(b, False)
-            tile(b, False)
+            if t < NR - 1 or b < 3:
+                tile(b, False)
+        if t == NR - 1:
+            result(True)
+            ts("xpr3", "xtr3", T.xt[:, 3:4 * A:4], T.xp[:, 3 * C:3 * C + A], 0.0078125, mul)
         if t < NR - 1:
             signs(True)
+            defects(True)
             parity(True)
-        else:
-            result(True)
         pack(False)
         if t == NR - 1:
             outputs(False)
@@ -611,10 +652,8 @@ def rank_program(g, core, T, topo):
         else:
             score(t + 1, False)
             send(t + 1, "codes")
-            ends("o")
-            role(2)
+            ends(True)
             signs(False)
-            role(3)
 
     for sem in [k for k in count if k != "out"] + ["out"]:
         if max(known[e].get(sem, 0) for e in eng) < count[sem]:

from concourse.mybir import dt, AluOpType, ActivationFunctionType

C, A, NR = 384, 192, 3
STEP = [1, 2, 4]
CW = C + 16
KEY = 801
OFF = 1159
S0 = KEY + OFF
S1 = S0 + 2 * C
W = S1 + C
B = 2560.0
BIG = 8388608.0
P = 4 * C

F, H, G, I, U, Q, S = "float32", "bfloat16", "float16", "int32", "uint16", "float8_e4m3fn_x4", "uint8"
SCRATCH = {}


def _sb(dtype, **kw):
    for k in kw:
        SCRATCH[k] = ("sbuf", [128, kw[k]], dtype)


_sb(H, x0=P, xt=P, xp=P, xq=3 * P, yp=3 * P, zt=P, z128=P, ut=512, vt=512, et=528,
    sg=C + 16, pp=C + 16, pb=C + 16, eb=C + 16, oddx=C + 16, neg2=A, ones=528, go=4 * 208, gr=4 * 208, rb=C, yk=C, dy=C, dj=CW,
    iotb=CW, nl=CW, nh=CW, tk=CW, szr=CW + 16, szp=CW, keep1=CW, keepb=CW, inc=CW, kp=A, kq=A, ev=C, cvb=C, s3=C, c3=C, ub=C, sig=C)
_sb(G, rp=CW, kc=CW, nv=CW, nv2=CW, hh=CW, uu=CW, tr=2 * C, seg=2 * C, id16=C, val=C, m0=C, sd=C)
_sb(Q, qu=128, qur=128, qv=128, qe=512, qw=512, qz=C, qx0=C, qx1=C, qx2=C, qx3=C, ql0=C, ql1=C, ql2=C)
_sb(S, su=128, sur=128, sv=128, se=512, sw=512, szz=C, sx0=C, sx1=C, sx2=C, sx3=C, sl0=C, sl1=C, sl2=C)
_sb(I, tz=64, i1=24, i2=26, i3=24, wi=24, oi=24)
_sb(U, ls=26 * 20, lu=8, lst0=24, lst1=24, lst2=24, ll0=16, ll1=16, ll2=16)
_sb(F, iot=776, sm=64 * 24, c16=64, c48=48, pk=96, pws=64, cor=40, cv1=C, krow=CW + 8, pa=CW + 8, dx=CW, lw=CW + 8, kabs=CW,
    rd=392, sc=C, nd1=C, vv=C, v2=C, ca=C, dw=W, aw=W, bt=W, base=W, dwg=C,
    ma=C, mc=C, mb=C, nr=C, yy=C, orow=C, otr=C, yo=C, otab=P + C)
SCRATCH["pd"] = ("psum", [128, 2048], F)
SCRATCH["pq"] = ("psum", [128, 2048], F)

SEMAPHORES = (["v0", "a0", "p0", "g0", "ltree", "lu_", "lx", "lw", "lv", "sent", "out", "dupx", "dupy", "sum"]
              + ["ac%d" % t for t in range(NR)] + ["al%d" % t for t in range(NR)])


def rank_program(g, core, T, topo):
    rank = T.rank_of(core)
    if rank is None:
        return
    op_ = AluOpType
    act = ActivationFunctionType
    n_ranks = len(T.cores)
    eng = {"v": g.vector, "a": g.scalar, "p": g.tensor, "g": g, "s": g.sync}
    known = {e: {} for e in eng}
    count = {}
    writer, readers = {}, {}

    def need(e, ev):
        sem, n, seen = ev
        if known[e].get(sem, 0) < n:
            eng[e].wait_ge(T.sem[sem], n)
            known[e][sem] = n
        for k in seen:
            if known[e].get(k, 0) < seen[k]:
                known[e][k] = seen[k]

    def before(e, r, w):
        evs = [writer[k] for k in r + w if k in writer]
        for k in w:
            evs = evs + readers.get(k, [])
        last = {}
        for ev in evs:
            if ev[0] not in last or last[ev[0]][1] < ev[1]:
                last[ev[0]] = ev
        evs = [last[k] for k in last]
        for ev in evs:
            if not [o for o in evs if o is not ev and o[2].get(ev[0], 0) >= ev[1]]:
                need(e, ev)

    def after(ev, r, w):
        for k in r:
            readers.setdefault(k, []).append(ev)
        for k in w:
            writer[k] = ev
            readers[k] = []

    def run(e, r, w, make):
        r, w = r.split(), w.split()
        before(e, r, w)
        sem = e + "0"
        n = count.get(sem, 0)
        make().then_inc(T.sem[sem], 1)
        count[sem] = n + 1
        after((sem, n + 1, dict(known[e])), r, w)

    def dmas(e, sem, r, w, pairs):
        r, w = r.split(), w.split()
        before(e, r, w)
        for o, i in pairs:
            eng[e].dma_start(o, i).then_inc(T.sem[sem], 16)
        count[sem] = count.get(sem, 0) + 16 * len(pairs)
        after((sem, count[sem], dict(known[e])), r, w)

    V = g.vector

    def tt(r, w, out, a, b, o):
        run("v", r, w, lambda: V.tensor_tensor(out, a, b, o))

    def ts(r, w, out, a, s1, o1, s2=None, o2=None):
        if o2 is None:
            run("v", r, w, lambda: V.tensor_scalar(out, a, s1, None, o1))
        else:
            run("v", r, w, lambda: V.tensor_scalar(out, a, s1, s2, o1, o2))

    def cp(r, w, out, a):
        run("v", r, w, lambda: V.tensor_copy(out, a))

    def scan(r, w, out, a, b, init, o1, o2):
        run("v", r, w, lambda: V.tensor_tensor_scan(out, a, b, init, o1, o2))

    def fill(w, out, c):
        run("v", "", w, lambda: V.memset(out, c))

    def ac(r, w, out, a, scale=1.0, bias=None, func=None):
        if func is None and bias is None:
            run("a", r, w, lambda: g.scalar.activation(out, a, act.Copy, scale=scale))
        else:
            f = act.Identity if func is None else func
            run("a", r, w, lambda: g.scalar.activation(out, a, f, bias=0.0 if bias is None else bias, scale=scale))

    def iota(w, out, pat, base, cm, small):
        if small:
            run("g", "", w, lambda: g.iota(out, pat, base, cm, allow_small_or_imprecise_dtypes=True))
        else:
            run("g", "", w, lambda: g.iota(out, pat, base, cm))

    def quant(r, w, q, s, x):
        run("v", r, w, lambda: V.quantize_mx(q, s, x))

    def mm(r, w, out, lq, ls, rq, rs):
        run("p", r, w, lambda: g.tensor.matmul_mx(out, lq, ls, rq, rs, True, True))

    slot, lslot, cslot = {}, {}, {}

    def sm(name, a=0, b=24, step=1):
        if name not in slot:
            slot[name] = len(slot)
        return T.sm[:, 64 * slot[name] + a:64 * slot[name] + b:step]

    def li(name, a=0, b=24, step=1):
        if name not in lslot:
            lslot[name] = len(lslot)
        return T.ls[:, 26 * lslot[name] + a:26 * lslot[name] + b:step]

    def cor(name):
        if name not in cslot:
            cslot[name] = len(cslot)
        return T.cor[:, cslot[name]:cslot[name] + 1]

    def ind(buf, n, lst, k=24, a=0):
        return T[buf][:, 0:n].indirect(li(lst, a, a + k))

    add, sub, mul, mx, mn = op_.add, op_.subtract, op_.mult, op_.max, op_.min

    def lin(name, src, m, c):
        names = [k for k in (m, c) if isinstance(k, str)]
        ac(" ".join([src] + names), name, cor(name), cor(src), cor(m) if m in names else m, cor(c) if c in names else c)

    def conv(r, src, init=2.0 * B):
        scan(r + " cv1", "sc sc2", T.sc[:], src, T.cv1[:], init, mn, add)
        return T.sc[:, 15:C:16]

    def small(h, a, b):
        scan("m0%d cvb" % h, "sd%d" % h, T.sd[:, a:b], T.m0[:, a:b], T.cvb[:, 0:b - a], 1024.0, mn, add)

    cut = [0, A + 16, CW]

    def along(row, r, o):
        scan("keep1 " + r, "pa", T.pa[:, 1:CW + 1], T.keep1[:], row[:], 0.0, mul, o)

    def parents(h, row="keepb"):
        tt("pa pa0 lpr lpr2 " + row, "hh%d" % h, T.hh[:, cut[h]:cut[h + 1]],
           ind("pa", CW + 1, "lpr2", 12) if h else ind("pa", CW + 1, "lpr", 13), T[row][:, cut[h]:cut[h + 1]], add)

    def down(h, row, r, o):
        a, b = cut[h], cut[h + 1]
        scan("hh%d uu0 %s" % (h, r), "uu%d" % h, T.uu[:, a:b], T.hh[:, a:b], row[:, a:b], T.uu[:, a - 1:a] if h else 0.0, mx, o)

    def turn(h):
        for k in range(2):
            run("v", "uu0 uu%d" % h, "tr%d%d" % (h, k),
                lambda: V.transpose(T.tr[:, C * k + A * h:C * k + A * h + A], T.uu[:, 16 * k + A * h:16 * k + A * h + A]))

    def join(h, least):
        for k in range(2):
            a = C * k + A * h
            if least:
                scan("kq9 kq25 kq15 kq31 tr%d%d" % (h, k), "seg%d%d" % (h, k), T.seg[:, a:a + A], T.tr[:, a:a + A], T.kq[:], 0.0, mn, add)
            else:
                scan("kp tr%d%d" % (h, k), "seg%d%d" % (h, k), T.seg[:, a:a + A], T.kp[:], T.tr[:, a:a + A], 0.0, mul, add)

    def pick(j, k):
        scan("seg00 seg01 seg10 seg11 c48a c48b", "pk%d" % k, T.pk[:, 48 * k:48 * k + 48], T.seg[:, j:2 * C:16], T.c48[:], -4096.0, mx, add)
        return T.pk[:, 48 * k + 1:48 * k + 24:2], T.pk[:, 48 * k + 25:48 * k + 48:2]

    def evens(h):
        back = slice(A * h + A - 1, A * h - 1 if h else None, -1)
        scan("oddx oddx_ ones", "ev%d" % h, T.ev[:, back], T.oddx[:, A * h + A + 1:A * h + 1:-1], T.ones[:, 0:A], 0.0, add, sub)

    def places(h):
        ac("ev%d base11" % h, "base1%d" % h, T.base[:, S1 + A * h:S1 + A * h + A], T.ev[:, A * h:A * h + A], 1.0,
           BIG + C if h else T.base[:, S1 + A:S1 + A + 1])

    def send(t, what):
        dst = T.cores[(rank + STEP[t]) % n_ranks]
        rid, pid, _ = topo.addr(dst)
        mask = topo.mask(core, dst)
        k = len(topo.engines(core, dst))
        if what == "codes":
            r = ["qxo%d" % t, "qxr%d" % t]
            pairs = [(T["ql%d" % t][:].bitcast(dt.uint8), T["qx%d" % t][:].bitcast(dt.uint8)), (T["sl%d" % t][:], T["sx%d" % t][:])]
            sem = "ac%d" % t
        else:
            r = ["lst%d" % t]
            pairs = [(T["ll%d" % t][:, 0:14], T["lst%d" % t][:, 0:14])]
            sem = "al%d" % t
        before("g", r, [])
        for o, i in pairs:
            g.remote_dma(o, i, T.sem[sem], T.sem.sent, pid, rid, mask)
        count["sent"] = count.get("sent", 0) + k * len(pairs)
        src = T.cores[(rank - STEP[t]) % n_ranks]
        count[sem] = len(topo.engines(src, core)) * len(pairs)
        writer[sem] = (sem, count[sem], {})

    def score(t, own):
        h, c0, bank = ("o", A, 0) if own else ("r", 0, 1)
        qx, sx = T["qx%d" % t], T["sx%d" % t]
        mm("qur sur qx%s%d" % (h, t), "pd%d" % bank, T.pd[:, 512 * bank:512 * bank + A], T.qur[:], T.sur[:], qx[:, c0:c0 + A], sx[:, c0:c0 + A])

    def signs(own):
        h, c0, bank = ("o", A, 0) if own else ("r", 0, 1)
        ts("pd%d" % bank, "sg" + h, T.sg[:, 1 + c0:1 + c0 + A], T.pd[:, 512 * bank:512 * bank + A], 0.0, op_.is_gt, 0.5, sub)

    def defects(own):
        h, c0 = ("o", A) if own else ("r", 0)
        ac("sg" + h, "dy" + h, T.dy[:, c0:c0 + A], T.sg[:, 1 + c0:1 + c0 + A], -1.0, -1.5)

    def parity(own):
        h, c0 = ("o", A) if own else ("r", 0)
        back = slice(c0 + A - 1, c0 - 1 if c0 else None, -1)
        sg = T.sg[:, c0 + A:c0:-1]
        scan("neg2 ppo sg" + h, "pp" + h, T.pp[:, back], sg, T.neg2[:], 1.0 if own else T.pp[:, A:A + 1], mul, mul)
        scan("neg2 pbo sg" + h, "pb" + h, T.pb[:, back], sg, T.neg2[:], 1.0 if own else T.pb[:, A:A + 1], mul, mul)
        if not own:
            ac("sgo sgr sg_ lpx xs xb", "dx", T.dx[:], ind("sg", C + 1, "lpx", 25), cor("xs"), cor("xb"))

    def ends(own):
        if own:
            tt("ppo pp_ pbo pb_ lendo", "ebo", T.eb[:, A + 1:C + 1], T.pp[:, A:C + 1].indirect(li("lendo", 0, 12)), T.pb[:, A + 1:C + 1], op_.not_equal)
        else:
            tt("ppo ppr pp_ pbo pbr lend", "ebr", T.eb[:, 1:A + 1], ind("pp", C + 1, "lend", 12), T.pb[:, 1:A + 1], op_.not_equal)

    def role():
        tt("ebo ebr eb_ lpx dx", "rp", T.rp[:], ind("eb", C + 1, "lpx", 25), T.dx[:], mul)

    def kind(own):
        h, c0 = ("o", A) if own else ("r", 0)
        scan("eb%s dy%s" % (h, h), "yk" + h, T.yk[:, c0:c0 + A], T.eb[:, 1 + c0:1 + c0 + A], T.dy[:, c0:c0 + A], 0.0, mx, add)

    def kinds():
        ac("yko ykr lid js jb", "dj", T.dj[:], ind("yk", C, "lid", 25), cor("js"), cor("jb"), act.Abs)
        ac("yko ykr", "oddx", T.oddx[:, 1:C + 1], T.yk[:], -1.0, -1.0, act.Abs)

    def unpack(t):
        for b in range(4):
            mm("qe%d ac%d" % (b, t), "pd%d" % b, T.pd[:, 512 * b:512 * b + C], T.qe[:, 128 * b:128 * b + 128], T.se[:, 128 * b:128 * b + 128],
               T["ql%d" % t][:], T["sl%d" % t][:])
        for b in range(4):
            ac("pd%d" % b, "yp%d" % b + (" yp" if b in (0, 3) else ""), T.yp[:, P + C * b:P + C * b + C], T.pd[:, 512 * b:512 * b + C])
        dmas("s", "dupy", "yp yp0 yp1 yp2 yp3", "ypa", [(T.yp[:, 0:P], T.yp[:, P:2 * P])])

    def planes(t):
        if t:
            ac(" ".join("xp%s%d" % (h, b) for h in "or" for b in range(4)), "xq", T.xq[:, P:2 * P], T.xp[:], 0.0078125)
        else:
            for b in range(4):
                ac("x0", "xq%d xq" % b if b == 3 else "xq%d" % b, T.xq[:, P + C * b:P + C * b + C], T.x0[:, b:4 * C:4])
        dmas("s", "dupx", "xq xq0 xq1 xq2 xq3", "xqa", [(T.xq[:, 0:P], T.xq[:, P:2 * P])])

    dmas("a", "ltree", "", "tz", [(T.tz[:, 4:28], T.sz[:]), (T.tz[:, 36:60], T.pr[:])])
    dmas("s", "lx", "", "x0", [(T.x0[:], T.x[:])])
    dmas("a", "lu_", "", "ut", [(T.ut[:], T.u[:])])
    dmas("s", "lw", "x0", "qw", [(T.qw[:].bitcast(dt.uint8), T.wc[:]), (T.sw[:], T.ws[:])])
    dmas("s", "lv", "", "vt", [(T.vt[:], T.v[:])])

    iota("i1", T.i1[:], [[0, 24]], 0, 1, False)
    iota("i3", T.i3[:, 0:16], [[1, 16]], 128, -1, False)
    iota("i2", T.i2[:], [[16, 26]], 0, 0, False)
    iota("iotb", T.iotb[:], [[1, CW]], 0, 0, True)
    iota("iot", T.iot[:, 0:CW], [[1, CW]], 0, 0, True)
    fill("pw", T.pws[:, 48:64], 2.0)
    fill("ones", T.ones[:], 1.0)
    run("g", "ones", "kp", lambda: g.affine_select(T.kp[:], T.ones[:, 0:A], [[0, 12], [1, 16]], op_.is_gt, 0.0, 0, 0))
    run("g", "ones", "et", lambda: g.affine_select(T.et[:], T.ones[:], [[1, 528]], op_.is_equal, 0.0, -3, -4))
    iota("iot2", T.iot[:, CW:776], [[1, 776 - CW]], CW, 0, True)

    ac("ones", "bt", T.bt[:, S0 + 1:S1 + 2:2], T.ones[:, 0:C + 1], 0.0)
    ac("ones", "aw", T.aw[:, S0:S1:2], T.ones[:, 0:C], -2048.0)
    scan("pw", "pw2", T.pws[:, 0:16], T.pws[:, 48:64], T.pws[:, 48:64], 1.0, mul, mx)
    ts("i1", "ih", T.i3[:, 16:17], T.i1[:, 0:1], 4, op_.arith_shift_right, 1, op_.bitwise_and)
    fill("tz0", T.tz[:, 0:4], -1)
    ts("i3", "i3", T.i3[:, 0:16], T.i3[:, 0:16], 15, op_.bitwise_and)
    fill("tz1", T.tz[:, 28:36], -1)
    ts("i1 ih", "i1", T.i1[:], T.i1[:], 15, op_.bitwise_and)
    cp("ih", "hi", cor("hi"), T.i3[:, 16:17])
    fill("tz2", T.tz[:, 60:64], -1)
    ts("i3", "c16m", T.c16[:, 48:64], T.i3[:, 0:16], 0.0, op_.is_equal)
    ts("i1", "a8", cor("a8"), T.i1[:, 0:1], 8.0, op_.is_ge)
    ts("i1", "z0", cor("z0"), T.i1[:, 0:1], 0.0, op_.is_equal)
    tt("c16m pw2", "pw3", T.pws[:, 16:32], T.c16[:, 48:64], T.pws[:, 0:16], mul)
    ts("i1", "e9", cor("e9"), T.i1[:, 0:1], 9.0, op_.is_equal)
    tt("i1 i2", "n", sm("n"), T.i1[:], T.i2[:, 0:24], add)
    cp("i1", "j16", cor("j16"), T.i1[:, 0:1])
    scan("pw3", "thr", T.pws[:, 32:48], T.pws[:, 16:32], T.pws[:, 16:32], 0.0, add, mx)
    thr = T.pws[:, 47:48]
    for name, src, m, c in [("lo", "hi", -1.0, 1.0), ("h17", "hi", 16.0, 1.0), ("ks", "a8", -1.0, 2.0), ("k1", "a8", 2.0 * C - 1.0, KEY + 1.0),
                            ("k2", "hi", "ks", 0.0), ("tkb", "a8", 4096.0, 800.0), ("kb", "a8", 6144.0, -2048.0),
                            ("kr", "k2", -16.0, "k1")]:
        lin(name, src, m, c)
    fill("szr_", T.szr[:, 0:1], 0.0)
    cp("i2", "lu", T.lu[:], T.i2[:, 0:8])
    ac("ones", "neg2", T.neg2[:], T.ones[:, 0:A], -2.0)
    cp("i1", "lp16", li("lp16"), T.i1[:])
    ts("i3", "c16b", T.c16[:, 32:48], T.i3[:, 0:16], 15.0, op_.is_equal, 2.0 * B, mul)
    ac("c16m", "c16a", T.c16[:, 16:32], T.c16[:, 48:64], -B)
    ac("ones", "kq", T.kq[:], T.ones[:, 0:A], 0.0)
    ac("ones", "aw_", T.aw[:, S1:W], T.ones[:, 0:C], -2048.0)

    ts("tz tz1 tz2 lo", "za", sm("za", 0, 58), T.tz[:, 4:62], cor("lo"), mul)
    ts("tz tz0 tz1 tz2 hi", "zb", sm("zb", 0, 58), T.tz[:, 3:61], cor("hi"), mul)
    tt("tz n", "end", sm("end"), T.tz[:, 4:28], sm("n"), add)
    tt("thr z0", "thl", cor("thl"), thr, cor("z0"), sub)
    ts("thr", "th2", cor("th2"), thr, 2.0, mul)
    tt("za zb", "zc", sm("zc", 0, 58), sm("za", 0, 58), sm("zb", 0, 58), add)
    cp("end", "lend", li("lend"), sm("end"))
    ts("end", "lendo", li("lendo", 0, 12), sm("end", 12, 24), -float(A), add)
    ts("i2 h17", "lid0", sm("lid0", 0, 26), T.i2[:], cor("h17"), sub, 1.0, add)
    tt("n tz", "b", sm("b"), sm("n"), T.tz[:, 36:60], sub)
    cp("zc", "lsz", li("lsz", 0, 26), sm("zc", 0, 26))
    ts("zc h17", "lpr", li("lpr", 0, 26), sm("zc", 32, 58), cor("h17"), add)
    ac("iotb lsz", "szr", T.szr[:, 1:CW + 1], ind("iotb", CW, "lsz", 25))
    ac("szr szr_ lpr", "szp", T.szp[:], ind("szr", CW + 1, "lpr", 25))
    ts("iotb thl", "nh", T.nh[:], T.iotb[:], cor("thl"), op_.is_ge, 4096.0, mul)
    quant("ut", "qu", T.qu[:], T.su[:], T.ut[:])
    ts("zc", "lpx", li("lpx", 0, 26), sm("zc", 32, 58), 1.0, add)
    ts("lid0 j16", "lid", li("lid", 0, 26), sm("lid0", 0, 26), cor("j16"), add, C - 1.0, mn)
    ts("zc h17", "lpr2", li("lpr2", 0, 12), sm("zc", 45, 57), cor("h17"), add)
    tt("c16a c16b", "c16", T.c16[:, 0:16], T.c16[:, 16:32], T.c16[:, 32:48], add)
    cp("qu lu", "qur", T.qur[:].bitcast(dt.uint32), T.qu[:].bitcast(dt.uint32).indirect(T.lu[:]))
    cp("qu lu", "sur", T.sur[:], T.su[:].indirect(T.lu[:]))
    ts("szr thl", "nl", T.nl[:], T.szr[:, 1:CW + 1], cor("thl"), op_.is_ge, 1.0, add)
    ts("szr th2", "dj", T.dj[:], T.szr[:, 1:CW + 1], cor("th2"), op_.is_lt, -2.0, add)
    for w, ap, c in [("pa0", T.pa[:, 0:1], 0.0), ("pp_", T.pp[:, C:C + 1], 1.0), ("pb_", T.pb[:, C:C + 1], 1.0),
                     ("oddx_", T.oddx[:, C + 1:C + 2], 0.0), ("sg_", T.sg[:, 0:1], 0.5), ("eb_", T.eb[:, 0:1], 1.0), ("rd_", T.rd[:, 0:1], BIG)]:
        ac("ones", w, ap, T.ones[:, 0:1], c)
    quant("x0", "qxo0 qxr0", T.qx0[:], T.sx0[:], T.x0[:])
    score(0, True)
    score(0, False)
    send(0, "codes")
    iota("xq_", T.xq[:, 2 * P:3 * P], [[0, P]], 0, 0, True)
    iota("yp_", T.yp[:, 2 * P:3 * P], [[0, P]], 0, 0, True)
    iota("otab", T.otab[:], [[0, 5], [1, C]], 0, 0, True)
    for name, src, m, c in [("xs", "a8", 799.0, -799.0), ("xb", "a8", -400.5, 400.5), ("j1", "a8", 1536.0, 0.0),
                            ("ka", "a8", 1.0, -1.0), ("kj", "a8", 8192.0, 0.0),
                            ("js", "e9", -752.0, "j1"), ("jb", "e9", -1536.0, "j1"), ("ca0", "hi", -4096.0, 2048.0),
                            ("ca1", "hi", 2048.0, -2048.0 - OFF), ("k0", "z0", -2.0 * B, B), ("kp_", "z0", -1024.0, 511.0),
                            ("kl", "z0", -2.0 * B, B + P)]:
        lin(name, src, m, c)
    ac("ones ca0", "c48a", T.c48[:, 0:48:2], T.ones[:, 0:24], cor("ca0"))
    ac("ones ca1", "c48b", T.c48[:, 1:48:2], T.ones[:, 0:24], cor("ca1"))
    ac("nh tkb", "tk", T.tk[:], T.nh[:], 1.0, cor("tkb"))
    ac("iot ks kr", "krow", T.krow[:, 1:CW + 1], T.iot[:, 0:CW], cor("ks"), cor("kr"))
    for j, src, m, c in [(9, "lo", -4096.0, 0.0), (25, "lo", 4096.0, 0.0), (15, "hi", 8192.0, 0.0), (31, "hi", 0.0, 8192.0)]:
        lin("q%d" % j, src, m, c)
    ac("iot", "yy", T.yy[:], T.iot[:, 0:C], -1.0 / 2048, 1.0)
    for j in (9, 25, 15, 31):
        ac("ones kq q%d" % j, "kq%d" % j, T.kq[:, j:A:32], T.ones[:, 0:6], cor("q%d" % j))

    scan("nl dj", "inc", T.inc[:], T.nl[:], T.dj[:], 0.0, mx, add)
    ts("szp th2", "keep1", T.keep1[:], T.szp[:], cor("th2"), op_.is_lt)
    ts("szp thr kb", "keepb", T.keepb[:], T.szp[:], thr, op_.is_lt, cor("kb"), mul)
    along(T.inc, "inc", sub)
    signs(True)
    signs(False)
    defects(True)
    defects(False)
    parents(0)
    parity(True)
    parents(1)
    parity(False)
    planes(0)
    down(0, T.inc, "inc", sub)
    ends(True)
    down(1, T.inc, "inc", sub)
    ends(False)
    turn(0)
    turn(1)
    kind(True)
    kind(False)
    kinds()
    join(0, False)
    join(1, False)
    tt("tk lsz krow", "kc", T.kc[:], ind("tk", CW, "lsz", 25), T.krow[:, 1:CW + 1], mn)
    pe, po = pick(7, 0)
    role()
    ts("pk0", "de", sm("d", 0, 24, 2), pe, -1.0, mul, -OFF - 1.0, add)
    ts("pk0", "do", sm("d", 1, 24, 2), po, -1.0, mul, -OFF - 1.0, add)
    ts("b", "s1", sm("s1"), sm("b"), 1.0, op_.is_gt, 775.0, mul)
    ts("b", "s0", sm("s0"), sm("b"), 1.0, op_.is_equal, 771.0, mul)
    cp("de do", "ld", li("ld"), sm("d"))
    ts("de do", "d2", sm("d2"), sm("d"), 2.0, mul)
    ac("iot ld", "nd1", T.nd1[:], ind("iot", CW, "ld"), -1.0, -399.0)
    scan("rp kc", "nv", T.nv[:], T.rp[:], T.kc[:], 0.0, mx, sub)
    tt("d2 s1", "t10", sm("t10"), sm("d2"), sm("s1"), mx)
    tt("d2 s0", "t11", sm("t11"), sm("d2"), sm("s0"), mx)

    def statics(k):
        if k == 0:
            cp("t10", "lca", li("lca"), sm("t10"))
            cp("t11", "ldw", li("ldw"), sm("t11"))
            ts("tz", "lnm", li("lnm"), T.tz[:, 36:60], 2.0, mul, float(S0 + 3), add)
            ac("nd1", "dw0", T.dw[:, S1:W], T.nd1[:], -1.0, -399.0)
            ac("nd1", "dw1", T.dw[:, S0:S1:2], T.nd1[:], -1.0, -399.0)
            ac("iot iot2 ldw", "dw2", T.dw[:, S0 + 1:S1:2], ind("iot", 776, "ldw"), 1.0, -385.0)
        if k in (1, 11):
            a = A * (k // 11)
            scan("yy nd1", "vv%d" % k, T.vv[:, a:a + A], T.yy[:, a:a + A], T.nd1[:, a:a + A], 2.0, mn, sub)
        if k == 2:
            ac("iot iot2 lca", "ca", T.ca[:], ind("iot", 776, "lca"), -1.0, -797.0)
            ac("nd1", "v2", T.v2[:], T.nd1[:], -1.0, 401.0)
        if k == 3:
            ts("end", "lsib", li("lsib"), sm("end"), 2.0, mul, float(S0 + 1), add)
            fill("go_", T.go[:, A:4 * 208:208], 0.0)
        if k == 4:
            ac("c16 lp16", "cv1", T.cv1[:], ind("c16", 16, "lp16"))
        if k == 5:
            ac("cv1", "cvb", T.cvb[:], T.cv1[:], 512.0 / B)
        if k in (5, 6):
            for b in range(2 * k - 10, 2 * k - 8):
                quant("et", "qe%d" % b, T.qe[:, 128 * b:128 * b + 128], T.se[:, 128 * b:128 * b + 128], T.et[:, 3 - b:515 - b])
        if k == 7:
            cp("iot", "id16", T.id16[:], T.iot[:, 0:C])
            scan("nh nl", "keep1", T.keep1[:], T.nh[:], T.nl[:], 0.0, mx, mul)
            fill("lw_", T.lw[:, 0:1], 2.0)
            before("g", ["keep1", "lw", "lw_"], [])
            g.dma_start(T.lw[:, 0:CW], T.keep1[:], accum_op=add).then_inc(T.sem.sum, 16)
            count["sum"] = 16
            after(("sum", 16, dict(known["g"])), ["keep1"], ["lw"])
        if k == 9:
            ac("kr", "krow_", T.krow[:, 0:1], cor("kr"))
            ac("keep1", "nh", T.nh[:], T.keep1[:], -49152.0, 65536.0)
            ac("nl", "lw", T.lw[:, 1:CW + 1], T.nl[:], -4096.0, 4098.0)
            ac("nl", "nl", T.nl[:], T.nl[:], 0.25, -0.25)
            ac("krow krow_ lpr ka kj", "kabs", T.kabs[:], ind("krow", CW + 1, "lpr", 25), cor("ka"), cor("kj"))

    for t in range(NR):
        lst, ll = T["lst%d" % t], T["ll%d" % t]

        def once(k):
            if t == 0:
                statics(k)

        if t:
            parity(False)
            defects(False)
            kind(True)
            ends(False)
            role()
            kind(False)
            kinds()
        if t:
            scan("lw rp", "pa", T.pa[:, 1:CW + 1], T.lw[:, 0:CW], T.rp[:], 4096.0, add, mn)
            scan("rp kc", "nv", T.nv[:], T.rp[:], T.kc[:], 0.0, mx, sub)
            parents(0, "kabs")
            scan("dj nv", "nv2", T.nv2[:], T.dj[:], T.nv[:], 0.0, mx, add)
            parents(1, "kabs")
        else:
            along(T.nv, "nv", mn)
            once(0)
            scan("dj nv", "nv2", T.nv2[:], T.dj[:], T.nv[:], 0.0, mx, add)
            parents(0)
            parents(1)
        ac("nd1", "bt", T.bt[:, S0:S1:2], T.nd1[:], -1.0)
        ac("yko ykr", "rb", T.rb[:], T.yk[:], -1.0, -1.0, act.Relu)
        once(2)
        down(0, T.nv2, "nv2", mn)
        evens(1)
        once(1)
        down(1, T.nv2, "nv2", mn)
        if t:
            planes(t)
        turn(0)
        turn(1)
        join(0, True)
        join(1, True)
        evens(0)
        once(11)
        qe_, qo = pick(8, 1)
        ts("seg00 seg10", "l1e", li("l1", 0, 24, 2), T.seg[:, 25:C:32], -1.0, mul, float(OFF), add)
        ts("seg01 seg11", "l1o", li("l1", 1, 24, 2), T.seg[:, C + 25:2 * C:32], -1.0, mul, float(OFF), add)
        once(3)
        ts("pk1", "l2e", li("l2", 0, 24, 2), qe_, -1.0, mul)
        ts("pk1", "l2o", li("l2", 1, 24, 2), qo, -1.0, mul)
        cp("vv1 vv11 l1e l1o", "bt", ind("bt", W, "l1"), T.vv[:])
        ac("dw0 dw1 dw2 l2e l2o", "dwg", T.dwg[:], ind("dw", W, "l2"), 1.0, 400.0)
        once(4)
        ac("bt lnm", "ma", T.ma[:], ind("bt", W, "lnm"), 1.0, -784.0)
        scan("dwg v2", "nr", T.nr[:], T.dwg[:], T.v2[:], 0.0, mx, sub)
        tt("bt lsib ca", "aw aw_", T.aw[:, S0 + 1:S1:2], ind("bt", W, "lsib"), T.ca[:], add)
        ac("nr", "s3", T.s3[:], T.nr[:], 1.0, 400.0, act.Sign)
        places(1)
        ac("s3", "c3", T.c3[:], T.s3[:], 2.5, -1.0, act.Abs)
        ac("nr", "mc", T.mc[:], T.nr[:], 1.0, 399.0, act.Abs)
        places(0)
        ac("mc", "mb", T.mb[:], T.mc[:], 1.0, -BIG)
        s = conv("ma", T.ma[:])
        tt("aw aw_ l1e l1o nd1", "yy", T.yy[:], ind("aw", W, "l1"), T.nd1[:], mx)
        ts("sc k0", "wi", T.wi[:], s, cor("k0"), add, -2048.0, mul)
        scan("rb c3", "ub", T.ub[:], T.rb[:], T.c3[:], 0.0, mx, sub)
        ts("wi", "oi", T.oi[:], T.wi[:], 2047, op_.bitwise_and)
        scan("bt yy", "rd", T.rd[:, 1:C + 1], T.bt[:, S0:S1:2], T.yy[:], BIG, add, add)
        cp("oi", "lb", li("lb"), T.oi[:])
        ac("ub", "s3", T.s3[:], T.ub[:], -1.0, -1.25, act.Sign)
        ac("rd rd_", "base0", T.base[:, S0:S1:2], T.rd[:, 0:C])
        ac("s3", "sig", T.sig[:], T.s3[:], P / 2.0, P / 2.0)
        once(5)
        tt("rd rd_ lb ma", "base2", T.base[:, S0 + 1:S1:2], ind("rd", C + 1, "lb"), T.ma[:], add)
        once(6)
        unpack(t)
        once(9)
        for h, a, b in [(0, 0, 288), (1, 288, C)]:
            tt("base0 base10 base11 base2 l2e l2o mb", "m0%d" % h, T.m0[:, a:b], ind("base", W, "l2", (b - a) // 16, a // 16), T.mb[:, a:b], add)
        small(0, 0, 288)
        small(1, 288, C)
        scan("id16 sig", "val", T.val[:], T.id16[:] if t else T.iot[:, 0:C], T.sig[:], 0.0, mx, sub)
        ts("sd0 sd1 kp_", "lpos", li("lpos"), T.sd[:, 15:C:16], cor("kp_"), add)
        cp("val lpos", "orow", ind("orow", C, "lpos"), T.val[:])
        scan("orow cv1", "sc", T.sc[:, 0:224], T.orow[:, 0:224], T.cv1[:, 0:224], 2.0 * B, mn, add)
        scan("orow cv1", "sc2", T.sc[:, 224:C], T.orow[:, 224:C], T.cv1[:, 0:160], 2.0 * B, mn, add)
        ts("sc kl", "lst%d" % t, lst[:, 0:14], T.sc[:, 15:224:16], cor("kl"), add)
        send(t, "lists")
        ts("sc2 kl", "lsu%d" % t, lst[:, 14:24], T.sc[:, 239:C:16], cor("kl"), add)

        qn, sn = T["qx%d" % (t + 1)], T["sx%d" % (t + 1)]

        def gath(b, own):
            call = cp if own and b == 0 else ac
            a = P + C * b
            if own:
                call("xq xq_ lst%d lsu%d" % (t, t), "go%d" % b, T.go[:, 208 * b:208 * b + A], T.xq[:, a:a + P + C].indirect(lst[:, 12:24]))
            else:
                call("yp yp_ al%d" % t, "gr%d" % b, T.gr[:, 208 * b:208 * b + 208], T.yp[:, a:a + P + C].indirect(ll[:, 0:13]))

        def diff(b, own):
            a = C * b
            if own:
                tt("xq xqa go%d go_ lst%d lsu%d" % (b, t, t), "zo%d" % b, T.zt[:, 4 * A + b:4 * C:4],
                   T.xq[:, a:a + P + C].indirect(lst[:, 12:24]), T.go[:, 208 * b + 1:208 * b + 1 + A], sub)
            else:
                tt("yp ypa gr%d al%d" % (b, t), "zr%d" % b, T.zt[:, b:4 * A:4],
                   T.yp[:, a:a + P + C].indirect(ll[:, 0:12]), T.gr[:, 208 * b + 1:208 * b + 1 + A], sub)

        def big(b, own):
            h, c0 = ("o", A) if own else ("r", 0)
            ac("z%s%d" % (h, b), "zb%s%d" % (h, b), T.z128[:, C * b + c0:C * b + c0 + A], T.zt[:, 4 * c0 + b:4 * (c0 + A):4], 128.0)

        def product(own):
            h, c0, ps, pn = ("o", A, T.pd, "pd") if own else ("r", 0, T.pq, "pq")
            quant("z%s0 z%s1 z%s2 z%s3" % (h, h, h, h), "qz" + h, T.qz[:, c0:c0 + A], T.szz[:, c0:c0 + A], T.zt[:, 4 * c0:4 * (c0 + A)])
            for b in range(4):
                mm("qw qz" + h, "%s%d" % (pn, b), ps[:, 512 * b:512 * b + A], T.qw[:, 128 * b:128 * b + 128], T.sw[:, 128 * b:128 * b + 128],
                   T.qz[:, c0:c0 + A], T.szz[:, c0:c0 + A])

        def state(b, own):
            h, c0, ps, pn = ("o", A, T.pd, "pd") if own else ("r", 0, T.pq, "pq")
            tt("%s%d zb%s%d" % (pn, b, h, b), "xp%s%d" % (h, b), T.xp[:, C * b + c0:C * b + c0 + A], ps[:, 512 * b:512 * b + A],
               T.z128[:, C * b + c0:C * b + c0 + A], add)

        def tile(b, own):
            h, c0 = ("o", A) if own else ("r", 0)
            ac("xp%s%d" % (h, b), "xt%s%d" % (h, b), T.xt[:, 4 * c0 + b:4 * (c0 + A):4], T.xp[:, C * b + c0:C * b + c0 + A], 0.0078125)

        def pack(own):
            h, c0 = ("o", A) if own else ("r", 0)
            quant("xt%s0 xt%s1 xt%s2 xt%s3" % (h, h, h, h), "qx%s%d" % (h, t + 1), qn[:, c0:c0 + A], sn[:, c0:c0 + A], T.xt[:, 4 * c0:4 * (c0 + A)])

        def outputs(own):
            h, c0, bank = ("o", A, 0) if own else ("r", 0, 1)
            key = "qx%s3" % h
            mm("qv " + key, "pd%d" % bank, T.pd[:, 512 * bank:512 * bank + A], T.qv[:], T.sv[:], qn[:, c0:c0 + A], sn[:, c0:c0 + A])
            dmas("s", "out", key, "", [(T.oc[:, 4 * c0:4 * (c0 + A)], qn[:, c0:c0 + A].bitcast(dt.uint8))]
                 + ([] if own else [(T.osc[4 * k:4 * k + 4, :], sn[32 * k:32 * k + 4, :]) for k in range(4)]))

        def result(own):
            h, c0, bank = ("o", A, 0) if own else ("r", 0, 1)
            (ac if own else cp)("pd%d" % bank, "yo" + h, T.yo[:, c0:c0 + A], T.pd[:, 512 * bank:512 * bank + A])
            dmas("a", "out", "yo" + h, "", [(T.y[:, c0:c0 + A], T.yo[:, c0:c0 + A])])

        for b in range(4):
            gath(b, True)
        for b in range(4):
            diff(b, True)
        for b in range(4):
            big(b, True)
            if b == 2:
                gath(0, False)
        product(True)
        once(7)
        if t == NR - 1:
            quant("vt", "qv", T.qv[:], T.sv[:], T.vt[:])
        for b in range(1, 4):
            gath(b, False)
        diff(0, False)
        for b in range(4):
            state(b, True)
        for b in range(4):
            tile(b, True)
        for b in range(1, 4):
            diff(b, False)
        for b in range(4):
            big(b, False)
        if t == NR - 1:
            ac("otab lst%d lsu%d" % (t, t), "otr", T.otr[:], T.otab[:].indirect(lst[:, 0:24]))
            dmas("s", "out", "otr", "", [(T.ot[k:k + 1, :], T.otr[16 * k:16 * k + 1, :]) for k in range(8)])
        product(False)
        pack(True)
        if t == NR - 1:
            outputs(True)
        else:
            score(t + 1, True)
        for b in range(4):
            state(b, False)
            if t < NR - 1 or b < 3:
                tile(b, False)
        if t == NR - 1:
            result(True)
            ts("xpr3", "xtr3", T.xt[:, 3:4 * A:4], T.xp[:, 3 * C:3 * C + A], 0.0078125, mul)
        if t < NR - 1:
            signs(True)
            defects(True)
            parity(True)
        pack(False)
        if t == NR - 1:
            outputs(False)
            result(False)
        else:
            score(t + 1, False)
            send(t + 1, "codes")
            ends(True)
            signs(False)

    for sem in [k for k in count if k != "out"] + ["out"]:
        if max(known[e].get(sem, 0) for e in eng) < count[sem]:
            need("g", (sem, count[sem], {}))
